import numpy as np
import ml_dtypes


def mxq(x, axis, fmt="e4m3"):
    dtype, down = {"e4m3": (ml_dtypes.float8_e4m3fn, 7), "e5m2": (ml_dtypes.float8_e5m2, 14)}[fmt]
    v = np.moveaxis(np.asarray(x, np.float32).astype(ml_dtypes.bfloat16).astype(np.float64), axis, -1)
    blocks = v.reshape(v.shape[:-1] + (-1, 32))
    amax = np.abs(blocks).max(-1, keepdims=True)
    byte = np.maximum(np.where(amax > 0, np.frexp(amax)[1] - 1 + 127, 0) - down, 1)
    scale = np.exp2(byte - 127.0)
    codes = (blocks / scale).astype(np.float32).astype(dtype).astype(np.float64)
    return np.moveaxis((codes * scale).reshape(v.shape), -1, axis)


WIDE = False


def mx_kscale(k):
    if not WIDE:
        return np.ones(k)
    levels = np.array([24, -24, 12, -12, 0])
    if k % 512:
        return np.exp2(np.random.permutation(np.resize(levels, k // 32))).repeat(32)
    a = np.empty((k // 512, 16))
    for p in range(k // 512):
        a[p, :8] = np.random.permutation(np.resize(levels, 8))
        for g in range(8):
            far = levels[np.abs(levels - a[p, g]) >= 10]
            a[p, g + 8] = far[np.random.randint(len(far))]
    return np.exp2(a.ravel()).repeat(32)


def f64(x):
    return np.asarray(x).astype(np.float64)


def striped(idx):
    return np.tile(idx.reshape(-1, 16).T, (8, 1)).astype(np.uint16)


def unstriped(offs):
    return offs[:16].T.reshape(-1).astype(np.int64)


def striped8(idx):
    return np.concatenate([v.reshape(-1, 16).T for v in idx]).astype(np.uint16)


def unstriped8(offs):
    return np.stack([offs[16 * g:16 * g + 16].T.reshape(-1) for g in range(8)]).astype(np.int64)


E2M1 = np.array([0.0, 0.5, 1.0, 1.5, 2.0, 3.0, 4.0, 6.0, -0.0, -0.5, -1.0, -1.5, -2.0, -3.0, -4.0, -6.0])


def pack_weight(w, fmt):
    k, n = w.shape
    w = f64(np.asarray(w, np.float32).astype(ml_dtypes.bfloat16)).reshape(k // 32, 32, n)
    amax = np.abs(w).max(1)
    if fmt == "e4m3":
        byte = np.frexp(amax)[1] - 1 + 127 - 7
    else:
        mant, ex = np.frexp(amax / 6.0)
        byte = np.where(mant > 0.5, ex, ex - 1) + 127
    byte = np.clip(np.where(amax > 0, byte, 1), 1, 254)
    scaled = (w * np.exp2(127.0 - byte)[:, None, :]).reshape(k, n).astype(np.float32)
    by_word = np.ascontiguousarray(scaled.reshape(k // 512, 128, 4, n).transpose(0, 1, 3, 2))
    if fmt == "e4m3":
        words = by_word.astype(ml_dtypes.float8_e4m3fn).view(np.uint8)
    else:
        c = by_word.astype(ml_dtypes.float4_e2m1fn).view(np.uint8) & 0xF
        words = (c[..., 0::2] | (c[..., 1::2] << 4)).reshape(k // 512, 128, 2 * n)
    return np.ascontiguousarray(words), np.ascontiguousarray(byte.astype(np.uint8).reshape(k // 512, 16, n))


def unpack_weight(words, scales, fmt):
    g, _, n = scales.shape
    words = np.ascontiguousarray(words).reshape(g, 128, n, -1)
    if fmt == "e4m3":
        vals = words.view(ml_dtypes.float8_e4m3fn).astype(np.float64)
    else:
        nib = np.empty((g, 128, n, 4), np.uint8)
        nib[..., 0::2] = words & 0xF
        nib[..., 1::2] = words >> 4
        vals = E2M1[nib]
    vals = vals * np.repeat(np.exp2(scales.astype(np.float64) - 127.0), 8, axis=1)[..., None]
    return vals.transpose(0, 1, 3, 2).reshape(g * 512, n)


def pack_table4(v):
    words, scales = pack_weight(v, "e2m1")
    g, t = words.shape[0] // 2, v.shape[1]
    return np.ascontiguousarray(words.reshape(g, 2, 128, t, 2).transpose(0, 2, 3, 1, 4).reshape(g, 128, t, 4)), scales


def unpack_table4(words, scales):
    g, _, t, _ = words.shape
    return unpack_weight(words.reshape(g, 128, t, 2, 2).transpose(0, 3, 1, 2, 4).reshape(2 * g, 128, 2 * t), scales, "e2m1")


K, L, R, N, T, J = 512, 1024, 512, 512, 2048, 1024


def setup_inputs():
    n = np.random.standard_normal
    s = mx_kscale(K)[:, None]
    s2 = mx_kscale(L)[:, None]
    u = mx_kscale(R)[:, None]
    p_tab = pack_table4(n((L, T)) * s2)
    p_wa = pack_weight(n((K, R)) / np.sqrt(K) / s * u.T, "e2m1")
    p_wb = pack_weight(n((L, R)) / np.sqrt(L) / s2, "e4m3")
    return {
        "tab_words": p_tab[0],
        "tab_scales": p_tab[1],
        "xT": (n((K, T)) * s).astype(np.float32),
        "wgt2": np.repeat(np.random.uniform(0.5, 2.0, (8, J)), 16, axis=0).astype(np.float32),
        "wa_words": p_wa[0],
        "wa_scales": p_wa[1],
        "wb_words": p_wb[0],
        "wb_scales": p_wb[1],
        "wd": (n((R, N)) / np.sqrt(R) / u).astype(np.float32),
        "res": (n((N, J))).astype(np.float32),
        "offs": striped(np.random.permutation(T)[:J]),
        "offs2": striped8(np.stack([np.random.permutation(T)[:J] for _ in range(8)])),
    }


def reference(tab_words, tab_scales, xT, wgt2, wa_words, wa_scales, wb_words, wb_scales, wd, res, offs, offs2):
    idx = unstriped(offs)
    idx2 = unstriped8(offs2)
    tab_ = unpack_table4(tab_words, tab_scales)[:, idx]
    rows = np.arange(K)
    xg = f64(wgt2)[rows // 4 % 128] * f64(xT)[rows[:, None], idx2[rows % 512 // 64]]
    xT_ = mxq(xg, 0, "e4m3")
    wa_ = unpack_weight(wa_words, wa_scales, "e2m1")
    wb_ = unpack_weight(wb_words, wb_scales, "e4m3")
    ya = wa_.T @ xT_
    yb = wb_.T @ tab_
    h = ya * yb
    h_ = mxq(h, 0, "e4m3")
    wd_ = mxq(f64(wd), 0, "e4m3")
    y = wd_.T @ h_
    return f64(res) + y

@@ -1,0 +1,226 @@
+from contextlib import ExitStack
+
+import concourse.mybir as mybir
+
+K, L, R, N, T, J = 512, 1024, 512, 512, 2048, 1024
+FLOPS = 2 * J * (K * R + L * R + R * N)
+
+F32 = mybir.dt.float32
+BF16 = mybir.dt.bfloat16
+I32 = mybir.dt.int32
+U32 = mybir.dt.uint32
+U16 = mybir.dt.uint16
+U8 = mybir.dt.uint8
+FP8X4 = mybir.dt.float8_e4m3fn_x4
+FP4X4 = mybir.dt.float4_e2m1fn_x4
+MULT = mybir.AluOpType.mult
+ADD = mybir.AluOpType.add
+
+P = 128
+PACK = 4
+SUB = 128
+CHUNK = 256
+HALF = 512
+LIST = 16
+
+
+def tile_list_htabg_mul_res_kernel(
+    tc, tab_words, tab_scales, xT, wgt2, wa_words, wa_scales, wb_words, wb_scales, wd, res, offs, offs2, out
+):
+    nc = tc.nc
+    with ExitStack() as ctx:
+        keep = ctx.enter_context(tc.tile_pool(name="keep", bufs=1))
+        ring = ctx.enter_context(tc.tile_pool(name="ring", bufs=3))
+        psum = ctx.enter_context(tc.psum_pool(name="psum", bufs=4))
+
+        tab_list = keep.tile([P, J // LIST], U16, name="tab_list")
+        head_lists = keep.tile([P, J // LIST], U16, name="head_lists")
+        tab_w = keep.tile([P, T], I32, name="tab_w", align_bytes=64)
+        tab_s = keep.tile([P, T // 4], I32, name="tab_s", align_bytes=64)
+        w_s = keep.tile([P, 3, R // 4], I32, name="w_s", align_bytes=64)
+        got_s = keep.tile([P, J], U8, name="got_s", align_bytes=64)
+        got_s1 = keep.tile([P, J // 4], I32, name="got_s1", align_bytes=64)
+        got_w = keep.tile([P, J], U32, name="got_w", align_bytes=64)
+        parted = keep.tile([P, 2, 2 * J], U8, name="parted", align_bytes=64)
+        wa_raw = keep.tile([P, R // 2], I32, name="wa_raw", align_bytes=64)
+        wb_raw = keep.tile([P, 2, R], I32, name="wb_raw", align_bytes=64)
+        wa_c = keep.tile([P, 2 * R], U8, name="wa_c", align_bytes=64)
+        wb_c = keep.tile([P, 2, R], I32, name="wb_c", align_bytes=64)
+        w_sc = keep.tile([P, 3, R], U8, name="w_sc", align_bytes=64)
+        wgt = keep.tile([P, J], F32, name="wgt", align_bytes=64)
+        planes = [keep.tile([P, T], F32, name="plane%d" % i, align_bytes=64) for i in range(PACK)]
+        wd_raw = keep.tile([P, PACK, N], F32, name="wd_raw", align_bytes=64)
+        wd_bf = keep.tile([P, N, PACK], BF16, name="wd_bf", align_bytes=64)
+        wd_c = keep.tile([P, N], U32, name="wd_c", align_bytes=64)
+        wd_s = keep.tile([P, N], U8, name="wd_s", align_bytes=64)
+        res_sb = keep.tile([P, N // P, J], F32, name="res_sb", align_bytes=64)
+        picked = keep.tile([P, PACK, J], F32, name="picked", align_bytes=64)
+        yb_sb = keep.tile([P, J, PACK], F32, name="yb_sb", align_bytes=64)
+
+        nc.vector.memset(tab_s[:], 0)
+        nc.vector.memset(w_s[:], 0)
+        nc.vector.memset(got_s1[:], 0)
+
+        nc.sync.dma_start(tab_list[:], offs)
+        tab_scales_i = tab_scales.bitcast(I32)
+        for q in range(4):
+            nc.sync.dma_start(tab_s[32 * q : 32 * q + 8, :], tab_scales_i[:, 4 * q : 4 * q + 4, :])
+        nc.sync.dma_start(tab_w[:], tab_words[0].rearrange("p t b -> p (t b)").bitcast(I32))
+        nc.sync.dma_start(head_lists[:], offs2)
+        wa_scales_i = wa_scales.bitcast(I32)
+        wb_scales_i = wb_scales.bitcast(I32)
+        for q in range(4):
+            nc.gpsimd.dma_start(w_s[32 * q : 32 * q + 4, 0, :], wa_scales_i[0, 4 * q : 4 * q + 4, :])
+        nc.sync.dma_start(wgt[:], wgt2)
+        x_planes = xT.rearrange("(p i) t -> i p t", i=PACK)
+        nc.sync.dma_start(planes[0][:], x_planes[0])
+        for q in range(4):
+            nc.sync.dma_start(
+                w_s[32 * q : 32 * q + 4, 1:3, :], wb_scales_i[:, 4 * q : 4 * q + 4, :].rearrange("a r n -> r a n")
+            )
+        nc.sync.dma_start(wb_raw[:], wb_words.rearrange("a p r i -> p a (r i)").bitcast(I32))
+        nc.sync.dma_start(wa_raw[:], wa_words[0].bitcast(I32))
+        for i in range(1, PACK):
+            nc.sync.dma_start(planes[i][:], x_planes[i])
+        nc.sync.dma_start(wd_raw[:], wd.rearrange("(p i) n -> p i n", i=PACK))
+        res_v = res.rearrange("(b m) j -> m b j", m=P)
+        out_v = out.rearrange("(b m) j -> m b j", m=P)
+        for c in range(J // CHUNK):
+            cols = slice(c * CHUNK, (c + 1) * CHUNK)
+            nc.sync.dma_start(res_sb[:, :, cols], res_v[:, :, cols])
+
+        nc.vector.tensor_copy(got_s[:], tab_s[:].bitcast(U8).indirect(tab_list[:]))
+        got_s_i = got_s[:].bitcast(I32)
+        nc.gpsimd.dma_start(got_s1[0:100, :], got_s_i[4:104, :])
+        nc.vector.tensor_copy(got_w[:], tab_w[:].bitcast(U32).indirect(tab_list[:]))
+        nc.vector.tensor_copy(
+            wb_c[:].rearrange("p a (t m) -> p a t m", t=PACK), wb_raw[:].rearrange("p a (m t) -> p a t m", t=PACK)
+        )
+        nc.vector.tensor_copy(parted[:].bitcast(U16), got_w[:].bitcast(U16).rearrange("p (j d) -> p d j", d=2))
+        nc.vector.tensor_copy(
+            w_sc[:].rearrange("p a (t m) -> p a t m", t=PACK),
+            w_s[:].bitcast(U8).rearrange("p a (m t) -> p a t m", t=PACK),
+        )
+        nc.vector.tensor_copy(
+            wa_c[:].bitcast(U16).rearrange("p (t m) -> p t m", t=PACK),
+            wa_raw[:].bitcast(U16).rearrange("p (m t) -> p t m", t=PACK),
+        )
+
+        tab_planes = [got_s[:], got_s1[:].bitcast(U8)]
+        for s in range(J // SUB):
+            cols = slice(s * SUB, (s + 1) * SUB)
+            bank = psum.tile([P, PACK, SUB], F32, name="first", tag="first")
+            for t in range(PACK):
+                ch = slice(t * P, (t + 1) * P)
+                for a in range(2):
+                    nc.tensor.matmul_mx(
+                        out=bank[:, t, :],
+                        lhsT=wb_c[:, a, ch].bitcast(FP8X4),
+                        lhsT_scale=w_sc[:, 1 + a, ch],
+                        rhs=parted[:, a, 2 * s * SUB : 2 * (s + 1) * SUB].bitcast(FP4X4),
+                        rhs_scale=tab_planes[a][:, cols],
+                        start=(a == 0),
+                        stop=(a == 1),
+                    )
+            nc.scalar.copy(yb_sb[:, cols, :], bank[:].rearrange("p t n -> p n t"))
+
+        def pick(i, lo, hi):
+            nc.vector.tensor_tensor(
+                picked[:, i, lo:hi],
+                planes[i][:].indirect(head_lists[:, lo // LIST : hi // LIST]),
+                wgt[:, lo:hi],
+                MULT,
+            )
+
+        for i in range(PACK - 1):
+            for lo in range(0, J, HALF):
+                pick(i, lo, lo + HALF)
+
+        nc.scalar.copy(wd_bf[:], wd_raw[:].rearrange("p i n -> p n i"))
+
+        x_bf, x_c, x_s, h_bf, h_c, h_s, ya, y = {}, {}, {}, {}, {}, {}, {}, {}
+
+        def gather(c):
+            lo = c * CHUNK
+            pick(PACK - 1, lo, lo + CHUNK)
+            x_bf[c] = ring.tile([P, CHUNK, PACK], BF16, name="x_bf", align_bytes=64)
+            nc.scalar.copy(x_bf[c][:], picked[:, :, lo : lo + CHUNK].rearrange("p i n -> p n i"))
+
+        def quant_x(c):
+            x_c[c] = ring.tile([P, CHUNK], U32, name="x_c", align_bytes=64)
+            x_s[c] = ring.tile([P, CHUNK], U8, name="x_s", align_bytes=64)
+            nc.vector.quantize_mx(
+                out=x_c[c][:].bitcast(FP8X4), scales=x_s[c][:], in_=x_bf[c][:].rearrange("p n i -> p (n i)")
+            )
+            for u in range(CHUNK // SUB):
+                cols = slice(u * SUB, (u + 1) * SUB)
+                ya[c, u] = psum.tile([P, PACK, SUB], F32, name="first", tag="first")
+                for t in range(PACK):
+                    ch = slice(t * P, (t + 1) * P)
+                    nc.tensor.matmul_mx(
+                        out=ya[c, u][:, t, :],
+                        lhsT=wa_c[:, 2 * t * P : 2 * (t + 1) * P].bitcast(FP4X4),
+                        lhsT_scale=w_sc[:, 0, ch],
+                        rhs=x_c[c][:, cols].bitcast(FP8X4),
+                        rhs_scale=x_s[c][:, cols],
+                        start=True,
+                        stop=True,
+                    )
+
+        def product(c):
+            h_bf[c] = ring.tile([P, CHUNK, PACK], BF16, name="h_bf", align_bytes=64)
+            for u in range(CHUNK // SUB):
+                lo = c * CHUNK + u * SUB
+                nc.vector.tensor_tensor(
+                    h_bf[c][:, u * SUB : (u + 1) * SUB, :],
+                    ya[c, u][:].rearrange("p t n -> p n t"),
+                    yb_sb[:, lo : lo + SUB, :],
+                    MULT,
+                )
+
+        def quant_h(c):
+            h_c[c] = ring.tile([P, CHUNK], U32, name="h_c", align_bytes=64)
+            h_s[c] = ring.tile([P, CHUNK], U8, name="h_s", align_bytes=64)
+            nc.vector.quantize_mx(
+                out=h_c[c][:].bitcast(FP8X4), scales=h_s[c][:], in_=h_bf[c][:].rearrange("p n i -> p (n i)")
+            )
+            for g in range(2):
+                y[c, g] = psum.tile([P, 2, CHUNK], F32, name="second", tag="second")
+                for b in range(2):
+                    ch = slice((2 * g + b) * P, (2 * g + b + 1) * P)
+                    nc.tensor.matmul_mx(
+                        out=y[c, g][:, b, :],
+                        lhsT=wd_c[:, ch].bitcast(FP8X4),
+                        lhsT_scale=wd_s[:, ch],
+                        rhs=h_c[c][:].bitcast(FP8X4),
+                        rhs_scale=h_s[c][:],
+                        start=True,
+                        stop=True,
+                    )
+
+        def finish(c):
+            cols = slice(c * CHUNK, (c + 1) * CHUNK)
+            for g in range(2):
+                blocks = slice(2 * g, 2 * g + 2)
+                total = ring.tile([P, 2, CHUNK], F32, name="total", bufs=4)
+                nc.vector.tensor_tensor(total[:], y[c, g][:], res_sb[:, blocks, cols], ADD)
+                nc.sync.dma_start(out_v[:, blocks, cols], total[:])
+
+        chunks = J // CHUNK
+        gather(0)
+        gather(1)
+        nc.vector.quantize_mx(
+            out=wd_c[:].bitcast(FP8X4), scales=wd_s[:], in_=wd_bf[:].rearrange("p n i -> p (n i)")
+        )
+        quant_x(0)
+        for c in range(chunks + 1):
+            if c + 2 < chunks:
+                gather(c + 2)
+            if c < chunks:
+                product(c)
+            if c + 1 < chunks:
+                quant_x(c + 1)
+            if c >= 1:
+                finish(c - 1)
+            if c < chunks:
+                quant_h(c)

@@ -31,80 +31,88 @@ def tile_list_htabg_mul_res_kernel(
     with ExitStack() as ctx:
         keep = ctx.enter_context(tc.tile_pool(name="keep", bufs=1))
         ring = ctx.enter_context(tc.tile_pool(name="ring", bufs=3))
+        reuse = ctx.enter_context(tc.tile_pool(name="reuse", bufs=1))
         psum = ctx.enter_context(tc.psum_pool(name="psum", bufs=4))
+
+        def held(shape, dtype, name, tag=""):
+            return keep.tile(shape, dtype, name=name, tag=tag or name, align_bytes=64)
 
         tab_list = keep.tile([P, J // LIST], U16, name="tab_list")
         head_lists = keep.tile([P, J // LIST], U16, name="head_lists")
-        tab_w = keep.tile([P, T], I32, name="tab_w", align_bytes=64)
-        tab_s = keep.tile([P, T // 4], I32, name="tab_s", align_bytes=64)
-        w_s = keep.tile([P, 3, R // 4], I32, name="w_s", align_bytes=64)
-        got_s = keep.tile([P, J], U8, name="got_s", align_bytes=64)
-        got_s1 = keep.tile([P, J // 4], I32, name="got_s1", align_bytes=64)
-        got_w = keep.tile([P, J], U32, name="got_w", align_bytes=64)
-        parted = keep.tile([P, 2, 2 * J], U8, name="parted", align_bytes=64)
-        wa_raw = keep.tile([P, R // 2], I32, name="wa_raw", align_bytes=64)
-        wb_raw = keep.tile([P, 2, R], I32, name="wb_raw", align_bytes=64)
-        wa_c = keep.tile([P, 2 * R], U8, name="wa_c", align_bytes=64)
-        wb_c = keep.tile([P, 2, R], I32, name="wb_c", align_bytes=64)
-        w_sc = keep.tile([P, 3, R], U8, name="w_sc", align_bytes=64)
-        wgt = keep.tile([P, J], F32, name="wgt", align_bytes=64)
-        planes = [keep.tile([P, T], F32, name="plane%d" % i, align_bytes=64) for i in range(PACK)]
-        wd_raw = keep.tile([P, PACK, N], F32, name="wd_raw", align_bytes=64)
-        wd_bf = keep.tile([P, N, PACK], BF16, name="wd_bf", align_bytes=64)
-        wd_c = keep.tile([P, N], U32, name="wd_c", align_bytes=64)
-        wd_s = keep.tile([P, N], U8, name="wd_s", align_bytes=64)
-        res_sb = keep.tile([P, N // P, J], F32, name="res_sb", align_bytes=64)
-        picked = keep.tile([P, PACK, J], F32, name="picked", align_bytes=64)
-        yb_sb = keep.tile([P, J, PACK], F32, name="yb_sb", align_bytes=64)
+        tab_w = held([P, T], I32, "tab_w", "slot_b")
+        tab_s = reuse.tile([P, T // 4], I32, name="tab_s", offset=0, align_bytes=64)
+        wb_s = held([P, 2, R // 4], I32, "wb_s")
+        got_s = held([P, J], U8, "got_s")
+        got_s1 = held([P, J // 4], I32, "got_s1")
+        got_w = held([P, J], U32, "got_w")
+        parted = held([P, 2, 2 * J], U8, "parted")
+        wa_raw = held([P, R // 2], I32, "wa_raw")
+        wb_raw = held([P, 2, R], I32, "wb_raw", "slot_c")
+        wa_c = held([P, 2 * R], U8, "wa_c")
+        wb_c = held([P, 2, R], I32, "wb_c")
+        w_sc = held([P, 3, R], U8, "w_sc")
+        wgt = held([P, J], F32, "wgt")
+        planes = [held([P, T], F32, "plane0", "slot_d"), held([P, T], F32, "plane1", "slot_e")]
+        wd_bf = held([P, N, PACK], BF16, "wd_bf")
+        wd_c = held([P, N], U32, "wd_c")
+        wd_s = held([P, N], U8, "wd_s")
+        picked = held([P, PACK, J], F32, "picked")
+        yb_sb = held([P, J, PACK], F32, "yb_sb")
 
-        nc.vector.memset(tab_s[:], 0)
-        nc.vector.memset(w_s[:], 0)
+        nc.gpsimd.memset(tab_s[:], 0)
+        nc.vector.memset(wb_s[:], 0)
         nc.vector.memset(got_s1[:], 0)
 
-        nc.sync.dma_start(tab_list[:], offs)
         tab_scales_i = tab_scales.bitcast(I32)
+        wa_scales_i = wa_scales.bitcast(I32)
+        wb_scales_i = wb_scales.bitcast(I32)
+        x_planes = xT.rearrange("(p i) t -> i p t", i=PACK)
+        wd_v = wd.rearrange("(g t q) n -> q g t n", t=PACK, q=8)
+        res_v = res.rearrange("(b m) j -> m b j", m=P)
+        out_v = out.rearrange("(b m) j -> m b j", m=P)
+
+        nc.sync.dma_start(tab_list[:], offs)
         for q in range(4):
             nc.sync.dma_start(tab_s[32 * q : 32 * q + 8, :], tab_scales_i[:, 4 * q : 4 * q + 4, :])
         nc.sync.dma_start(tab_w[:], tab_words[0].rearrange("p t b -> p (t b)").bitcast(I32))
-        nc.sync.dma_start(head_lists[:], offs2)
-        wa_scales_i = wa_scales.bitcast(I32)
-        wb_scales_i = wb_scales.bitcast(I32)
-        for q in range(4):
-            nc.gpsimd.dma_start(w_s[32 * q : 32 * q + 4, 0, :], wa_scales_i[0, 4 * q : 4 * q + 4, :])
+        nc.sync.dma_start(wb_raw[:], wb_words.rearrange("a p r i -> p a (r i)").bitcast(I32))
         nc.sync.dma_start(wgt[:], wgt2)
-        x_planes = xT.rearrange("(p i) t -> i p t", i=PACK)
-        nc.sync.dma_start(planes[0][:], x_planes[0])
         for q in range(4):
             nc.sync.dma_start(
-                w_s[32 * q : 32 * q + 4, 1:3, :], wb_scales_i[:, 4 * q : 4 * q + 4, :].rearrange("a r n -> r a n")
+                wb_s[32 * q : 32 * q + 4, :, :], wb_scales_i[:, 4 * q : 4 * q + 4, :].rearrange("a r n -> r a n")
             )
-        nc.sync.dma_start(wb_raw[:], wb_words.rearrange("a p r i -> p a (r i)").bitcast(I32))
+        nc.sync.dma_start(planes[0][:], x_planes[0])
+        nc.sync.dma_start(head_lists[:], offs2)
+        nc.sync.dma_start(planes[1][:], x_planes[1])
         nc.sync.dma_start(wa_raw[:], wa_words[0].bitcast(I32))
-        for i in range(1, PACK):
-            nc.sync.dma_start(planes[i][:], x_planes[i])
-        nc.sync.dma_start(wd_raw[:], wd.rearrange("(p i) n -> p i n", i=PACK))
-        res_v = res.rearrange("(b m) j -> m b j", m=P)
-        out_v = out.rearrange("(b m) j -> m b j", m=P)
-        for c in range(J // CHUNK):
-            cols = slice(c * CHUNK, (c + 1) * CHUNK)
-            nc.sync.dma_start(res_sb[:, :, cols], res_v[:, :, cols])
 
         nc.vector.tensor_copy(got_s[:], tab_s[:].bitcast(U8).indirect(tab_list[:]))
-        got_s_i = got_s[:].bitcast(I32)
-        nc.gpsimd.dma_start(got_s1[0:100, :], got_s_i[4:104, :])
+        nc.sync.dma_start(got_s1[0:100, :], got_s[:].bitcast(I32)[4:104, :])
+        planes.append(reuse.tile([P, T], F32, name="plane2", offset=R, align_bytes=64))
+        nc.sync.dma_start(planes[2][:], x_planes[2])
+        wa_s = reuse.tile([P, R // 4], I32, name="wa_s", offset=0, align_bytes=64)
+        nc.gpsimd.memset(wa_s[:], 0)
+        for q in range(4):
+            nc.sync.dma_start(wa_s[32 * q : 32 * q + 4, :], wa_scales_i[0, 4 * q : 4 * q + 4, :])
+
         nc.vector.tensor_copy(got_w[:], tab_w[:].bitcast(U32).indirect(tab_list[:]))
-        nc.vector.tensor_copy(
-            wb_c[:].rearrange("p a (t m) -> p a t m", t=PACK), wb_raw[:].rearrange("p a (m t) -> p a t m", t=PACK)
-        )
+        planes.append(held([P, T], F32, "plane3", "slot_b"))
+        nc.sync.dma_start(planes[3][:], x_planes[3])
+
+        def permute(dst, src, run):
+            nc.vector.tensor_copy(
+                dst.rearrange("p (t g q) -> p t g q", t=PACK, q=run),
+                src.rearrange("p (g t q) -> p t g q", t=PACK, q=run),
+            )
+
+        permute(wb_c[:, 0, :], wb_raw[:, 0, :], 8)
         nc.vector.tensor_copy(parted[:].bitcast(U16), got_w[:].bitcast(U16).rearrange("p (j d) -> p d j", d=2))
-        nc.vector.tensor_copy(
-            w_sc[:].rearrange("p a (t m) -> p a t m", t=PACK),
-            w_s[:].bitcast(U8).rearrange("p a (m t) -> p a t m", t=PACK),
-        )
-        nc.vector.tensor_copy(
-            wa_c[:].bitcast(U16).rearrange("p (t m) -> p t m", t=PACK),
-            wa_raw[:].bitcast(U16).rearrange("p (m t) -> p t m", t=PACK),
-        )
+        permute(wb_c[:, 1, :], wb_raw[:, 1, :], 8)
+        for a in (1, 2):
+            permute(w_sc[:, a, :].bitcast(I32), wb_s[:, a - 1, :], 2)
+        wd_raw = held([P, PACK, N], F32, "wd_raw", "slot_c")
+        for q in (0, 4, 1, 5, 2, 6, 3, 7):
+            nc.sync.dma_start(wd_raw[q:P:8, :, :], wd_v[q])
 
         tab_planes = [got_s[:], got_s1[:].bitcast(U8)]
         for s in range(J // SUB):
@@ -132,11 +140,28 @@ def tile_list_htabg_mul_res_kernel(
                 MULT,
             )
 
+        res_sb = []
         for i in range(PACK - 1):
             for lo in range(0, J, HALF):
                 pick(i, lo, lo + HALF)
+            if i < 2:
+                res_sb.append(held([P, N // P, HALF], F32, "res%d" % i, ("slot_d", "slot_e")[i]))
+                nc.sync.dma_start(res_sb[i][:], res_v[:, :, i * HALF : (i + 1) * HALF])
+            if i == 1:
+                permute(w_sc[:, 0, :].bitcast(I32), wa_s[:], 2)
+                permute(wa_c[:].bitcast(I32), wa_raw[:], 4)
 
-        nc.scalar.copy(wd_bf[:], wd_raw[:].rearrange("p i n -> p n i"))
+        def cast_wd(g):
+            ch = slice(g * 256, (g + 1) * 256)
+            nc.scalar.copy(wd_bf[:, ch, :], wd_raw[:, :, ch].rearrange("p i n -> p n i"))
+
+        def quant_wd(g):
+            ch = slice(g * 256, (g + 1) * 256)
+            nc.vector.quantize_mx(
+                out=wd_c[:, ch].bitcast(FP8X4),
+                scales=wd_s[:, ch],
+                in_=wd_bf[:, ch, :].rearrange("p n i -> p (n i)"),
+            )
 
         x_bf, x_c, x_s, h_bf, h_c, h_s, ya, y = {}, {}, {}, {}, {}, {}, {}, {}
 
@@ -203,15 +228,14 @@ def tile_list_htabg_mul_res_kernel(
             for g in range(2):
                 blocks = slice(2 * g, 2 * g + 2)
                 total = ring.tile([P, 2, CHUNK], F32, name="total", bufs=4)
-                nc.vector.tensor_tensor(total[:], y[c, g][:], res_sb[:, blocks, cols], ADD)
+                nc.vector.tensor_tensor(total[:], y[c, g][:], res_sb[c // 2][:, blocks, (c % 2) * CHUNK : (c % 2 + 1) * CHUNK], ADD)
                 nc.sync.dma_start(out_v[:, blocks, cols], total[:])
 
         chunks = J // CHUNK
         gather(0)
         gather(1)
-        nc.vector.quantize_mx(
-            out=wd_c[:].bitcast(FP8X4), scales=wd_s[:], in_=wd_bf[:].rearrange("p n i -> p (n i)")
-        )
+        cast_wd(0)
+        cast_wd(1)
         quant_x(0)
         for c in range(chunks + 1):
             if c + 2 < chunks:
@@ -222,5 +246,8 @@ def tile_list_htabg_mul_res_kernel(
                 quant_x(c + 1)
             if c >= 1:
                 finish(c - 1)
+            if c == 0:
+                quant_wd(0)
+                quant_wd(1)
             if c < chunks:
                 quant_h(c)

@@ -22,6 +22,7 @@ SUB = 128
 CHUNK = 256
 HALF = 512
 LIST = 16
+PLANE_BYTES = 4 * T
 
 
 def tile_list_htabg_mul_res_kernel(
@@ -32,6 +33,7 @@ def tile_list_htabg_mul_res_kernel(
         keep = ctx.enter_context(tc.tile_pool(name="keep", bufs=1))
         ring = ctx.enter_context(tc.tile_pool(name="ring", bufs=3))
         reuse = ctx.enter_context(tc.tile_pool(name="reuse", bufs=1))
+        reuse0 = ctx.enter_context(tc.tile_pool(name="reuse0", bufs=1))
         psum = ctx.enter_context(tc.psum_pool(name="psum", bufs=4))
 
         def held(shape, dtype, name, tag=""):
@@ -39,82 +41,89 @@ def tile_list_htabg_mul_res_kernel(
 
         tab_list = keep.tile([P, J // LIST], U16, name="tab_list")
         head_lists = keep.tile([P, J // LIST], U16, name="head_lists")
-        tab_w = held([P, T], I32, "tab_w", "slot_b")
-        tab_s = reuse.tile([P, T // 4], I32, name="tab_s", offset=0, align_bytes=64)
+        tab_w = held([P, T], I32, "tab_w")
+        tab_s = reuse.tile([P, T // 4], I32, name="tab_s", offset=PLANE_BYTES - 512, align_bytes=64)
         wb_s = held([P, 2, R // 4], I32, "wb_s")
         got_s = held([P, J], U8, "got_s")
-        got_s1 = held([P, J // 4], I32, "got_s1")
+        tab_sc = held([P, 2, J // 4], I32, "tab_sc")
         got_w = held([P, J], U32, "got_w")
         parted = held([P, 2, 2 * J], U8, "parted")
-        wa_raw = held([P, R // 2], I32, "wa_raw")
         wb_raw = held([P, 2, R], I32, "wb_raw", "slot_c")
         wa_c = held([P, 2 * R], U8, "wa_c")
         wb_c = held([P, 2, R], I32, "wb_c")
-        w_sc = held([P, 3, R], U8, "w_sc")
+        wb_sc = held([P, 2, R], U8, "wb_sc")
         wgt = held([P, J], F32, "wgt")
-        planes = [held([P, T], F32, "plane0", "slot_d"), held([P, T], F32, "plane1", "slot_e")]
+        planes = [
+            reuse0.tile([P, T], F32, name="plane0", offset=0, align_bytes=64),
+            held([P, T], F32, "plane1", "slot_e"),
+        ]
         wd_bf = held([P, N, PACK], BF16, "wd_bf")
         wd_c = held([P, N], U32, "wd_c")
         wd_s = held([P, N], U8, "wd_s")
         picked = held([P, PACK, J], F32, "picked")
         yb_sb = held([P, J, PACK], F32, "yb_sb")
 
-        nc.gpsimd.memset(tab_s[:], 0)
-        nc.vector.memset(wb_s[:], 0)
-        nc.vector.memset(got_s1[:], 0)
+        wa_s = held([P, R // 4], I32, "wa_s")
+        nc.gpsimd.memset(wb_s[:], 0)
+        nc.gpsimd.memset(wa_s[:], 0)
+        for q in range(4):
+            nc.vector.memset(tab_s[32 * q : 32 * q + 24, :], 0)
+        nc.vector.memset(tab_sc[:], 0)
 
         tab_scales_i = tab_scales.bitcast(I32)
         wa_scales_i = wa_scales.bitcast(I32)
         wb_scales_i = wb_scales.bitcast(I32)
         x_planes = xT.rearrange("(p i) t -> i p t", i=PACK)
-        wd_v = wd.rearrange("(g t q) n -> q g t n", t=PACK, q=8)
+        wd_v = wd.rearrange("(m t q) n -> q m t n", t=PACK, q=4)
         res_v = res.rearrange("(b m) j -> m b j", m=P)
         out_v = out.rearrange("(b m) j -> m b j", m=P)
 
         nc.sync.dma_start(tab_list[:], offs)
         for q in range(4):
-            nc.sync.dma_start(tab_s[32 * q : 32 * q + 8, :], tab_scales_i[:, 4 * q : 4 * q + 4, :])
+            nc.sync.dma_start(tab_s[32 * q + 24 : 32 * q + 32, :], tab_scales_i[:, 4 * q : 4 * q + 4, :])
         nc.sync.dma_start(tab_w[:], tab_words[0].rearrange("p t b -> p (t b)").bitcast(I32))
         nc.sync.dma_start(wb_raw[:], wb_words.rearrange("a p r i -> p a (r i)").bitcast(I32))
         nc.sync.dma_start(wgt[:], wgt2)
+        nc.sync.dma_start(head_lists[:], offs2)
         for q in range(4):
             nc.sync.dma_start(
                 wb_s[32 * q : 32 * q + 4, :, :], wb_scales_i[:, 4 * q : 4 * q + 4, :].rearrange("a r n -> r a n")
             )
-        nc.sync.dma_start(planes[0][:], x_planes[0])
-        nc.sync.dma_start(head_lists[:], offs2)
+            if q == 0:
+                nc.sync.dma_start(planes[0][:], x_planes[0])
         nc.sync.dma_start(planes[1][:], x_planes[1])
-        nc.sync.dma_start(wa_raw[:], wa_words[0].bitcast(I32))
+        for q in range(4):
+            nc.gpsimd.dma_start(wa_s[32 * q : 32 * q + 4, :], wa_scales_i[0, 4 * q : 4 * q + 4, :])
 
         nc.vector.tensor_copy(got_s[:], tab_s[:].bitcast(U8).indirect(tab_list[:]))
-        nc.sync.dma_start(got_s1[0:100, :], got_s[:].bitcast(I32)[4:104, :])
-        planes.append(reuse.tile([P, T], F32, name="plane2", offset=R, align_bytes=64))
+        for a in range(2):
+            nc.scalar.dma_start(tab_sc[0:100, a, :], got_s[:].bitcast(I32)[24 + 4 * a : 124 + 4 * a, :])
+        planes.append(reuse.tile([P, T], F32, name="plane2", offset=0, align_bytes=64))
         nc.sync.dma_start(planes[2][:], x_planes[2])
-        wa_s = reuse.tile([P, R // 4], I32, name="wa_s", offset=0, align_bytes=64)
-        nc.gpsimd.memset(wa_s[:], 0)
-        for q in range(4):
-            nc.sync.dma_start(wa_s[32 * q : 32 * q + 4, :], wa_scales_i[0, 4 * q : 4 * q + 4, :])
+        planes.append(reuse.tile([P, T], F32, name="plane3", offset=PLANE_BYTES + 1024, align_bytes=64))
+        nc.sync.dma_start(planes[3][:], x_planes[3])
+        wa_raw = reuse.tile([P, R // 2], I32, name="wa_raw", offset=PLANE_BYTES, align_bytes=64)
+        nc.sync.dma_start(wa_raw[:], wa_words[0].bitcast(I32))
 
         nc.vector.tensor_copy(got_w[:], tab_w[:].bitcast(U32).indirect(tab_list[:]))
-        planes.append(held([P, T], F32, "plane3", "slot_b"))
-        nc.sync.dma_start(planes[3][:], x_planes[3])
 
         def permute(dst, src, run):
             nc.vector.tensor_copy(
-                dst.rearrange("p (t g q) -> p t g q", t=PACK, q=run),
-                src.rearrange("p (g t q) -> p t g q", t=PACK, q=run),
+                dst.rearrange("p (t m q) -> p m t q", t=PACK, q=run),
+                src.rearrange("p (m t q) -> p m t q", t=PACK, q=run),
             )
 
-        permute(wb_c[:, 0, :], wb_raw[:, 0, :], 8)
+        permute(wb_c[:, 0, :], wb_raw[:, 0, :], 4)
         nc.vector.tensor_copy(parted[:].bitcast(U16), got_w[:].bitcast(U16).rearrange("p (j d) -> p d j", d=2))
-        permute(wb_c[:, 1, :], wb_raw[:, 1, :], 8)
-        for a in (1, 2):
-            permute(w_sc[:, a, :].bitcast(I32), wb_s[:, a - 1, :], 2)
+        permute(wb_c[:, 1, :], wb_raw[:, 1, :], 4)
+        nc.vector.tensor_copy(
+            wb_sc[:].bitcast(I32).rearrange("p a (t m) -> p a m t", t=PACK),
+            wb_s[:].rearrange("p a (m t) -> p a m t", t=PACK),
+        )
         wd_raw = held([P, PACK, N], F32, "wd_raw", "slot_c")
-        for q in (0, 4, 1, 5, 2, 6, 3, 7):
-            nc.sync.dma_start(wd_raw[q:P:8, :, :], wd_v[q])
+        for q in range(4):
+            nc.sync.dma_start(wd_raw[q:P:4, :, :], wd_v[q])
 
-        tab_planes = [got_s[:], got_s1[:].bitcast(U8)]
         for s in range(J // SUB):
             cols = slice(s * SUB, (s + 1) * SUB)
             bank = psum.tile([P, PACK, SUB], F32, name="first", tag="first")
@@ -124,9 +133,9 @@ def tile_list_htabg_mul_res_kernel(
                     nc.tensor.matmul_mx(
                         out=bank[:, t, :],
                         lhsT=wb_c[:, a, ch].bitcast(FP8X4),
-                        lhsT_scale=w_sc[:, 1 + a, ch],
+                        lhsT_scale=wb_sc[:, a, ch],
                         rhs=parted[:, a, 2 * s * SUB : 2 * (s + 1) * SUB].bitcast(FP4X4),
-                        rhs_scale=tab_planes[a][:, cols],
+                        rhs_scale=tab_sc[:, a, :].bitcast(U8)[:, cols],
                         start=(a == 0),
                         stop=(a == 1),
                     )
@@ -144,12 +153,15 @@ def tile_list_htabg_mul_res_kernel(
         for i in range(PACK - 1):
             for lo in range(0, J, HALF):
                 pick(i, lo, lo + HALF)
-            if i < 2:
-                res_sb.append(held([P, N // P, HALF], F32, "res%d" % i, ("slot_d", "slot_e")[i]))
-                nc.sync.dma_start(res_sb[i][:], res_v[:, :, i * HALF : (i + 1) * HALF])
+            if i == 0:
+                res_sb.append(reuse0.tile([P, N // P, HALF], F32, name="res0", offset=R, align_bytes=64))
+                nc.sync.dma_start(res_sb[0][:], res_v[:, :, 0:HALF])
             if i == 1:
-                permute(w_sc[:, 0, :].bitcast(I32), wa_s[:], 2)
-                permute(wa_c[:].bitcast(I32), wa_raw[:], 4)
+                res_sb.append(held([P, N // P, HALF], F32, "res1", "slot_e"))
+                nc.sync.dma_start(res_sb[1][:], res_v[:, :, HALF:J])
+                wa_sc = reuse0.tile([P, R], U8, name="wa_sc", offset=0, align_bytes=64)
+                permute(wa_sc[:].bitcast(I32), wa_s[:], 1)
+                permute(wa_c[:].bitcast(I32), wa_raw[:], 2)
 
         def cast_wd(g):
             ch = slice(g * 256, (g + 1) * 256)
@@ -185,7 +197,7 @@ def tile_list_htabg_mul_res_kernel(
                     nc.tensor.matmul_mx(
                         out=ya[c, u][:, t, :],
                         lhsT=wa_c[:, 2 * t * P : 2 * (t + 1) * P].bitcast(FP4X4),
-                        lhsT_scale=w_sc[:, 0, ch],
+                        lhsT_scale=wa_sc[:, ch],
                         rhs=x_c[c][:, cols].bitcast(FP8X4),
                         rhs_scale=x_s[c][:, cols],
                         start=True,

@@ -31,9 +31,10 @@ def tile_list_htabg_mul_res_kernel(
     nc = tc.nc
     with ExitStack() as ctx:
         keep = ctx.enter_context(tc.tile_pool(name="keep", bufs=1))
-        ring = ctx.enter_context(tc.tile_pool(name="ring", bufs=3))
+        ring = ctx.enter_context(tc.tile_pool(name="ring", bufs=4))
         reuse = ctx.enter_context(tc.tile_pool(name="reuse", bufs=1))
         reuse0 = ctx.enter_context(tc.tile_pool(name="reuse0", bufs=1))
+        reuse1 = ctx.enter_context(tc.tile_pool(name="reuse1", bufs=1))
         psum = ctx.enter_context(tc.psum_pool(name="psum", bufs=4))
 
         def held(shape, dtype, name, tag=""):
@@ -41,15 +42,14 @@ def tile_list_htabg_mul_res_kernel(
 
         tab_list = keep.tile([P, J // LIST], U16, name="tab_list")
         head_lists = keep.tile([P, J // LIST], U16, name="head_lists")
-        tab_w = held([P, T], I32, "tab_w")
+        tab_w = reuse1.tile([P, T], I32, name="tab_w", offset=1024, align_bytes=64)
         tab_s = reuse.tile([P, T // 4], I32, name="tab_s", offset=PLANE_BYTES - 512, align_bytes=64)
-        wb_s = held([P, 2, R // 4], I32, "wb_s")
+        w_s = held([P, 3, R // 4], I32, "w_s")
         got_s = held([P, J], U8, "got_s")
         tab_sc = held([P, 2, J // 4], I32, "tab_sc")
         got_w = held([P, J], U32, "got_w")
         parted = held([P, 2, 2 * J], U8, "parted")
-        wb_raw = held([P, 2, R], I32, "wb_raw", "slot_c")
-        wa_c = held([P, 2 * R], U8, "wa_c")
+        wb_raw = held([P, 2, R], I32, "wb_raw")
         wb_c = held([P, 2, R], I32, "wb_c")
         wb_sc = held([P, 2, R], U8, "wb_sc")
         wgt = held([P, J], F32, "wgt")
@@ -58,17 +58,14 @@ def tile_list_htabg_mul_res_kernel(
             held([P, T], F32, "plane1", "slot_e"),
         ]
         wd_bf = held([P, N, PACK], BF16, "wd_bf")
-        wd_c = held([P, N], U32, "wd_c")
         wd_s = held([P, N], U8, "wd_s")
         picked = held([P, PACK, J], F32, "picked")
         yb_sb = held([P, J, PACK], F32, "yb_sb")
 
-        wa_s = held([P, R // 4], I32, "wa_s")
-        nc.gpsimd.memset(wb_s[:], 0)
-        nc.gpsimd.memset(wa_s[:], 0)
+        nc.gpsimd.memset(w_s[:], 0)
         for q in range(4):
             nc.vector.memset(tab_s[32 * q : 32 * q + 24, :], 0)
-        nc.vector.memset(tab_sc[:], 0)
+        nc.gpsimd.memset(tab_sc[:], 0)
 
         tab_scales_i = tab_scales.bitcast(I32)
         wa_scales_i = wa_scales.bitcast(I32)
@@ -83,46 +80,51 @@ def tile_list_htabg_mul_res_kernel(
             nc.sync.dma_start(tab_s[32 * q + 24 : 32 * q + 32, :], tab_scales_i[:, 4 * q : 4 * q + 4, :])
         nc.sync.dma_start(tab_w[:], tab_words[0].rearrange("p t b -> p (t b)").bitcast(I32))
         nc.sync.dma_start(wb_raw[:], wb_words.rearrange("a p r i -> p a (r i)").bitcast(I32))
-        nc.sync.dma_start(wgt[:], wgt2)
+        nc.sync.dma_start(planes[0][:], x_planes[0])
         nc.sync.dma_start(head_lists[:], offs2)
+        nc.sync.dma_start(wgt[:], wgt2)
         for q in range(4):
             nc.sync.dma_start(
-                wb_s[32 * q : 32 * q + 4, :, :], wb_scales_i[:, 4 * q : 4 * q + 4, :].rearrange("a r n -> r a n")
+                w_s[32 * q : 32 * q + 4, 0:2, :], wb_scales_i[:, 4 * q : 4 * q + 4, :].rearrange("a r n -> r a n")
             )
-            if q == 0:
-                nc.sync.dma_start(planes[0][:], x_planes[0])
         nc.sync.dma_start(planes[1][:], x_planes[1])
         for q in range(4):
-            nc.gpsimd.dma_start(wa_s[32 * q : 32 * q + 4, :], wa_scales_i[0, 4 * q : 4 * q + 4, :])
+            nc.sync.dma_start(w_s[32 * q : 32 * q + 4, 2, :], wa_scales_i[0, 4 * q : 4 * q + 4, :])
 
         nc.vector.tensor_copy(got_s[:], tab_s[:].bitcast(U8).indirect(tab_list[:]))
         for a in range(2):
             nc.scalar.dma_start(tab_sc[0:100, a, :], got_s[:].bitcast(I32)[24 + 4 * a : 124 + 4 * a, :])
         planes.append(reuse.tile([P, T], F32, name="plane2", offset=0, align_bytes=64))
-        nc.sync.dma_start(planes[2][:], x_planes[2])
-        planes.append(reuse.tile([P, T], F32, name="plane3", offset=PLANE_BYTES + 1024, align_bytes=64))
-        nc.sync.dma_start(planes[3][:], x_planes[3])
         wa_raw = reuse.tile([P, R // 2], I32, name="wa_raw", offset=PLANE_BYTES, align_bytes=64)
+        wd_raw = [reuse.tile([P, PACK, N // 2], F32, name="wd_raw0", offset=PLANE_BYTES + 1024, align_bytes=64)]
+
+        def load_wd(g):
+            for q in range(4):
+                nc.sync.dma_start(wd_raw[g][q:P:4, :, :], wd_v[q, :, :, g * 256 : (g + 1) * 256])
+
+        nc.sync.dma_start(planes[2][:], x_planes[2])
+        load_wd(0)
         nc.sync.dma_start(wa_raw[:], wa_words[0].bitcast(I32))
 
         nc.vector.tensor_copy(got_w[:], tab_w[:].bitcast(U32).indirect(tab_list[:]))
+        planes.append(reuse1.tile([P, T], F32, name="plane3", offset=0, align_bytes=64))
+        wd_raw.append(reuse1.tile([P, PACK, N // 2], F32, name="wd_raw1", offset=PLANE_BYTES, align_bytes=64))
+        nc.sync.dma_start(planes[3][:], x_planes[3])
+        load_wd(1)
 
         def permute(dst, src, run):
             nc.vector.tensor_copy(
-                dst.rearrange("p (t m q) -> p m t q", t=PACK, q=run),
-                src.rearrange("p (m t q) -> p m t q", t=PACK, q=run),
+                dst.rearrange("p (t m q) -> p t m q", t=PACK, q=run),
+                src.rearrange("p (m t q) -> p t m q", t=PACK, q=run),
             )
 
         permute(wb_c[:, 0, :], wb_raw[:, 0, :], 4)
         nc.vector.tensor_copy(parted[:].bitcast(U16), got_w[:].bitcast(U16).rearrange("p (j d) -> p d j", d=2))
         permute(wb_c[:, 1, :], wb_raw[:, 1, :], 4)
         nc.vector.tensor_copy(
-            wb_sc[:].bitcast(I32).rearrange("p a (t m) -> p a m t", t=PACK),
-            wb_s[:].rearrange("p a (m t) -> p a m t", t=PACK),
+            wb_sc[:].bitcast(I32).rearrange("p a (t m) -> p a t m", t=PACK),
+            w_s[:, 0:2, :].rearrange("p a (m t) -> p a t m", t=PACK),
         )
-        wd_raw = held([P, PACK, N], F32, "wd_raw", "slot_c")
-        for q in range(4):
-            nc.sync.dma_start(wd_raw[q:P:4, :, :], wd_v[q])
 
         for s in range(J // SUB):
             cols = slice(s * SUB, (s + 1) * SUB)
@@ -160,12 +162,19 @@ def tile_list_htabg_mul_res_kernel(
                 res_sb.append(held([P, N // P, HALF], F32, "res1", "slot_e"))
                 nc.sync.dma_start(res_sb[1][:], res_v[:, :, HALF:J])
                 wa_sc = reuse0.tile([P, R], U8, name="wa_sc", offset=0, align_bytes=64)
-                permute(wa_sc[:].bitcast(I32), wa_s[:], 1)
-                permute(wa_c[:].bitcast(I32), wa_raw[:], 2)
+                permute(wa_sc[:].bitcast(I32), w_s[:, 2, :], 1)
+        wd_c = reuse.tile([P, N], U32, name="wd_c", offset=0, align_bytes=64)
+        wa_c = reuse.tile([P, 2 * R], U8, name="wa_c", offset=4 * N, align_bytes=64)
+        permute(wa_c[:].bitcast(I32), wa_raw[:], 2)
+
+        def interleave(dst, src):
+            nc.scalar.copy(
+                dst.rearrange("p (c e) i -> p c i e", e=4), src.rearrange("p i (c e) -> p c i e", e=4)
+            )
 
         def cast_wd(g):
             ch = slice(g * 256, (g + 1) * 256)
-            nc.scalar.copy(wd_bf[:, ch, :], wd_raw[:, :, ch].rearrange("p i n -> p n i"))
+            interleave(wd_bf[:, ch, :], wd_raw[g][:])
 
         def quant_wd(g):
             ch = slice(g * 256, (g + 1) * 256)
@@ -181,7 +190,7 @@ def tile_list_htabg_mul_res_kernel(
             lo = c * CHUNK
             pick(PACK - 1, lo, lo + CHUNK)
             x_bf[c] = ring.tile([P, CHUNK, PACK], BF16, name="x_bf", align_bytes=64)
-            nc.scalar.copy(x_bf[c][:], picked[:, :, lo : lo + CHUNK].rearrange("p i n -> p n i"))
+            interleave(x_bf[c][:], picked[:, :, lo : lo + CHUNK])
 
         def quant_x(c):
             x_c[c] = ring.tile([P, CHUNK], U32, name="x_c", align_bytes=64)
@@ -221,19 +230,20 @@ def tile_list_htabg_mul_res_kernel(
             nc.vector.quantize_mx(
                 out=h_c[c][:].bitcast(FP8X4), scales=h_s[c][:], in_=h_bf[c][:].rearrange("p n i -> p (n i)")
             )
-            for g in range(2):
-                y[c, g] = psum.tile([P, 2, CHUNK], F32, name="second", tag="second")
-                for b in range(2):
-                    ch = slice((2 * g + b) * P, (2 * g + b + 1) * P)
-                    nc.tensor.matmul_mx(
-                        out=y[c, g][:, b, :],
-                        lhsT=wd_c[:, ch].bitcast(FP8X4),
-                        lhsT_scale=wd_s[:, ch],
-                        rhs=h_c[c][:].bitcast(FP8X4),
-                        rhs_scale=h_s[c][:],
-                        start=True,
-                        stop=True,
-                    )
+
+        def second(c, g):
+            y[c, g] = psum.tile([P, 2, CHUNK], F32, name="second", tag="second")
+            for b in range(2):
+                ch = slice((2 * g + b) * P, (2 * g + b + 1) * P)
+                nc.tensor.matmul_mx(
+                    out=y[c, g][:, b, :],
+                    lhsT=wd_c[:, ch].bitcast(FP8X4),
+                    lhsT_scale=wd_s[:, ch],
+                    rhs=h_c[c][:].bitcast(FP8X4),
+                    rhs_scale=h_s[c][:],
+                    start=True,
+                    stop=True,
+                )
 
         def finish(c):
             cols = slice(c * CHUNK, (c + 1) * CHUNK)
@@ -244,22 +254,26 @@ def tile_list_htabg_mul_res_kernel(
                 nc.sync.dma_start(out_v[:, blocks, cols], total[:])
 
         chunks = J // CHUNK
+        cast_wd(0)
         gather(0)
         gather(1)
-        cast_wd(0)
+        gather(2)
         cast_wd(1)
+        gather(3)
         quant_x(0)
-        for c in range(chunks + 1):
+        quant_x(1)
+        quant_wd(0)
+        for c in range(chunks):
+            product(c)
+            if c == 1:
+                quant_wd(1)
+                second(0, 1)
             if c + 2 < chunks:
-                gather(c + 2)
-            if c < chunks:
-                product(c)
-            if c + 1 < chunks:
-                quant_x(c + 1)
+                quant_x(c + 2)
             if c >= 1:
                 finish(c - 1)
-            if c == 0:
-                quant_wd(0)
-                quant_wd(1)
-            if c < chunks:
-                quant_h(c)
+            quant_h(c)
+            second(c, 0)
+            if c >= 1:
+                second(c, 1)
+        finish(chunks - 1)

@@ -245,13 +245,13 @@ def tile_list_htabg_mul_res_kernel(
                     stop=True,
                 )
 
-        def finish(c):
+        def finish(c, g, lo=0, hi=2, queue=nc.sync):
             cols = slice(c * CHUNK, (c + 1) * CHUNK)
-            for g in range(2):
-                blocks = slice(2 * g, 2 * g + 2)
-                total = ring.tile([P, 2, CHUNK], F32, name="total", bufs=4)
-                nc.vector.tensor_tensor(total[:], y[c, g][:], res_sb[c // 2][:, blocks, (c % 2) * CHUNK : (c % 2 + 1) * CHUNK], ADD)
-                nc.sync.dma_start(out_v[:, blocks, cols], total[:])
+            res_cols = slice((c % 2) * CHUNK, (c % 2 + 1) * CHUNK)
+            blocks = slice(2 * g + lo, 2 * g + hi)
+            total = ring.tile([P, hi - lo, CHUNK], F32, name="total", bufs=9)
+            nc.vector.tensor_tensor(total[:], y[c, g][:, lo:hi, :], res_sb[c // 2][:, blocks, res_cols], ADD)
+            queue.dma_start(out_v[:, blocks, cols], total[:])
 
         chunks = J // CHUNK
         cast_wd(0)
@@ -271,9 +271,14 @@ def tile_list_htabg_mul_res_kernel(
             if c + 2 < chunks:
                 quant_x(c + 2)
             if c >= 1:
-                finish(c - 1)
+                finish(c - 1, 0)
+            if 1 <= c < chunks - 1:
+                finish(c - 1, 1)
             quant_h(c)
             second(c, 0)
             if c >= 1:
                 second(c, 1)
-        finish(chunks - 1)
+        finish(chunks - 2, 1)
+        finish(chunks - 1, 0)
+        finish(chunks - 1, 1, 0, 1)
+        finish(chunks - 1, 1, 1, 2, nc.scalar)

@@ -23,6 +23,7 @@ CHUNK = 256
 HALF = 512
 LIST = 16
 PLANE_BYTES = 4 * T
+SCALE_ROW0 = 96
 
 
 def tile_list_htabg_mul_res_kernel(
@@ -32,39 +33,37 @@ def tile_list_htabg_mul_res_kernel(
     with ExitStack() as ctx:
         keep = ctx.enter_context(tc.tile_pool(name="keep", bufs=1))
         ring = ctx.enter_context(tc.tile_pool(name="ring", bufs=4))
-        reuse = ctx.enter_context(tc.tile_pool(name="reuse", bufs=1))
-        reuse0 = ctx.enter_context(tc.tile_pool(name="reuse0", bufs=1))
-        reuse1 = ctx.enter_context(tc.tile_pool(name="reuse1", bufs=1))
-        psum = ctx.enter_context(tc.psum_pool(name="psum", bufs=4))
+        after_words = ctx.enter_context(tc.tile_pool(name="after_words", bufs=1))
+        after_wb = ctx.enter_context(tc.tile_pool(name="after_wb", bufs=1))
+        psum = ctx.enter_context(tc.psum_pool(name="psum", bufs=8))
 
         def held(shape, dtype, name, tag=""):
             return keep.tile(shape, dtype, name=name, tag=tag or name, align_bytes=64)
 
         tab_list = keep.tile([P, J // LIST], U16, name="tab_list")
         head_lists = keep.tile([P, J // LIST], U16, name="head_lists")
-        tab_w = reuse1.tile([P, T], I32, name="tab_w", offset=1024, align_bytes=64)
-        tab_s = reuse.tile([P, T // 4], I32, name="tab_s", offset=PLANE_BYTES - 512, align_bytes=64)
-        w_s = held([P, 3, R // 4], I32, "w_s")
+        tab_s = held([P, T // 4], I32, "tab_s")
+        tab_w = after_words.tile([P, T], I32, name="tab_w", offset=2048, align_bytes=64)
+        wb_raw = after_wb.tile([P, 2, R], I32, name="wb_raw", offset=PLANE_BYTES - 2048, align_bytes=64)
+        wb_s = held([P, 2, R // 4], I32, "wb_s")
         got_s = held([P, J], U8, "got_s")
         tab_sc = held([P, 2, J // 4], I32, "tab_sc")
         got_w = held([P, J], U32, "got_w")
         parted = held([P, 2, 2 * J], U8, "parted")
-        wb_raw = held([P, 2, R], I32, "wb_raw")
         wb_c = held([P, 2, R], I32, "wb_c")
         wb_sc = held([P, 2, R], U8, "wb_sc")
+        wa_c = held([P, 2 * R], U8, "wa_c")
+        wa_sc = held([P, R], U8, "wa_sc")
         wgt = held([P, J], F32, "wgt")
-        planes = [
-            reuse0.tile([P, T], F32, name="plane0", offset=0, align_bytes=64),
-            held([P, T], F32, "plane1", "slot_e"),
-        ]
+        planes = [held([P, T], F32, "plane0", "slot0"), held([P, T], F32, "plane1", "slot1")]
         wd_bf = held([P, N, PACK], BF16, "wd_bf")
+        wd_c = held([P, N], U32, "wd_c")
         wd_s = held([P, N], U8, "wd_s")
         picked = held([P, PACK, J], F32, "picked")
         yb_sb = held([P, J, PACK], F32, "yb_sb")
 
-        nc.gpsimd.memset(w_s[:], 0)
-        for q in range(4):
-            nc.vector.memset(tab_s[32 * q : 32 * q + 24, :], 0)
+        nc.gpsimd.memset(wb_s[:], 0)
+        nc.vector.memset(tab_s[0:SCALE_ROW0, :], 0)
         nc.gpsimd.memset(tab_sc[:], 0)
 
         tab_scales_i = tab_scales.bitcast(I32)
@@ -76,59 +75,52 @@ def tile_list_htabg_mul_res_kernel(
         out_v = out.rearrange("(b m) j -> m b j", m=P)
 
         nc.sync.dma_start(tab_list[:], offs)
-        for q in range(4):
-            nc.sync.dma_start(tab_s[32 * q + 24 : 32 * q + 32, :], tab_scales_i[:, 4 * q : 4 * q + 4, :])
+        nc.sync.dma_start(tab_s[SCALE_ROW0:P, :], tab_scales_i.rearrange("a q n -> q a n"))
         nc.sync.dma_start(tab_w[:], tab_words[0].rearrange("p t b -> p (t b)").bitcast(I32))
         nc.sync.dma_start(wb_raw[:], wb_words.rearrange("a p r i -> p a (r i)").bitcast(I32))
-        nc.sync.dma_start(planes[0][:], x_planes[0])
         nc.sync.dma_start(head_lists[:], offs2)
         nc.sync.dma_start(wgt[:], wgt2)
+        nc.sync.dma_start(planes[0][:], x_planes[0])
         for q in range(4):
             nc.sync.dma_start(
-                w_s[32 * q : 32 * q + 4, 0:2, :], wb_scales_i[:, 4 * q : 4 * q + 4, :].rearrange("a r n -> r a n")
+                wb_s[32 * q : 32 * q + 4, :, :], wb_scales_i[:, 4 * q : 4 * q + 4, :].rearrange("a r n -> r a n")
             )
         nc.sync.dma_start(planes[1][:], x_planes[1])
-        for q in range(4):
-            nc.sync.dma_start(w_s[32 * q : 32 * q + 4, 2, :], wa_scales_i[0, 4 * q : 4 * q + 4, :])
 
         nc.vector.tensor_copy(got_s[:], tab_s[:].bitcast(U8).indirect(tab_list[:]))
-        for a in range(2):
-            nc.scalar.dma_start(tab_sc[0:100, a, :], got_s[:].bitcast(I32)[24 + 4 * a : 124 + 4 * a, :])
-        planes.append(reuse.tile([P, T], F32, name="plane2", offset=0, align_bytes=64))
-        wa_raw = reuse.tile([P, R // 2], I32, name="wa_raw", offset=PLANE_BYTES, align_bytes=64)
-        wd_raw = [reuse.tile([P, PACK, N // 2], F32, name="wd_raw0", offset=PLANE_BYTES + 1024, align_bytes=64)]
-
-        def load_wd(g):
-            for q in range(4):
-                nc.sync.dma_start(wd_raw[g][q:P:4, :, :], wd_v[q, :, :, g * 256 : (g + 1) * 256])
-
-        nc.sync.dma_start(planes[2][:], x_planes[2])
-        load_wd(0)
-        nc.sync.dma_start(wa_raw[:], wa_words[0].bitcast(I32))
+        for q in range(4):
+            row = SCALE_ROW0 + 8 * q
+            nc.scalar.dma_start(tab_sc[32 * q : 32 * q + 4, :, :], got_s[:].bitcast(I32)[row : row + 8, :])
 
         nc.vector.tensor_copy(got_w[:], tab_w[:].bitcast(U32).indirect(tab_list[:]))
-        planes.append(reuse1.tile([P, T], F32, name="plane3", offset=0, align_bytes=64))
-        wd_raw.append(reuse1.tile([P, PACK, N // 2], F32, name="wd_raw1", offset=PLANE_BYTES, align_bytes=64))
-        nc.sync.dma_start(planes[3][:], x_planes[3])
-        load_wd(1)
+        planes.append(after_words.tile([P, T], F32, name="plane2", offset=0, align_bytes=64))
+        wa_raw = after_words.tile([P, R // 2], I32, name="wa_raw", offset=PLANE_BYTES, align_bytes=64)
+        wa_s = after_words.tile([P, R // 4], I32, name="wa_s", offset=PLANE_BYTES + 1024, align_bytes=64)
+        nc.gpsimd.memset(wa_s[:], 0)
+        nc.sync.dma_start(planes[2][:], x_planes[2])
+        nc.sync.dma_start(wa_raw[:], wa_words[0].bitcast(I32))
+        for q in range(4):
+            nc.sync.dma_start(wa_s[32 * q : 32 * q + 4, :], wa_scales_i[0, 4 * q : 4 * q + 4, :])
 
         def permute(dst, src, run):
             nc.vector.tensor_copy(
-                dst.rearrange("p (t m q) -> p t m q", t=PACK, q=run),
-                src.rearrange("p (m t q) -> p t m q", t=PACK, q=run),
+                dst.rearrange("p (a t m q) -> p a t m q", t=PACK, m=32, q=run),
+                src.rearrange("p (a m t q) -> p a t m q", t=PACK, m=32, q=run),
             )
 
-        permute(wb_c[:, 0, :], wb_raw[:, 0, :], 4)
         nc.vector.tensor_copy(parted[:].bitcast(U16), got_w[:].bitcast(U16).rearrange("p (j d) -> p d j", d=2))
-        permute(wb_c[:, 1, :], wb_raw[:, 1, :], 4)
-        nc.vector.tensor_copy(
-            wb_sc[:].bitcast(I32).rearrange("p a (t m) -> p a t m", t=PACK),
-            w_s[:, 0:2, :].rearrange("p a (m t) -> p a t m", t=PACK),
-        )
+        permute(wb_c[:].rearrange("p a r -> p (a r)"), wb_raw[:].rearrange("p a r -> p (a r)"), 4)
+        permute(wb_sc[:].rearrange("p a r -> p (a r)").bitcast(I32), wb_s[:].rearrange("p a r -> p (a r)"), 1)
+
+        planes.append(after_wb.tile([P, T], F32, name="plane3", offset=0, align_bytes=64))
+        wd_raw = after_wb.tile([P, PACK, N], F32, name="wd_raw", offset=PLANE_BYTES, align_bytes=64)
+        nc.sync.dma_start(planes[3][:], x_planes[3])
+        for q in range(4):
+            nc.sync.dma_start(wd_raw[q:P:4, :, :], wd_v[q])
 
         for s in range(J // SUB):
             cols = slice(s * SUB, (s + 1) * SUB)
-            bank = psum.tile([P, PACK, SUB], F32, name="first", tag="first")
+            bank = psum.tile([P, PACK, SUB], F32, name="yb", tag="bank")
             for t in range(PACK):
                 ch = slice(t * P, (t + 1) * P)
                 for a in range(2):
@@ -153,19 +145,12 @@ def tile_list_htabg_mul_res_kernel(
 
         res_sb = []
         for i in range(PACK - 1):
-            for lo in range(0, J, HALF):
-                pick(i, lo, lo + HALF)
-            if i == 0:
-                res_sb.append(reuse0.tile([P, N // P, HALF], F32, name="res0", offset=R, align_bytes=64))
-                nc.sync.dma_start(res_sb[0][:], res_v[:, :, 0:HALF])
-            if i == 1:
-                res_sb.append(held([P, N // P, HALF], F32, "res1", "slot_e"))
-                nc.sync.dma_start(res_sb[1][:], res_v[:, :, HALF:J])
-                wa_sc = reuse0.tile([P, R], U8, name="wa_sc", offset=0, align_bytes=64)
-                permute(wa_sc[:].bitcast(I32), w_s[:, 2, :], 1)
-        wd_c = reuse.tile([P, N], U32, name="wd_c", offset=0, align_bytes=64)
-        wa_c = reuse.tile([P, 2 * R], U8, name="wa_c", offset=4 * N, align_bytes=64)
+            pick(i, 0, J)
+            if i < 2:
+                res_sb.append(held([P, N // P, HALF], F32, "res%d" % i, "slot%d" % i))
+                nc.sync.dma_start(res_sb[i][:], res_v[:, :, i * HALF : (i + 1) * HALF])
         permute(wa_c[:].bitcast(I32), wa_raw[:], 2)
+        permute(wa_sc[:].bitcast(I32), wa_s[:], 1)
 
         def interleave(dst, src):
             nc.scalar.copy(
@@ -174,7 +159,7 @@ def tile_list_htabg_mul_res_kernel(
 
         def cast_wd(g):
             ch = slice(g * 256, (g + 1) * 256)
-            interleave(wd_bf[:, ch, :], wd_raw[g][:])
+            interleave(wd_bf[:, ch, :], wd_raw[:, :, ch])
 
         def quant_wd(g):
             ch = slice(g * 256, (g + 1) * 256)
@@ -200,7 +185,7 @@ def tile_list_htabg_mul_res_kernel(
             )
             for u in range(CHUNK // SUB):
                 cols = slice(u * SUB, (u + 1) * SUB)
-                ya[c, u] = psum.tile([P, PACK, SUB], F32, name="first", tag="first")
+                ya[c, u] = psum.tile([P, PACK, SUB], F32, name="ya", tag="bank")
                 for t in range(PACK):
                     ch = slice(t * P, (t + 1) * P)
                     nc.tensor.matmul_mx(
@@ -232,7 +217,7 @@ def tile_list_htabg_mul_res_kernel(
             )
 
         def second(c, g):
-            y[c, g] = psum.tile([P, 2, CHUNK], F32, name="second", tag="second")
+            y[c, g] = psum.tile([P, 2, CHUNK], F32, name="y", tag="bank")
             for b in range(2):
                 ch = slice((2 * g + b) * P, (2 * g + b + 1) * P)
                 nc.tensor.matmul_mx(
@@ -254,31 +239,29 @@ def tile_list_htabg_mul_res_kernel(
             queue.dma_start(out_v[:, blocks, cols], total[:])
 
         chunks = J // CHUNK
+        for c in range(chunks):
+            gather(c)
         cast_wd(0)
-        gather(0)
-        gather(1)
-        gather(2)
         cast_wd(1)
-        gather(3)
         quant_x(0)
         quant_x(1)
-        quant_wd(0)
         for c in range(chunks):
             product(c)
-            if c == 1:
-                quant_wd(1)
-                second(0, 1)
             if c + 2 < chunks:
                 quant_x(c + 2)
             if c >= 1:
-                finish(c - 1, 0)
-            if 1 <= c < chunks - 1:
-                finish(c - 1, 1)
-            quant_h(c)
+                quant_h(c - 1)
+            if c == 2:
+                quant_wd(0)
+                quant_wd(1)
+        for c in range(chunks):
+            if c == chunks - 1:
+                quant_h(c)
             second(c, 0)
-            if c >= 1:
-                second(c, 1)
-        finish(chunks - 2, 1)
-        finish(chunks - 1, 0)
+            second(c, 1)
+        for c in range(chunks):
+            finish(c, 0)
+            if c < chunks - 1:
+                finish(c, 1)
         finish(chunks - 1, 1, 0, 1)
         finish(chunks - 1, 1, 1, 2, nc.scalar)

@@ -35,6 +35,8 @@ def tile_list_htabg_mul_res_kernel(
         ring = ctx.enter_context(tc.tile_pool(name="ring", bufs=4))
         after_words = ctx.enter_context(tc.tile_pool(name="after_words", bufs=1))
         after_wb = ctx.enter_context(tc.tile_pool(name="after_wb", bufs=1))
+        after_pick = ctx.enter_context(tc.tile_pool(name="after_pick", bufs=1))
+        after_wd = ctx.enter_context(tc.tile_pool(name="after_wd", bufs=1))
         psum = ctx.enter_context(tc.psum_pool(name="psum", bufs=8))
 
         def held(shape, dtype, name, tag=""):
@@ -42,7 +44,7 @@ def tile_list_htabg_mul_res_kernel(
 
         tab_list = keep.tile([P, J // LIST], U16, name="tab_list")
         head_lists = keep.tile([P, J // LIST], U16, name="head_lists")
-        tab_s = held([P, T // 4], I32, "tab_s")
+        tab_s = held([P, T // 4], I32, "tab_s", "slot1")
         tab_w = after_words.tile([P, T], I32, name="tab_w", offset=2048, align_bytes=64)
         wb_raw = after_wb.tile([P, 2, R], I32, name="wb_raw", offset=PLANE_BYTES - 2048, align_bytes=64)
         wb_s = held([P, 2, R // 4], I32, "wb_s")
@@ -55,8 +57,13 @@ def tile_list_htabg_mul_res_kernel(
         wa_c = held([P, 2 * R], U8, "wa_c")
         wa_sc = held([P, R], U8, "wa_sc")
         wgt = held([P, J], F32, "wgt")
-        planes = [held([P, T], F32, "plane0", "slot0"), held([P, T], F32, "plane1", "slot1")]
-        wd_bf = held([P, N, PACK], BF16, "wd_bf")
+        planes = [
+            after_pick.tile([P, T], F32, name="plane0", offset=2048, align_bytes=64),
+        ]
+        wd_bf = [
+            held([P, N // 2, PACK], BF16, "wd_bf0", "h1"),
+            after_wd.tile([P, N // 2, PACK], BF16, name="wd_bf1", offset=0, align_bytes=64),
+        ]
         wd_c = held([P, N], U32, "wd_c")
         wd_s = held([P, N], U8, "wd_s")
         picked = held([P, PACK, J], F32, "picked")
@@ -76,21 +83,23 @@ def tile_list_htabg_mul_res_kernel(
 
         nc.sync.dma_start(tab_list[:], offs)
         nc.sync.dma_start(tab_s[SCALE_ROW0:P, :], tab_scales_i.rearrange("a q n -> q a n"))
+        nc.sync.dma_start(head_lists[:], offs2)
         nc.sync.dma_start(tab_w[:], tab_words[0].rearrange("p t b -> p (t b)").bitcast(I32))
         nc.sync.dma_start(wb_raw[:], wb_words.rearrange("a p r i -> p a (r i)").bitcast(I32))
-        nc.sync.dma_start(head_lists[:], offs2)
-        nc.sync.dma_start(wgt[:], wgt2)
-        nc.sync.dma_start(planes[0][:], x_planes[0])
         for q in range(4):
             nc.sync.dma_start(
                 wb_s[32 * q : 32 * q + 4, :, :], wb_scales_i[:, 4 * q : 4 * q + 4, :].rearrange("a r n -> r a n")
             )
-        nc.sync.dma_start(planes[1][:], x_planes[1])
+        nc.sync.dma_start(wgt[:], wgt2)
+        nc.sync.dma_start(planes[0][:], x_planes[0])
 
         nc.vector.tensor_copy(got_s[:], tab_s[:].bitcast(U8).indirect(tab_list[:]))
         for q in range(4):
             row = SCALE_ROW0 + 8 * q
-            nc.scalar.dma_start(tab_sc[32 * q : 32 * q + 4, :, :], got_s[:].bitcast(I32)[row : row + 8, :])
+            nc.sync.dma_start(tab_sc[32 * q : 32 * q + 4, :, :], got_s[:].bitcast(I32)[row : row + 8, :])
+
+        planes.append(held([P, T], F32, "plane1", "slot1"))
+        nc.sync.dma_start(planes[1][:], x_planes[1])
 
         nc.vector.tensor_copy(got_w[:], tab_w[:].bitcast(U32).indirect(tab_list[:]))
         planes.append(after_words.tile([P, T], F32, name="plane2", offset=0, align_bytes=64))
@@ -113,10 +122,14 @@ def tile_list_htabg_mul_res_kernel(
         permute(wb_sc[:].rearrange("p a r -> p (a r)").bitcast(I32), wb_s[:].rearrange("p a r -> p (a r)"), 1)
 
         planes.append(after_wb.tile([P, T], F32, name="plane3", offset=0, align_bytes=64))
-        wd_raw = after_wb.tile([P, PACK, N], F32, name="wd_raw", offset=PLANE_BYTES, align_bytes=64)
+        wd_raw = [after_wb.tile([P, PACK, N // 2], F32, name="wd_raw0", offset=PLANE_BYTES, align_bytes=64)]
+
+        def load_wd(g):
+            for q in range(4):
+                nc.sync.dma_start(wd_raw[g][q:P:4, :, :], wd_v[q, :, :, g * 256 : (g + 1) * 256])
+
         nc.sync.dma_start(planes[3][:], x_planes[3])
-        for q in range(4):
-            nc.sync.dma_start(wd_raw[q:P:4, :, :], wd_v[q])
+        load_wd(0)
 
         for s in range(J // SUB):
             cols = slice(s * SUB, (s + 1) * SUB)
@@ -146,9 +159,15 @@ def tile_list_htabg_mul_res_kernel(
         res_sb = []
         for i in range(PACK - 1):
             pick(i, 0, J)
+            if i == 0:
+                wd_raw.append(after_pick.tile([P, PACK, N // 2], F32, name="wd_raw1", offset=0, align_bytes=64))
+                res_sb.append(after_pick.tile([P, N // P, HALF], F32, name="res0", offset=4096, align_bytes=64))
+            if i == 1:
+                res_sb.append(held([P, N // P, HALF], F32, "res1", "slot1"))
             if i < 2:
-                res_sb.append(held([P, N // P, HALF], F32, "res%d" % i, "slot%d" % i))
                 nc.sync.dma_start(res_sb[i][:], res_v[:, :, i * HALF : (i + 1) * HALF])
+            if i == 0:
+                load_wd(1)
         permute(wa_c[:].bitcast(I32), wa_raw[:], 2)
         permute(wa_sc[:].bitcast(I32), wa_s[:], 1)
 
@@ -158,15 +177,14 @@ def tile_list_htabg_mul_res_kernel(
             )
 
         def cast_wd(g):
-            ch = slice(g * 256, (g + 1) * 256)
-            interleave(wd_bf[:, ch, :], wd_raw[:, :, ch])
+            interleave(wd_bf[g][:], wd_raw[g][:])
 
         def quant_wd(g):
             ch = slice(g * 256, (g + 1) * 256)
             nc.vector.quantize_mx(
                 out=wd_c[:, ch].bitcast(FP8X4),
                 scales=wd_s[:, ch],
-                in_=wd_bf[:, ch, :].rearrange("p n i -> p (n i)"),
+                in_=wd_bf[g][:].rearrange("p n i -> p (n i)"),
             )
 
         x_bf, x_c, x_s, h_bf, h_c, h_s, ya, y = {}, {}, {}, {}, {}, {}, {}, {}
@@ -174,7 +192,12 @@ def tile_list_htabg_mul_res_kernel(
         def gather(c):
             lo = c * CHUNK
             pick(PACK - 1, lo, lo + CHUNK)
-            x_bf[c] = ring.tile([P, CHUNK, PACK], BF16, name="x_bf", align_bytes=64)
+            if c == 2:
+                x_bf[c] = after_wb.tile([P, CHUNK, PACK], BF16, name="x_bf2", offset=PLANE_BYTES + 2048, align_bytes=64)
+            elif c == 3:
+                x_bf[c] = held([P, CHUNK, PACK], BF16, "x_bf3", "x3")
+            else:
+                x_bf[c] = ring.tile([P, CHUNK, PACK], BF16, name="x_bf", align_bytes=64)
             interleave(x_bf[c][:], picked[:, :, lo : lo + CHUNK])
 
         def quant_x(c):
@@ -199,7 +222,10 @@ def tile_list_htabg_mul_res_kernel(
                     )
 
         def product(c):
-            h_bf[c] = ring.tile([P, CHUNK, PACK], BF16, name="h_bf", align_bytes=64)
+            if c == 3:
+                h_bf[c] = after_wd.tile([P, CHUNK, PACK], BF16, name="h_bf3", offset=1024, align_bytes=64)
+            else:
+                h_bf[c] = held([P, CHUNK, PACK], BF16, "h_bf%d" % c, "h%d" % c)
             for u in range(CHUNK // SUB):
                 lo = c * CHUNK + u * SUB
                 nc.vector.tensor_tensor(
@@ -210,7 +236,10 @@ def tile_list_htabg_mul_res_kernel(
                 )
 
         def quant_h(c):
-            h_c[c] = ring.tile([P, CHUNK], U32, name="h_c", align_bytes=64)
+            if c == 2:
+                h_c[c] = after_wd.tile([P, CHUNK], U32, name="h_c2", offset=0, align_bytes=64)
+            else:
+                h_c[c] = ring.tile([P, CHUNK], U32, name="h_c", align_bytes=64)
             h_s[c] = ring.tile([P, CHUNK], U8, name="h_s", align_bytes=64)
             nc.vector.quantize_mx(
                 out=h_c[c][:].bitcast(FP8X4), scales=h_s[c][:], in_=h_bf[c][:].rearrange("p n i -> p (n i)")
@@ -238,30 +267,52 @@ def tile_list_htabg_mul_res_kernel(
             nc.vector.tensor_tensor(total[:], y[c, g][:, lo:hi, :], res_sb[c // 2][:, blocks, res_cols], ADD)
             queue.dma_start(out_v[:, blocks, cols], total[:])
 
-        chunks = J // CHUNK
-        for c in range(chunks):
-            gather(c)
+        def finish_beside(c, g, total):
+            cols = slice(c * CHUNK, (c + 1) * CHUNK)
+            res_cols = slice((c % 2) * CHUNK, (c % 2 + 1) * CHUNK)
+            blocks = slice(2 * g, 2 * g + 2)
+            if (c, g) == (1, 0):
+                y_sb = after_pick.tile([P, 2, CHUNK], F32, name="y_sb1", offset=0, align_bytes=64)
+            else:
+                y_sb = ring.tile([P, 2, CHUNK], F32, name="y_sb", align_bytes=64)
+            nc.scalar.copy(y_sb[:], y[c, g][:])
+            nc.gpsimd.tensor_tensor(total[:], y_sb[:], res_sb[c // 2][:, blocks, res_cols], ADD)
+            nc.sync.dma_start(out_v[:, blocks, cols], total[:])
+
+        gather(0)
+        gather(1)
         cast_wd(0)
-        cast_wd(1)
+        gather(2)
+        gather(3)
         quant_x(0)
         quant_x(1)
-        for c in range(chunks):
-            product(c)
-            if c + 2 < chunks:
-                quant_x(c + 2)
-            if c >= 1:
-                quant_h(c - 1)
-            if c == 2:
-                quant_wd(0)
-                quant_wd(1)
-        for c in range(chunks):
-            if c == chunks - 1:
-                quant_h(c)
-            second(c, 0)
-            second(c, 1)
-        for c in range(chunks):
-            finish(c, 0)
-            if c < chunks - 1:
-                finish(c, 1)
-        finish(chunks - 1, 1, 0, 1)
-        finish(chunks - 1, 1, 1, 2, nc.scalar)
+        product(0)
+        quant_wd(0)
+        quant_h(0)
+        second(0, 0)
+        quant_x(2)
+        product(1)
+        quant_x(3)
+        quant_h(1)
+        second(1, 0)
+        finish_beside(0, 0, held([P, 2, CHUNK], F32, "total0", "h1"))
+        cast_wd(1)
+        product(2)
+        quant_wd(1)
+        second(0, 1)
+        second(1, 1)
+        quant_h(2)
+        second(2, 0)
+        second(2, 1)
+        finish_beside(1, 0, held([P, 2, CHUNK], F32, "total1", "h2"))
+        product(3)
+        finish(0, 1)
+        quant_h(3)
+        second(3, 0)
+        second(3, 1)
+        finish_beside(1, 1, after_wd.tile([P, 2, CHUNK], F32, name="total2", offset=1024, align_bytes=64))
+        finish(2, 0)
+        finish(2, 1)
+        finish(3, 0)
+        finish(3, 1, 0, 1)
+        finish(3, 1, 1, 2, nc.scalar)

@@ -1,6 +1,7 @@
 from contextlib import ExitStack
 
 import concourse.mybir as mybir
+from concourse.masks import make_identity
 
 K, L, R, N, T, J = 512, 1024, 512, 512, 2048, 1024
 FLOPS = 2 * J * (K * R + L * R + R * N)
@@ -35,8 +36,7 @@ def tile_list_htabg_mul_res_kernel(
         ring = ctx.enter_context(tc.tile_pool(name="ring", bufs=4))
         after_words = ctx.enter_context(tc.tile_pool(name="after_words", bufs=1))
         after_wb = ctx.enter_context(tc.tile_pool(name="after_wb", bufs=1))
-        after_pick = ctx.enter_context(tc.tile_pool(name="after_pick", bufs=1))
-        after_wd = ctx.enter_context(tc.tile_pool(name="after_wd", bufs=1))
+        after_scales = ctx.enter_context(tc.tile_pool(name="after_scales", bufs=1))
         psum = ctx.enter_context(tc.psum_pool(name="psum", bufs=8))
 
         def held(shape, dtype, name, tag=""):
@@ -44,7 +44,7 @@ def tile_list_htabg_mul_res_kernel(
 
         tab_list = keep.tile([P, J // LIST], U16, name="tab_list")
         head_lists = keep.tile([P, J // LIST], U16, name="head_lists")
-        tab_s = held([P, T // 4], I32, "tab_s", "slot1")
+        tab_s = after_scales.tile([P, T // 4], I32, name="tab_s", offset=PLANE_BYTES - 1024, align_bytes=64)
         tab_w = after_words.tile([P, T], I32, name="tab_w", offset=2048, align_bytes=64)
         wb_raw = after_wb.tile([P, 2, R], I32, name="wb_raw", offset=PLANE_BYTES - 2048, align_bytes=64)
         wb_s = held([P, 2, R // 4], I32, "wb_s")
@@ -54,23 +54,20 @@ def tile_list_htabg_mul_res_kernel(
         parted = held([P, 2, 2 * J], U8, "parted")
         wb_c = held([P, 2, R], I32, "wb_c")
         wb_sc = held([P, 2, R], U8, "wb_sc")
-        wa_c = held([P, 2 * R], U8, "wa_c")
         wa_sc = held([P, R], U8, "wa_sc")
         wgt = held([P, J], F32, "wgt")
-        planes = [
-            after_pick.tile([P, T], F32, name="plane0", offset=2048, align_bytes=64),
-        ]
-        wd_bf = [
-            held([P, N // 2, PACK], BF16, "wd_bf0", "h1"),
-            after_wd.tile([P, N // 2, PACK], BF16, name="wd_bf1", offset=0, align_bytes=64),
-        ]
-        wd_c = held([P, N], U32, "wd_c")
+        w_rows = held([P, P], F32, "w_rows")
+        w_cols = held([P, J // P, P], F32, "w_cols")
+        ident = held([P, P], F32, "ident")
+        planes = [held([P, T], F32, "plane0", "slot0")]
         wd_s = held([P, N], U8, "wd_s")
         picked = held([P, PACK, J], F32, "picked")
         yb_sb = held([P, J, PACK], F32, "yb_sb")
 
         nc.gpsimd.memset(wb_s[:], 0)
         nc.vector.memset(tab_s[0:SCALE_ROW0, :], 0)
+        nc.vector.memset(w_rows[64:P, :], 0.0)
+        make_identity(nc, ident[:])
         nc.gpsimd.memset(tab_sc[:], 0)
 
         tab_scales_i = tab_scales.bitcast(I32)
@@ -83,33 +80,50 @@ def tile_list_htabg_mul_res_kernel(
 
         nc.sync.dma_start(tab_list[:], offs)
         nc.sync.dma_start(tab_s[SCALE_ROW0:P, :], tab_scales_i.rearrange("a q n -> q a n"))
-        nc.sync.dma_start(head_lists[:], offs2)
+        nc.sync.dma_start(w_rows[0:64, :], wgt2.rearrange("(g r) (c m) -> g r c m", r=LIST, m=P)[:, 0])
         nc.sync.dma_start(tab_w[:], tab_words[0].rearrange("p t b -> p (t b)").bitcast(I32))
         nc.sync.dma_start(wb_raw[:], wb_words.rearrange("a p r i -> p a (r i)").bitcast(I32))
         for q in range(4):
             nc.sync.dma_start(
                 wb_s[32 * q : 32 * q + 4, :, :], wb_scales_i[:, 4 * q : 4 * q + 4, :].rearrange("a r n -> r a n")
             )
-        nc.sync.dma_start(wgt[:], wgt2)
+        nc.sync.dma_start(head_lists[:], offs2)
         nc.sync.dma_start(planes[0][:], x_planes[0])
+
+        turned = psum.tile([P, P], F32, name="turned", tag="bank")
+        nc.tensor.transpose(turned[:], w_rows[:], ident[:])
+        nc.scalar.copy(
+            w_cols[:].rearrange("m c (g r) -> m c g r", r=LIST),
+            turned[:, 0:64].rearrange("m (g c) -> m c g", c=J // P).unsqueeze(3).to_broadcast([P, J // P, 8, LIST]),
+        )
+        for half in range(2):
+            spread = psum.tile([P, PACK, P], F32, name="spread", tag="bank")
+            for c in range(PACK):
+                nc.tensor.transpose(spread[:, c, :], w_cols[:, PACK * half + c, :], ident[:])
+            nc.scalar.copy(wgt[:, half * HALF : (half + 1) * HALF], spread[:].rearrange("p c m -> p (c m)"))
 
         nc.vector.tensor_copy(got_s[:], tab_s[:].bitcast(U8).indirect(tab_list[:]))
         for q in range(4):
             row = SCALE_ROW0 + 8 * q
             nc.sync.dma_start(tab_sc[32 * q : 32 * q + 4, :, :], got_s[:].bitcast(I32)[row : row + 8, :])
 
-        planes.append(held([P, T], F32, "plane1", "slot1"))
+        planes.append(after_scales.tile([P, T], F32, name="plane1", offset=0, align_bytes=64))
+        wa_s = after_scales.tile([P, R // 4], I32, name="wa_s", offset=PLANE_BYTES, align_bytes=64)
+        nc.gpsimd.memset(wa_s[:], 0)
         nc.sync.dma_start(planes[1][:], x_planes[1])
+        for q in range(4):
+            nc.sync.dma_start(wa_s[32 * q : 32 * q + 4, :], wa_scales_i[0, 4 * q : 4 * q + 4, :])
 
         nc.vector.tensor_copy(got_w[:], tab_w[:].bitcast(U32).indirect(tab_list[:]))
         planes.append(after_words.tile([P, T], F32, name="plane2", offset=0, align_bytes=64))
-        wa_raw = after_words.tile([P, R // 2], I32, name="wa_raw", offset=PLANE_BYTES, align_bytes=64)
-        wa_s = after_words.tile([P, R // 4], I32, name="wa_s", offset=PLANE_BYTES + 1024, align_bytes=64)
-        nc.gpsimd.memset(wa_s[:], 0)
+        wd_raw = [after_words.tile([P, PACK, N // 2], F32, name="wd_raw0", offset=PLANE_BYTES, align_bytes=64)]
+
+        def load_wd(g):
+            for q in range(4):
+                nc.sync.dma_start(wd_raw[g][q:P:4, :, :], wd_v[q, :, :, g * 256 : (g + 1) * 256])
+
         nc.sync.dma_start(planes[2][:], x_planes[2])
-        nc.sync.dma_start(wa_raw[:], wa_words[0].bitcast(I32))
-        for q in range(4):
-            nc.sync.dma_start(wa_s[32 * q : 32 * q + 4, :], wa_scales_i[0, 4 * q : 4 * q + 4, :])
+        load_wd(0)
 
         def permute(dst, src, run):
             nc.vector.tensor_copy(
@@ -117,19 +131,16 @@ def tile_list_htabg_mul_res_kernel(
                 src.rearrange("p (a m t q) -> p a t m q", t=PACK, m=32, q=run),
             )
 
-        nc.vector.tensor_copy(parted[:].bitcast(U16), got_w[:].bitcast(U16).rearrange("p (j d) -> p d j", d=2))
         permute(wb_c[:].rearrange("p a r -> p (a r)"), wb_raw[:].rearrange("p a r -> p (a r)"), 4)
+        nc.vector.tensor_copy(parted[:].bitcast(U16), got_w[:].bitcast(U16).rearrange("p (j d) -> p d j", d=2))
         permute(wb_sc[:].rearrange("p a r -> p (a r)").bitcast(I32), wb_s[:].rearrange("p a r -> p (a r)"), 1)
 
         planes.append(after_wb.tile([P, T], F32, name="plane3", offset=0, align_bytes=64))
-        wd_raw = [after_wb.tile([P, PACK, N // 2], F32, name="wd_raw0", offset=PLANE_BYTES, align_bytes=64)]
-
-        def load_wd(g):
-            for q in range(4):
-                nc.sync.dma_start(wd_raw[g][q:P:4, :, :], wd_v[q, :, :, g * 256 : (g + 1) * 256])
-
+        wa_raw = after_wb.tile([P, R // 2], I32, name="wa_raw", offset=PLANE_BYTES, align_bytes=64)
+        wd_raw.append(after_wb.tile([P, PACK, N // 2], F32, name="wd_raw1", offset=PLANE_BYTES + 1024, align_bytes=64))
         nc.sync.dma_start(planes[3][:], x_planes[3])
-        load_wd(0)
+        nc.sync.dma_start(wa_raw[:], wa_words[0].bitcast(I32))
+        load_wd(1)
 
         for s in range(J // SUB):
             cols = slice(s * SUB, (s + 1) * SUB)
@@ -160,15 +171,11 @@ def tile_list_htabg_mul_res_kernel(
         for i in range(PACK - 1):
             pick(i, 0, J)
             if i == 0:
-                wd_raw.append(after_pick.tile([P, PACK, N // 2], F32, name="wd_raw1", offset=0, align_bytes=64))
-                res_sb.append(after_pick.tile([P, N // P, HALF], F32, name="res0", offset=4096, align_bytes=64))
+                res_sb.append(held([P, N // P, HALF], F32, "res0", "slot0"))
             if i == 1:
-                res_sb.append(held([P, N // P, HALF], F32, "res1", "slot1"))
+                res_sb.append(after_scales.tile([P, N // P, HALF], F32, name="res1", offset=0, align_bytes=64))
             if i < 2:
                 nc.sync.dma_start(res_sb[i][:], res_v[:, :, i * HALF : (i + 1) * HALF])
-            if i == 0:
-                load_wd(1)
-        permute(wa_c[:].bitcast(I32), wa_raw[:], 2)
         permute(wa_sc[:].bitcast(I32), wa_s[:], 1)
 
         def interleave(dst, src):
@@ -176,7 +183,10 @@ def tile_list_htabg_mul_res_kernel(
                 dst.rearrange("p (c e) i -> p c i e", e=4), src.rearrange("p i (c e) -> p c i e", e=4)
             )
 
+        wd_bf = {}
+
         def cast_wd(g):
+            wd_bf[g] = held([P, N // 2, PACK], BF16, "wd_bf%d" % g, ("wd_bf0", "picked")[g])
             interleave(wd_bf[g][:], wd_raw[g][:])
 
         def quant_wd(g):
@@ -191,13 +201,9 @@ def tile_list_htabg_mul_res_kernel(
 
         def gather(c):
             lo = c * CHUNK
-            pick(PACK - 1, lo, lo + CHUNK)
-            if c == 2:
-                x_bf[c] = after_wb.tile([P, CHUNK, PACK], BF16, name="x_bf2", offset=PLANE_BYTES + 2048, align_bytes=64)
-            elif c == 3:
-                x_bf[c] = held([P, CHUNK, PACK], BF16, "x_bf3", "x3")
-            else:
-                x_bf[c] = ring.tile([P, CHUNK, PACK], BF16, name="x_bf", align_bytes=64)
+            if c < 3:
+                pick(PACK - 1, lo, J if c == 2 else lo + CHUNK)
+            x_bf[c] = held([P, CHUNK, PACK], BF16, "x_bf%d" % c, ("wd_c", "h0", "x2", "x3")[c])
             interleave(x_bf[c][:], picked[:, :, lo : lo + CHUNK])
 
         def quant_x(c):
@@ -222,10 +228,7 @@ def tile_list_htabg_mul_res_kernel(
                     )
 
         def product(c):
-            if c == 3:
-                h_bf[c] = after_wd.tile([P, CHUNK, PACK], BF16, name="h_bf3", offset=1024, align_bytes=64)
-            else:
-                h_bf[c] = held([P, CHUNK, PACK], BF16, "h_bf%d" % c, "h%d" % c)
+            h_bf[c] = held([P, CHUNK, PACK], BF16, "h_bf%d" % c, ("h0", "h1", "picked", "h3")[c])
             for u in range(CHUNK // SUB):
                 lo = c * CHUNK + u * SUB
                 nc.vector.tensor_tensor(
@@ -236,10 +239,7 @@ def tile_list_htabg_mul_res_kernel(
                 )
 
         def quant_h(c):
-            if c == 2:
-                h_c[c] = after_wd.tile([P, CHUNK], U32, name="h_c2", offset=0, align_bytes=64)
-            else:
-                h_c[c] = ring.tile([P, CHUNK], U32, name="h_c", align_bytes=64)
+            h_c[c] = ring.tile([P, CHUNK], U32, name="h_c", align_bytes=64)
             h_s[c] = ring.tile([P, CHUNK], U8, name="h_s", align_bytes=64)
             nc.vector.quantize_mx(
                 out=h_c[c][:].bitcast(FP8X4), scales=h_s[c][:], in_=h_bf[c][:].rearrange("p n i -> p (n i)")
@@ -271,46 +271,47 @@ def tile_list_htabg_mul_res_kernel(
             cols = slice(c * CHUNK, (c + 1) * CHUNK)
             res_cols = slice((c % 2) * CHUNK, (c % 2 + 1) * CHUNK)
             blocks = slice(2 * g, 2 * g + 2)
-            if (c, g) == (1, 0):
-                y_sb = after_pick.tile([P, 2, CHUNK], F32, name="y_sb1", offset=0, align_bytes=64)
+            if c == 0:
+                y_sb = after_wb.tile([P, 2, CHUNK], F32, name="y_sb0", offset=PLANE_BYTES + 2048, align_bytes=64)
             else:
-                y_sb = ring.tile([P, 2, CHUNK], F32, name="y_sb", align_bytes=64)
+                y_sb = held([P, 2, CHUNK], F32, "y_sb1")
             nc.scalar.copy(y_sb[:], y[c, g][:])
             nc.gpsimd.tensor_tensor(total[:], y_sb[:], res_sb[c // 2][:, blocks, res_cols], ADD)
             nc.sync.dma_start(out_v[:, blocks, cols], total[:])
 
-        gather(0)
-        gather(1)
         cast_wd(0)
-        gather(2)
-        gather(3)
+        for c in range(4):
+            gather(c)
+        cast_wd(1)
+        wa_c = after_wb.tile([P, 2 * R], U8, name="wa_c", offset=0, align_bytes=64)
+        permute(wa_c[:].bitcast(I32), wa_raw[:], 2)
         quant_x(0)
+        wd_c = held([P, N], U32, "wd_c")
+        quant_wd(0)
         quant_x(1)
         product(0)
-        quant_wd(0)
+        quant_x(2)
         quant_h(0)
         second(0, 0)
-        quant_x(2)
-        product(1)
         quant_x(3)
+        product(1)
+        quant_wd(1)
         quant_h(1)
         second(1, 0)
-        finish_beside(0, 0, held([P, 2, CHUNK], F32, "total0", "h1"))
-        cast_wd(1)
-        product(2)
-        quant_wd(1)
         second(0, 1)
         second(1, 1)
+        finish_beside(0, 0, held([P, 2, CHUNK], F32, "total0", "h1"))
+        product(2)
+        finish(0, 1)
         quant_h(2)
         second(2, 0)
         second(2, 1)
-        finish_beside(1, 0, held([P, 2, CHUNK], F32, "total1", "h2"))
+        finish_beside(1, 0, held([P, 2, CHUNK], F32, "total1", "picked"))
         product(3)
-        finish(0, 1)
+        finish(1, 1)
         quant_h(3)
         second(3, 0)
         second(3, 1)
-        finish_beside(1, 1, after_wd.tile([P, 2, CHUNK], F32, name="total2", offset=1024, align_bytes=64))
         finish(2, 0)
         finish(2, 1)
         finish(3, 0)

@@ -62,7 +62,7 @@ def tile_list_htabg_mul_res_kernel(
         planes = [held([P, T], F32, "plane0", "slot0")]
         wd_s = held([P, N], U8, "wd_s")
         picked = held([P, PACK, J], F32, "picked")
-        yb_sb = held([P, J, PACK], F32, "yb_sb")
+        yb_sb = held([P, J // SUB, SUB // 2, PACK, 2], F32, "yb_sb")
 
         nc.gpsimd.memset(wb_s[:], 0)
         nc.vector.memset(tab_s[0:SCALE_ROW0, :], 0)
@@ -157,7 +157,7 @@ def tile_list_htabg_mul_res_kernel(
                         start=(a == 0),
                         stop=(a == 1),
                     )
-            nc.scalar.copy(yb_sb[:, cols, :], bank[:].rearrange("p t n -> p n t"))
+            nc.scalar.copy(yb_sb[:, s], bank[:].rearrange("p t (c e) -> p c t e", e=2))
 
         def pick(i, lo, hi):
             nc.vector.tensor_tensor(
@@ -230,11 +230,10 @@ def tile_list_htabg_mul_res_kernel(
         def product(c):
             h_bf[c] = held([P, CHUNK, PACK], BF16, "h_bf%d" % c, ("h0", "h1", "picked", "h3")[c])
             for u in range(CHUNK // SUB):
-                lo = c * CHUNK + u * SUB
                 nc.vector.tensor_tensor(
-                    h_bf[c][:, u * SUB : (u + 1) * SUB, :],
-                    ya[c, u][:].rearrange("p t n -> p n t"),
-                    yb_sb[:, lo : lo + SUB, :],
+                    h_bf[c][:, u * SUB : (u + 1) * SUB, :].rearrange("p (c e) t -> p c t e", e=2),
+                    ya[c, u][:].rearrange("p t (c e) -> p c t e", e=2),
+                    yb_sb[:, 2 * c + u],
                     MULT,
                 )
 

@@ -33,27 +33,29 @@ def tile_list_htabg_mul_res_kernel(
     nc = tc.nc
     with ExitStack() as ctx:
         keep = ctx.enter_context(tc.tile_pool(name="keep", bufs=1))
-        ring = ctx.enter_context(tc.tile_pool(name="ring", bufs=4))
-        after_words = ctx.enter_context(tc.tile_pool(name="after_words", bufs=1))
+        ring = ctx.enter_context(tc.tile_pool(name="ring", bufs=1))
         after_wb = ctx.enter_context(tc.tile_pool(name="after_wb", bufs=1))
         after_scales = ctx.enter_context(tc.tile_pool(name="after_scales", bufs=1))
-        psum = ctx.enter_context(tc.psum_pool(name="psum", bufs=8))
+        psum = ctx.enter_context(tc.psum_pool(name="psum", bufs=6))
+        psum_late = ctx.enter_context(tc.psum_pool(name="psum_late", bufs=2))
 
         def held(shape, dtype, name, tag=""):
             return keep.tile(shape, dtype, name=name, tag=tag or name, align_bytes=64)
 
+        def placed(pool, offset, shape, dtype, name):
+            return pool.tile(shape, dtype, name=name, offset=offset, align_bytes=64)
+
         tab_list = keep.tile([P, J // LIST], U16, name="tab_list")
         head_lists = keep.tile([P, J // LIST], U16, name="head_lists")
-        tab_s = after_scales.tile([P, T // 4], I32, name="tab_s", offset=PLANE_BYTES - 1024, align_bytes=64)
-        tab_w = after_words.tile([P, T], I32, name="tab_w", offset=2048, align_bytes=64)
-        wb_raw = after_wb.tile([P, 2, R], I32, name="wb_raw", offset=PLANE_BYTES - 2048, align_bytes=64)
+        tab_s = placed(after_scales, PLANE_BYTES - 512, [P, T // 4], I32, "tab_s")
+        tab_w = held([P, T], I32, "tab_w")
+        wb_raw = placed(after_wb, PLANE_BYTES - 512, [P, 2, R], I32, "wb_raw")
         wb_s = held([P, 2, R // 4], I32, "wb_s")
         got_s = held([P, J], U8, "got_s")
         tab_sc = held([P, 2, J // 4], I32, "tab_sc")
-        got_w = held([P, J], U32, "got_w")
-        parted = held([P, 2, 2 * J], U8, "parted")
         wb_c = held([P, 2, R], I32, "wb_c")
         wb_sc = held([P, 2, R], U8, "wb_sc")
+        wa_c = held([P, 2 * R], U8, "wa_c")
         wa_sc = held([P, R], U8, "wa_sc")
         wgt = held([P, J], F32, "wgt")
         w_rows = held([P, P], F32, "w_rows")
@@ -61,8 +63,14 @@ def tile_list_htabg_mul_res_kernel(
         ident = held([P, P], F32, "ident")
         planes = [held([P, T], F32, "plane0", "slot0")]
         wd_s = held([P, N], U8, "wd_s")
-        picked = held([P, PACK, J], F32, "picked")
-        yb_sb = held([P, J // SUB, SUB // 2, PACK, 2], F32, "yb_sb")
+        MAIN = 3 * CHUNK
+        picked = held([P, PACK * MAIN], F32, "picked")
+        picked_main = picked[:].rearrange("p (i j) -> p i j", i=PACK)
+        last = held([P, PACK * CHUNK], F32, "last")
+        picked_last = last[:].rearrange("p (i j) -> p i j", i=PACK)
+
+        def unit_bf16(unit):
+            return picked[:, unit * CHUNK : (unit + 1) * CHUNK].bitcast(BF16).rearrange("p (n i) -> p n i", i=PACK)
 
         nc.gpsimd.memset(wb_s[:], 0)
         nc.vector.memset(tab_s[0:SCALE_ROW0, :], 0)
@@ -74,7 +82,7 @@ def tile_list_htabg_mul_res_kernel(
         wa_scales_i = wa_scales.bitcast(I32)
         wb_scales_i = wb_scales.bitcast(I32)
         x_planes = xT.rearrange("(p i) t -> i p t", i=PACK)
-        wd_v = wd.rearrange("(m t q) n -> q m t n", t=PACK, q=4)
+        wd_v = wd.rearrange("(m t q) n -> t m q n", t=PACK, q=4)
         res_v = res.rearrange("(b m) j -> m b j", m=P)
         out_v = out.rearrange("(b m) j -> m b j", m=P)
 
@@ -107,23 +115,14 @@ def tile_list_htabg_mul_res_kernel(
             row = SCALE_ROW0 + 8 * q
             nc.sync.dma_start(tab_sc[32 * q : 32 * q + 4, :, :], got_s[:].bitcast(I32)[row : row + 8, :])
 
-        planes.append(after_scales.tile([P, T], F32, name="plane1", offset=0, align_bytes=64))
-        wa_s = after_scales.tile([P, R // 4], I32, name="wa_s", offset=PLANE_BYTES, align_bytes=64)
+        planes.append(placed(after_scales, 0, [P, T], F32, "plane1"))
+        wa_s = placed(after_scales, PLANE_BYTES, [P, R // 4], I32, "wa_s")
+        planes.append(placed(after_scales, PLANE_BYTES + 1024, [P, T], F32, "plane2"))
         nc.gpsimd.memset(wa_s[:], 0)
         nc.sync.dma_start(planes[1][:], x_planes[1])
+        nc.sync.dma_start(planes[2][:], x_planes[2])
         for q in range(4):
             nc.sync.dma_start(wa_s[32 * q : 32 * q + 4, :], wa_scales_i[0, 4 * q : 4 * q + 4, :])
-
-        nc.vector.tensor_copy(got_w[:], tab_w[:].bitcast(U32).indirect(tab_list[:]))
-        planes.append(after_words.tile([P, T], F32, name="plane2", offset=0, align_bytes=64))
-        wd_raw = [after_words.tile([P, PACK, N // 2], F32, name="wd_raw0", offset=PLANE_BYTES, align_bytes=64)]
-
-        def load_wd(g):
-            for q in range(4):
-                nc.sync.dma_start(wd_raw[g][q:P:4, :, :], wd_v[q, :, :, g * 256 : (g + 1) * 256])
-
-        nc.sync.dma_start(planes[2][:], x_planes[2])
-        load_wd(0)
 
         def permute(dst, src, run):
             nc.vector.tensor_copy(
@@ -131,127 +130,133 @@ def tile_list_htabg_mul_res_kernel(
                 src.rearrange("p (a m t q) -> p a t m q", t=PACK, m=32, q=run),
             )
 
+        def pick(i, lo, hi):
+            dst = picked[:, i * MAIN + lo : i * MAIN + hi] if hi <= MAIN else last[:, i * CHUNK : (i + 1) * CHUNK]
+            nc.vector.tensor_tensor(
+                dst, planes[i][:].indirect(head_lists[:, lo // LIST : hi // LIST]), wgt[:, lo:hi], MULT
+            )
+
+        yb, yb_sb = {}, {}
+
+
+        def empty_yb(c, u):
+            shape = [P, CHUNK // SUB, SUB // 2, PACK, 2]
+            if c == 3 and u == 0:
+                yb_sb[c] = placed(after_wb, 15360, shape, F32, "yb_sb3")
+            elif u == 0:
+                yb_sb[c] = held(shape, F32, "yb_sb%d" % c)
+            nc.scalar.copy(yb_sb[c][:, u], yb[c, u][:].rearrange("p t (c e) -> p c t e", e=2))
+
+        def table_product(half):
+            for s in range(HALF // SUB):
+                c, u = divmod(half * (HALF // SUB) + s, CHUNK // SUB)
+                cols = slice(half * HALF + s * SUB, half * HALF + (s + 1) * SUB)
+                bank = (psum if c < 3 else psum_late).tile([P, PACK, SUB], F32, name="yb", tag="bank")
+                for t in range(PACK):
+                    ch = slice(t * P, (t + 1) * P)
+                    for a in range(2):
+                        nc.tensor.matmul_mx(
+                            out=bank[:, t, :],
+                            lhsT=wb_c[:, a, ch].bitcast(FP8X4),
+                            lhsT_scale=wb_sc[:, a, ch],
+                            rhs=parted[:, a, 2 * cols.start : 2 * cols.stop].bitcast(FP4X4),
+                            rhs_scale=tab_sc[:, a, :].bitcast(U8)[:, cols],
+                            start=(a == 0),
+                            stop=(a == 1),
+                        )
+                yb[c, u] = bank
+                if c < 3:
+                    empty_yb(c, u)
+
+        got_w = held([P, J], U32, "got_w")
+        parted = held([P, 2, 2 * J], U8, "parted")
+        nc.vector.tensor_copy(got_w[:], tab_w[:].bitcast(U32).indirect(tab_list[:]))
         permute(wb_c[:].rearrange("p a r -> p (a r)"), wb_raw[:].rearrange("p a r -> p (a r)"), 4)
         nc.vector.tensor_copy(parted[:].bitcast(U16), got_w[:].bitcast(U16).rearrange("p (j d) -> p d j", d=2))
         permute(wb_sc[:].rearrange("p a r -> p (a r)").bitcast(I32), wb_s[:].rearrange("p a r -> p (a r)"), 1)
+        table_product(0)
+        table_product(1)
 
-        planes.append(after_wb.tile([P, T], F32, name="plane3", offset=0, align_bytes=64))
-        wa_raw = after_wb.tile([P, R // 2], I32, name="wa_raw", offset=PLANE_BYTES, align_bytes=64)
-        wd_raw.append(after_wb.tile([P, PACK, N // 2], F32, name="wd_raw1", offset=PLANE_BYTES + 1024, align_bytes=64))
+        planes.append(placed(after_wb, 0, [P, T], F32, "plane3"))
+        wa_raw = placed(after_wb, PLANE_BYTES + 2048, [P, R // 2], I32, "wa_raw")
+        wd_raw = placed(after_wb, PLANE_BYTES + 3072, [P, PACK, N], F32, "wd_raw")
         nc.sync.dma_start(planes[3][:], x_planes[3])
         nc.sync.dma_start(wa_raw[:], wa_words[0].bitcast(I32))
-        load_wd(1)
+        for t in range(PACK):
+            nc.sync.dma_start(wd_raw[:, t, :], wd_v[t])
 
-        for s in range(J // SUB):
-            cols = slice(s * SUB, (s + 1) * SUB)
-            bank = psum.tile([P, PACK, SUB], F32, name="yb", tag="bank")
-            for t in range(PACK):
-                ch = slice(t * P, (t + 1) * P)
-                for a in range(2):
-                    nc.tensor.matmul_mx(
-                        out=bank[:, t, :],
-                        lhsT=wb_c[:, a, ch].bitcast(FP8X4),
-                        lhsT_scale=wb_sc[:, a, ch],
-                        rhs=parted[:, a, 2 * s * SUB : 2 * (s + 1) * SUB].bitcast(FP4X4),
-                        rhs_scale=tab_sc[:, a, :].bitcast(U8)[:, cols],
-                        start=(a == 0),
-                        stop=(a == 1),
-                    )
-            nc.scalar.copy(yb_sb[:, s], bank[:].rearrange("p t (c e) -> p c t e", e=2))
-
-        def pick(i, lo, hi):
-            nc.vector.tensor_tensor(
-                picked[:, i, lo:hi],
-                planes[i][:].indirect(head_lists[:, lo // LIST : hi // LIST]),
-                wgt[:, lo:hi],
-                MULT,
-            )
-
-        res_sb = []
-        for i in range(PACK - 1):
-            pick(i, 0, J)
-            if i == 0:
-                res_sb.append(held([P, N // P, HALF], F32, "res0", "slot0"))
-            if i == 1:
-                res_sb.append(after_scales.tile([P, N // P, HALF], F32, name="res1", offset=0, align_bytes=64))
-            if i < 2:
-                nc.sync.dma_start(res_sb[i][:], res_v[:, :, i * HALF : (i + 1) * HALF])
-        permute(wa_sc[:].bitcast(I32), wa_s[:], 1)
+        pick(0, 0, MAIN)
+        pick(0, MAIN, J)
+        res_sb = [held([P, N // P, HALF], F32, "res0", "slot0")]
+        nc.sync.dma_start(res_sb[0][:], res_v[:, :, 0:HALF])
+        pick(1, 0, MAIN)
+        pick(1, MAIN, J)
+        res_sb.append(placed(after_scales, 0, [P, N // P, HALF], F32, "res1"))
+        nc.sync.dma_start(res_sb[1][:], res_v[:, :, HALF:J])
+        pick(2, 0, MAIN)
 
         def interleave(dst, src):
             nc.scalar.copy(
                 dst.rearrange("p (c e) i -> p c i e", e=4), src.rearrange("p i (c e) -> p c i e", e=4)
             )
 
-        wd_bf = {}
+        def quantise(codes, scales, src):
+            nc.vector.quantize_mx(out=codes.bitcast(FP8X4), scales=scales, in_=src.rearrange("p n i -> p (n i)"))
 
-        def cast_wd(g):
-            wd_bf[g] = held([P, N // 2, PACK], BF16, "wd_bf%d" % g, ("wd_bf0", "picked")[g])
-            interleave(wd_bf[g][:], wd_raw[g][:])
+        x_c, x_s, h_c, h_s, ya, y, wd_c, y_sb = {}, {}, {}, {}, {}, {}, {}, {}
 
-        def quant_wd(g):
-            ch = slice(g * 256, (g + 1) * 256)
-            nc.vector.quantize_mx(
-                out=wd_c[:, ch].bitcast(FP8X4),
-                scales=wd_s[:, ch],
-                in_=wd_bf[g][:].rearrange("p n i -> p (n i)"),
-            )
-
-        x_bf, x_c, x_s, h_bf, h_c, h_s, ya, y = {}, {}, {}, {}, {}, {}, {}, {}
-
-        def gather(c):
-            lo = c * CHUNK
-            if c < 3:
-                pick(PACK - 1, lo, J if c == 2 else lo + CHUNK)
-            x_bf[c] = held([P, CHUNK, PACK], BF16, "x_bf%d" % c, ("wd_c", "h0", "x2", "x3")[c])
-            interleave(x_bf[c][:], picked[:, :, lo : lo + CHUNK])
-
-        def quant_x(c):
+        def new_x(c):
             x_c[c] = ring.tile([P, CHUNK], U32, name="x_c", align_bytes=64)
             x_s[c] = ring.tile([P, CHUNK], U8, name="x_s", align_bytes=64)
-            nc.vector.quantize_mx(
-                out=x_c[c][:].bitcast(FP8X4), scales=x_s[c][:], in_=x_bf[c][:].rearrange("p n i -> p (n i)")
-            )
-            for u in range(CHUNK // SUB):
-                cols = slice(u * SUB, (u + 1) * SUB)
-                ya[c, u] = psum.tile([P, PACK, SUB], F32, name="ya", tag="bank")
-                for t in range(PACK):
-                    ch = slice(t * P, (t + 1) * P)
-                    nc.tensor.matmul_mx(
-                        out=ya[c, u][:, t, :],
-                        lhsT=wa_c[:, 2 * t * P : 2 * (t + 1) * P].bitcast(FP4X4),
-                        lhsT_scale=wa_sc[:, ch],
-                        rhs=x_c[c][:, cols].bitcast(FP8X4),
-                        rhs_scale=x_s[c][:, cols],
-                        start=True,
-                        stop=True,
-                    )
 
-        def product(c):
-            h_bf[c] = held([P, CHUNK, PACK], BF16, "h_bf%d" % c, ("h0", "h1", "picked", "h3")[c])
-            for u in range(CHUNK // SUB):
-                nc.vector.tensor_tensor(
-                    h_bf[c][:, u * SUB : (u + 1) * SUB, :].rearrange("p (c e) t -> p c t e", e=2),
-                    ya[c, u][:].rearrange("p t (c e) -> p c t e", e=2),
-                    yb_sb[:, 2 * c + u],
-                    MULT,
+        def first(c, u):
+            cols = slice(u * SUB, (u + 1) * SUB)
+            ya[c, u] = psum.tile([P, PACK, SUB], F32, name="ya", tag="bank")
+            for t in range(PACK):
+                ch = slice(t * P, (t + 1) * P)
+                nc.tensor.matmul_mx(
+                    out=ya[c, u][:, t, :],
+                    lhsT=wa_c[:, 2 * t * P : 2 * (t + 1) * P].bitcast(FP4X4),
+                    lhsT_scale=wa_sc[:, ch],
+                    rhs=x_c[c][:, cols].bitcast(FP8X4),
+                    rhs_scale=x_s[c][:, cols],
+                    start=True,
+                    stop=True,
                 )
 
-        def quant_h(c):
-            h_c[c] = ring.tile([P, CHUNK], U32, name="h_c", align_bytes=64)
-            h_s[c] = ring.tile([P, CHUNK], U8, name="h_s", align_bytes=64)
-            nc.vector.quantize_mx(
-                out=h_c[c][:].bitcast(FP8X4), scales=h_s[c][:], in_=h_bf[c][:].rearrange("p n i -> p (n i)")
+        def quant_x(c, src):
+            new_x(c)
+            quantise(x_c[c][:], x_s[c][:], src)
+            first(c, 0)
+            first(c, 1)
+
+        def product(c, u, dst):
+            nc.vector.tensor_tensor(
+                dst.rearrange("p (c e) t -> p c t e", e=2),
+                ya[c, u][:].rearrange("p t (c e) -> p c t e", e=2),
+                yb_sb[c][:, u],
+                MULT,
             )
+
+        def products(c, h_bf):
+            for u in range(CHUNK // SUB):
+                product(c, u, h_bf[:, u * SUB : (u + 1) * SUB, :])
+
+        def new_h(c):
+            h_c[c] = held([P, CHUNK], U32, "h_c%d" % c)
+            h_s[c] = held([P, CHUNK], U8, "h_s%d" % c)
+
+        def quant_h(c, src):
+            new_h(c)
+            quantise(h_c[c][:], h_s[c][:], src)
 
         def second(c, g):
             y[c, g] = psum.tile([P, 2, CHUNK], F32, name="y", tag="bank")
             for b in range(2):
-                ch = slice((2 * g + b) * P, (2 * g + b + 1) * P)
                 nc.tensor.matmul_mx(
                     out=y[c, g][:, b, :],
-                    lhsT=wd_c[:, ch].bitcast(FP8X4),
-                    lhsT_scale=wd_s[:, ch],
+                    lhsT=wd_c[g][:, b * P : (b + 1) * P].bitcast(FP8X4),
+                    lhsT_scale=wd_s[:, (2 * g + b) * P : (2 * g + b + 1) * P],
                     rhs=h_c[c][:].bitcast(FP8X4),
                     rhs_scale=h_s[c][:],
                     start=True,
@@ -262,57 +267,97 @@ def tile_list_htabg_mul_res_kernel(
             cols = slice(c * CHUNK, (c + 1) * CHUNK)
             res_cols = slice((c % 2) * CHUNK, (c % 2 + 1) * CHUNK)
             blocks = slice(2 * g + lo, 2 * g + hi)
-            total = ring.tile([P, hi - lo, CHUNK], F32, name="total", bufs=9)
+            total = ring.tile([P, hi - lo, CHUNK], F32, name="total", bufs=6)
             nc.vector.tensor_tensor(total[:], y[c, g][:, lo:hi, :], res_sb[c // 2][:, blocks, res_cols], ADD)
             queue.dma_start(out_v[:, blocks, cols], total[:])
+
+        def empty(c, g):
+            if (c, g) == (0, 0):
+                y_sb[c, g] = placed(after_wb, 15360, [P, 2, CHUNK], F32, "y_sb00")
+            else:
+                y_sb[c, g] = held([P, 2, CHUNK], F32, "y_sb%d%d" % (c, g))
+            nc.scalar.copy(y_sb[c, g][:], y[c, g][:])
 
         def finish_beside(c, g, total):
             cols = slice(c * CHUNK, (c + 1) * CHUNK)
             res_cols = slice((c % 2) * CHUNK, (c % 2 + 1) * CHUNK)
             blocks = slice(2 * g, 2 * g + 2)
-            if c == 0:
-                y_sb = after_wb.tile([P, 2, CHUNK], F32, name="y_sb0", offset=PLANE_BYTES + 2048, align_bytes=64)
-            else:
-                y_sb = held([P, 2, CHUNK], F32, "y_sb1")
-            nc.scalar.copy(y_sb[:], y[c, g][:])
-            nc.gpsimd.tensor_tensor(total[:], y_sb[:], res_sb[c // 2][:, blocks, res_cols], ADD)
+            nc.gpsimd.tensor_tensor(total[:], y_sb[c, g][:], res_sb[c // 2][:, blocks, res_cols], ADD)
             nc.sync.dma_start(out_v[:, blocks, cols], total[:])
 
-        cast_wd(0)
-        for c in range(4):
-            gather(c)
-        cast_wd(1)
-        wa_c = after_wb.tile([P, 2 * R], U8, name="wa_c", offset=0, align_bytes=64)
+        wide, pair = [P, CHUNK, PACK], [P, 2, CHUNK]
+        pick(3, 0, CHUNK)
+        x_bf0 = [unit_bf16(11), held([P, SUB, PACK], BF16, "x_bf0b")[:]]
+        for u in range(2):
+            interleave(x_bf0[u], picked_main[:, :, u * SUB : (u + 1) * SUB])
         permute(wa_c[:].bitcast(I32), wa_raw[:], 2)
-        quant_x(0)
-        wd_c = held([P, N], U32, "wd_c")
-        quant_wd(0)
-        quant_x(1)
-        product(0)
-        quant_x(2)
-        quant_h(0)
+        permute(wa_sc[:].bitcast(I32), wa_s[:], 1)
+        pick(3, CHUNK, 2 * CHUNK)
+        x_bf1 = held(wide, BF16, "x_bf1")
+        interleave(x_bf1[:], picked_main[:, :, CHUNK : 2 * CHUNK])
+        wd_bf0 = last[:, 2 * CHUNK : 4 * CHUNK].bitcast(BF16).rearrange("p (n i) -> p n i", i=PACK)
+        interleave(wd_bf0, wd_raw[:, :, 0:256])
+        wd_bf1 = placed(after_wb, 8192, wide, BF16, "wd_bf1")
+        interleave(wd_bf1[:], wd_raw[:, :, 256:512])
+
+        new_x(0)
+        for u in range(2):
+            cols = slice(u * SUB, (u + 1) * SUB)
+            quantise(x_c[0][:, cols], x_s[0][:, cols], x_bf0[u])
+            first(0, u)
+        pick(3, 2 * CHUNK, MAIN)
+
+        x_bf2 = placed(after_wb, 12288, wide, BF16, "x_bf2")
+        interleave(x_bf2[:], picked_main[:, :, 2 * CHUNK : MAIN])
+        h_bf0 = held(wide, BF16, "h_bf0")
+        products(0, h_bf0)
+        quant_x(1, x_bf1[:])
+        wd_c[0] = held([P, N // 2], U32, "wd_c0", "yb_sb0")
+        quantise(wd_c[0][:], wd_s[:, 0:256], wd_bf0)
+        quant_h(0, h_bf0[:])
         second(0, 0)
-        quant_x(3)
-        product(1)
-        quant_wd(1)
-        quant_h(1)
-        second(1, 0)
+        empty(0, 0)
+        pick(2, MAIN, J)
+        pick(3, MAIN, J)
+        wd_c[1] = placed(after_scales, PLANE_BYTES + 1024, [P, N // 2], U32, "wd_c1")
+        quantise(wd_c[1][:], wd_s[:, 256:512], wd_bf1[:])
         second(0, 1)
+        x_bf3 = placed(after_wb, 9216, wide, BF16, "x_bf3")
+        interleave(x_bf3[:], picked_last)
+        empty(0, 1)
+        quant_x(2, x_bf2[:])
+
+        finish_beside(0, 0, placed(after_wb, 13312, pair, F32, "total00"))
+        for u in range(2):
+            empty_yb(3, u)
+        h_bf1 = placed(after_wb, 11264, wide, BF16, "h_bf1")
+        products(1, h_bf1)
+        new_x(3)
+        quantise(x_c[3][:], x_s[3][:], x_bf3[:])
+        quant_h(1, h_bf1[:])
         second(1, 1)
-        finish_beside(0, 0, held([P, 2, CHUNK], F32, "total0", "h1"))
-        product(2)
-        finish(0, 1)
-        quant_h(2)
-        second(2, 0)
-        second(2, 1)
-        finish_beside(1, 0, held([P, 2, CHUNK], F32, "total1", "picked"))
-        product(3)
+        second(1, 0)
+        first(3, 0)
+        first(3, 1)
+        empty(1, 0)
+
+        finish_beside(0, 1, placed(after_wb, 10240, pair, F32, "total01"))
+        h_bf2 = placed(after_wb, 8192, wide, BF16, "h_bf2")
+        products(2, h_bf2)
         finish(1, 1)
-        quant_h(3)
+        quant_h(2, h_bf2[:])
+        second(2, 1)
+        second(2, 0)
+
+        finish_beside(1, 0, placed(after_wb, 8192, pair, F32, "total10"))
+        h_bf3 = held(wide, BF16, "h_bf3", "h3")
+        products(3, h_bf3)
+        finish(2, 1)
+        quant_h(3, h_bf3[:])
         second(3, 0)
         second(3, 1)
+
         finish(2, 0)
-        finish(2, 1)
         finish(3, 0)
         finish(3, 1, 0, 1)
         finish(3, 1, 1, 2, nc.scalar)

@@ -36,6 +36,7 @@ def tile_list_htabg_mul_res_kernel(
         ring = ctx.enter_context(tc.tile_pool(name="ring", bufs=1))
         after_wb = ctx.enter_context(tc.tile_pool(name="after_wb", bufs=1))
         after_scales = ctx.enter_context(tc.tile_pool(name="after_scales", bufs=1))
+        late = ctx.enter_context(tc.tile_pool(name="late", bufs=1))
         psum = ctx.enter_context(tc.psum_pool(name="psum", bufs=6))
         psum_late = ctx.enter_context(tc.psum_pool(name="psum_late", bufs=2))
 
@@ -50,7 +51,7 @@ def tile_list_htabg_mul_res_kernel(
         tab_s = placed(after_scales, PLANE_BYTES - 512, [P, T // 4], I32, "tab_s")
         tab_w = held([P, T], I32, "tab_w")
         wb_raw = placed(after_wb, PLANE_BYTES - 512, [P, 2, R], I32, "wb_raw")
-        wb_s = held([P, 2, R // 4], I32, "wb_s")
+        wb_s = held([P, 2, R // 4], I32, "wb_s", "rows")
         got_s = held([P, J], U8, "got_s")
         tab_sc = held([P, 2, J // 4], I32, "tab_sc")
         wb_c = held([P, 2, R], I32, "wb_c")
@@ -61,16 +62,11 @@ def tile_list_htabg_mul_res_kernel(
         w_rows = held([P, P], F32, "w_rows")
         w_cols = held([P, J // P, P], F32, "w_cols")
         ident = held([P, P], F32, "ident")
-        planes = [held([P, T], F32, "plane0", "slot0")]
+        planes = [held([P, T], F32, "plane0")]
         wd_s = held([P, N], U8, "wd_s")
         MAIN = 3 * CHUNK
         picked = held([P, PACK * MAIN], F32, "picked")
         picked_main = picked[:].rearrange("p (i j) -> p i j", i=PACK)
-        last = held([P, PACK * CHUNK], F32, "last")
-        picked_last = last[:].rearrange("p (i j) -> p i j", i=PACK)
-
-        def unit_bf16(unit):
-            return picked[:, unit * CHUNK : (unit + 1) * CHUNK].bitcast(BF16).rearrange("p (n i) -> p n i", i=PACK)
 
         nc.gpsimd.memset(wb_s[:], 0)
         nc.vector.memset(tab_s[0:SCALE_ROW0, :], 0)
@@ -185,15 +181,11 @@ def tile_list_htabg_mul_res_kernel(
         for t in range(PACK):
             nc.sync.dma_start(wd_raw[:, t, :], wd_v[t])
 
-        pick(0, 0, MAIN)
-        pick(0, MAIN, J)
-        res_sb = [held([P, N // P, HALF], F32, "res0", "slot0")]
-        nc.sync.dma_start(res_sb[0][:], res_v[:, :, 0:HALF])
-        pick(1, 0, MAIN)
-        pick(1, MAIN, J)
-        res_sb.append(placed(after_scales, 0, [P, N // P, HALF], F32, "res1"))
-        nc.sync.dma_start(res_sb[1][:], res_v[:, :, HALF:J])
-        pick(2, 0, MAIN)
+        res_sb = [held([P, N // P, HALF], F32, "res0", "rows"), held([P, N // P, HALF], F32, "res1", "parted")]
+        for half in range(2):
+            nc.sync.dma_start(res_sb[half][:], res_v[:, :, half * HALF : (half + 1) * HALF])
+        for i in range(PACK - 1):
+            pick(i, 0, MAIN)
 
         def interleave(dst, src):
             nc.scalar.copy(
@@ -287,25 +279,27 @@ def tile_list_htabg_mul_res_kernel(
 
         wide, pair = [P, CHUNK, PACK], [P, 2, CHUNK]
         pick(3, 0, CHUNK)
-        x_bf0 = [unit_bf16(11), held([P, SUB, PACK], BF16, "x_bf0b")[:]]
+        x_bf0 = [placed(late, 0, [P, SUB, PACK], BF16, "x_bf0a")[:], held([P, SUB, PACK], BF16, "x_bf0b")[:]]
         for u in range(2):
             interleave(x_bf0[u], picked_main[:, :, u * SUB : (u + 1) * SUB])
         permute(wa_c[:].bitcast(I32), wa_raw[:], 2)
         permute(wa_sc[:].bitcast(I32), wa_s[:], 1)
-        pick(3, CHUNK, 2 * CHUNK)
+        pick(3, CHUNK, MAIN)
         x_bf1 = held(wide, BF16, "x_bf1")
         interleave(x_bf1[:], picked_main[:, :, CHUNK : 2 * CHUNK])
-        wd_bf0 = last[:, 2 * CHUNK : 4 * CHUNK].bitcast(BF16).rearrange("p (n i) -> p n i", i=PACK)
-        interleave(wd_bf0, wd_raw[:, :, 0:256])
-        wd_bf1 = placed(after_wb, 8192, wide, BF16, "wd_bf1")
-        interleave(wd_bf1[:], wd_raw[:, :, 256:512])
 
         new_x(0)
         for u in range(2):
             cols = slice(u * SUB, (u + 1) * SUB)
             quantise(x_c[0][:, cols], x_s[0][:, cols], x_bf0[u])
             first(0, u)
-        pick(3, 2 * CHUNK, MAIN)
+        last = placed(late, 0, [P, PACK * CHUNK], F32, "last")
+        picked_last = last[:].rearrange("p (i j) -> p i j", i=PACK)
+        pick(0, MAIN, J)
+        wd_bf0 = last[:, 2 * CHUNK : 4 * CHUNK].bitcast(BF16).rearrange("p (n i) -> p n i", i=PACK)
+        interleave(wd_bf0, wd_raw[:, :, 0:256])
+        wd_bf1 = placed(after_wb, 8192, wide, BF16, "wd_bf1")
+        interleave(wd_bf1[:], wd_raw[:, :, 256:512])
 
         x_bf2 = placed(after_wb, 12288, wide, BF16, "x_bf2")
         interleave(x_bf2[:], picked_main[:, :, 2 * CHUNK : MAIN])
@@ -317,8 +311,8 @@ def tile_list_htabg_mul_res_kernel(
         quant_h(0, h_bf0[:])
         second(0, 0)
         empty(0, 0)
-        pick(2, MAIN, J)
-        pick(3, MAIN, J)
+        for i in range(1, PACK):
+            pick(i, MAIN, J)
         wd_c[1] = placed(after_scales, PLANE_BYTES + 1024, [P, N // 2], U32, "wd_c1")
         quantise(wd_c[1][:], wd_s[:, 256:512], wd_bf1[:])
         second(0, 1)

@@ -84,15 +84,13 @@ def tile_list_htabg_mul_res_kernel(
 
         nc.sync.dma_start(tab_list[:], offs)
         nc.sync.dma_start(tab_s[SCALE_ROW0:P, :], tab_scales_i.rearrange("a q n -> q a n"))
-        nc.sync.dma_start(w_rows[0:64, :], wgt2.rearrange("(g r) (c m) -> g r c m", r=LIST, m=P)[:, 0])
         nc.sync.dma_start(tab_w[:], tab_words[0].rearrange("p t b -> p (t b)").bitcast(I32))
+        nc.sync.dma_start(w_rows[0:64, :], wgt2.rearrange("(g r) (c m) -> g r c m", r=LIST, m=P)[:, 0])
         nc.sync.dma_start(wb_raw[:], wb_words.rearrange("a p r i -> p a (r i)").bitcast(I32))
-        for q in range(4):
-            nc.sync.dma_start(
-                wb_s[32 * q : 32 * q + 4, :, :], wb_scales_i[:, 4 * q : 4 * q + 4, :].rearrange("a r n -> r a n")
-            )
-        nc.sync.dma_start(head_lists[:], offs2)
+        for r in range(4):
+            nc.sync.dma_start(wb_s[r:P:32, :, :], wb_scales_i.rearrange("a (q r) n -> r q a n", r=4)[r])
         nc.sync.dma_start(planes[0][:], x_planes[0])
+        nc.sync.dma_start(head_lists[:], offs2)
 
         turned = psum.tile([P, P], F32, name="turned", tag="bank")
         nc.tensor.transpose(turned[:], w_rows[:], ident[:])
@@ -107,7 +105,7 @@ def tile_list_htabg_mul_res_kernel(
             nc.scalar.copy(wgt[:, half * HALF : (half + 1) * HALF], spread[:].rearrange("p c m -> p (c m)"))
 
         nc.vector.tensor_copy(got_s[:], tab_s[:].bitcast(U8).indirect(tab_list[:]))
-        for q in range(4):
+        for q in (0, 2, 1, 3):
             row = SCALE_ROW0 + 8 * q
             nc.sync.dma_start(tab_sc[32 * q : 32 * q + 4, :, :], got_s[:].bitcast(I32)[row : row + 8, :])
 
@@ -117,8 +115,8 @@ def tile_list_htabg_mul_res_kernel(
         nc.gpsimd.memset(wa_s[:], 0)
         nc.sync.dma_start(planes[1][:], x_planes[1])
         nc.sync.dma_start(planes[2][:], x_planes[2])
-        for q in range(4):
-            nc.sync.dma_start(wa_s[32 * q : 32 * q + 4, :], wa_scales_i[0, 4 * q : 4 * q + 4, :])
+        for r in range(4):
+            nc.sync.dma_start(wa_s[r:P:32, :], wa_scales_i[0].rearrange("(q r) n -> r q n", r=4)[r])
 
         def permute(dst, src, run):
             nc.vector.tensor_copy(

@@ -62,7 +62,7 @@ def tile_list_htabg_mul_res_kernel(
         w_rows = held([P, P], F32, "w_rows")
         w_cols = held([P, J // P, P], F32, "w_cols")
         ident = held([P, P], F32, "ident")
-        planes = [held([P, T], F32, "plane0")]
+        planes = [held([P, T], F32, "plane0", "slot0")]
         wd_s = held([P, N], U8, "wd_s")
         MAIN = 3 * CHUNK
         picked = held([P, PACK * MAIN], F32, "picked")
@@ -296,8 +296,10 @@ def tile_list_htabg_mul_res_kernel(
         pick(0, MAIN, J)
         wd_bf0 = last[:, 2 * CHUNK : 4 * CHUNK].bitcast(BF16).rearrange("p (n i) -> p n i", i=PACK)
         interleave(wd_bf0, wd_raw[:, :, 0:256])
-        wd_bf1 = placed(after_wb, 8192, wide, BF16, "wd_bf1")
-        interleave(wd_bf1[:], wd_raw[:, :, 256:512])
+        wd_bf1 = held(wide, BF16, "wd_bf1", "slot0")
+        nc.gpsimd.tensor_scalar(
+            wd_bf1[:], wd_raw[:, :, 256:512].rearrange("p i n -> p n i"), 1.0, 0.0, op0=MULT, op1=ADD
+        )
 
         x_bf2 = placed(after_wb, 12288, wide, BF16, "x_bf2")
         interleave(x_bf2[:], picked_main[:, :, 2 * CHUNK : MAIN])
@@ -314,7 +316,7 @@ def tile_list_htabg_mul_res_kernel(
         wd_c[1] = placed(after_scales, PLANE_BYTES + 1024, [P, N // 2], U32, "wd_c1")
         quantise(wd_c[1][:], wd_s[:, 256:512], wd_bf1[:])
         second(0, 1)
-        x_bf3 = placed(after_wb, 9216, wide, BF16, "x_bf3")
+        x_bf3 = held(wide, BF16, "x_bf3", "slot0")
         interleave(x_bf3[:], picked_last)
         empty(0, 1)
         quant_x(2, x_bf2[:])
@@ -333,15 +335,15 @@ def tile_list_htabg_mul_res_kernel(
         first(3, 1)
         empty(1, 0)
 
-        finish_beside(0, 1, placed(after_wb, 10240, pair, F32, "total01"))
-        h_bf2 = placed(after_wb, 8192, wide, BF16, "h_bf2")
+        finish_beside(0, 1, placed(after_wb, 11264, pair, F32, "total01"))
+        h_bf2 = held(wide, BF16, "h_bf2", "slot0")
         products(2, h_bf2)
         finish(1, 1)
         quant_h(2, h_bf2[:])
         second(2, 1)
         second(2, 0)
 
-        finish_beside(1, 0, placed(after_wb, 8192, pair, F32, "total10"))
+        finish_beside(1, 0, held(pair, F32, "total10", "slot0"))
         h_bf3 = held(wide, BF16, "h_bf3", "h3")
         products(3, h_bf3)
         finish(2, 1)

@@ -36,9 +36,7 @@ def tile_list_htabg_mul_res_kernel(
         ring = ctx.enter_context(tc.tile_pool(name="ring", bufs=1))
         after_wb = ctx.enter_context(tc.tile_pool(name="after_wb", bufs=1))
         after_scales = ctx.enter_context(tc.tile_pool(name="after_scales", bufs=1))
-        late = ctx.enter_context(tc.tile_pool(name="late", bufs=1))
-        psum = ctx.enter_context(tc.psum_pool(name="psum", bufs=6))
-        psum_late = ctx.enter_context(tc.psum_pool(name="psum_late", bufs=2))
+        psum = ctx.enter_context(tc.psum_pool(name="psum", bufs=8))
 
         def held(shape, dtype, name, tag=""):
             return keep.tile(shape, dtype, name=name, tag=tag or name, align_bytes=64)
@@ -54,7 +52,6 @@ def tile_list_htabg_mul_res_kernel(
         wb_s = held([P, 2, R // 4], I32, "wb_s", "rows")
         got_s = held([P, J], U8, "got_s")
         tab_sc = held([P, 2, J // 4], I32, "tab_sc")
-        wb_c = held([P, 2, R], I32, "wb_c")
         wb_sc = held([P, 2, R], U8, "wb_sc")
         wa_c = held([P, 2 * R], U8, "wa_c")
         wa_sc = held([P, R], U8, "wa_sc")
@@ -64,9 +61,7 @@ def tile_list_htabg_mul_res_kernel(
         ident = held([P, P], F32, "ident")
         planes = [held([P, T], F32, "plane0", "slot0")]
         wd_s = held([P, N], U8, "wd_s")
-        MAIN = 3 * CHUNK
-        picked = held([P, PACK * MAIN], F32, "picked")
-        picked_main = picked[:].rearrange("p (i j) -> p i j", i=PACK)
+        picked = [held([P, PACK * HALF], F32, "picked0", "low"), held([P, PACK * HALF], F32, "picked1", "high")]
 
         nc.gpsimd.memset(wb_s[:], 0)
         nc.vector.memset(tab_s[0:SCALE_ROW0, :], 0)
@@ -78,14 +73,14 @@ def tile_list_htabg_mul_res_kernel(
         wa_scales_i = wa_scales.bitcast(I32)
         wb_scales_i = wb_scales.bitcast(I32)
         x_planes = xT.rearrange("(p i) t -> i p t", i=PACK)
-        wd_v = wd.rearrange("(m t q) n -> t m q n", t=PACK, q=4)
+        wd_v = wd.rearrange("(g t s) n -> t g s n", t=PACK, s=8)
         res_v = res.rearrange("(b m) j -> m b j", m=P)
         out_v = out.rearrange("(b m) j -> m b j", m=P)
 
         nc.sync.dma_start(tab_list[:], offs)
         nc.sync.dma_start(tab_s[SCALE_ROW0:P, :], tab_scales_i.rearrange("a q n -> q a n"))
-        nc.sync.dma_start(tab_w[:], tab_words[0].rearrange("p t b -> p (t b)").bitcast(I32))
         nc.sync.dma_start(w_rows[0:64, :], wgt2.rearrange("(g r) (c m) -> g r c m", r=LIST, m=P)[:, 0])
+        nc.sync.dma_start(tab_w[:], tab_words[0].rearrange("p t b -> p (t b)").bitcast(I32))
         nc.sync.dma_start(wb_raw[:], wb_words.rearrange("a p r i -> p a (r i)").bitcast(I32))
         for r in range(4):
             nc.sync.dma_start(wb_s[r:P:32, :, :], wb_scales_i.rearrange("a (q r) n -> r q a n", r=4)[r])
@@ -119,16 +114,24 @@ def tile_list_htabg_mul_res_kernel(
             nc.sync.dma_start(wa_s[r:P:32, :], wa_scales_i[0].rearrange("(q r) n -> r q n", r=4)[r])
 
         def permute(dst, src, run):
-            nc.vector.tensor_copy(
-                dst.rearrange("p (a t m q) -> p a t m q", t=PACK, m=32, q=run),
-                src.rearrange("p (a m t q) -> p a t m q", t=PACK, m=32, q=run),
+            nc.scalar.copy(
+                dst.bitcast(U32).rearrange("p (a t g s) -> p a t g s", t=PACK, g=16, s=run),
+                src.bitcast(U32).rearrange("p (a g t s) -> p a t g s", t=PACK, g=16, s=run),
             )
 
         def pick(i, lo, hi):
-            dst = picked[:, i * MAIN + lo : i * MAIN + hi] if hi <= MAIN else last[:, i * CHUNK : (i + 1) * CHUNK]
+            half = lo // HALF
+            at = i * HALF - half * HALF
             nc.vector.tensor_tensor(
-                dst, planes[i][:].indirect(head_lists[:, lo // LIST : hi // LIST]), wgt[:, lo:hi], MULT
+                picked[half][:, at + lo : at + hi],
+                planes[i][:].indirect(head_lists[:, lo // LIST : hi // LIST]),
+                wgt[:, lo:hi],
+                MULT,
             )
+
+        def picked_chunk(c):
+            rows = picked[c // 2][:].rearrange("p (i j) -> p i j", i=PACK)
+            return rows[:, :, (c % 2) * CHUNK : (c % 2 + 1) * CHUNK]
 
         yb, yb_sb = {}, {}
 
@@ -136,16 +139,16 @@ def tile_list_htabg_mul_res_kernel(
         def empty_yb(c, u):
             shape = [P, CHUNK // SUB, SUB // 2, PACK, 2]
             if c == 3 and u == 0:
-                yb_sb[c] = placed(after_wb, 15360, shape, F32, "yb_sb3")
+                yb_sb[c] = held(shape, F32, "yb_sb3", "high")
             elif u == 0:
                 yb_sb[c] = held(shape, F32, "yb_sb%d" % c)
             nc.scalar.copy(yb_sb[c][:, u], yb[c, u][:].rearrange("p t (c e) -> p c t e", e=2))
 
-        def table_product(half):
-            for s in range(HALF // SUB):
-                c, u = divmod(half * (HALF // SUB) + s, CHUNK // SUB)
-                cols = slice(half * HALF + s * SUB, half * HALF + (s + 1) * SUB)
-                bank = (psum if c < 3 else psum_late).tile([P, PACK, SUB], F32, name="yb", tag="bank")
+        def table_product(c):
+            for u in range(CHUNK // SUB):
+                lo = (c % 2) * CHUNK + u * SUB
+                cols = slice(c * CHUNK + u * SUB, c * CHUNK + (u + 1) * SUB)
+                bank = psum.tile([P, PACK, SUB], F32, name="yb", tag="bank")
                 for t in range(PACK):
                     ch = slice(t * P, (t + 1) * P)
                     for a in range(2):
@@ -153,7 +156,7 @@ def tile_list_htabg_mul_res_kernel(
                             out=bank[:, t, :],
                             lhsT=wb_c[:, a, ch].bitcast(FP8X4),
                             lhsT_scale=wb_sc[:, a, ch],
-                            rhs=parted[:, a, 2 * cols.start : 2 * cols.stop].bitcast(FP4X4),
+                            rhs=parted[c // 2][:, a, 2 * lo : 2 * (lo + SUB)].bitcast(FP4X4),
                             rhs_scale=tab_sc[:, a, :].bitcast(U8)[:, cols],
                             start=(a == 0),
                             stop=(a == 1),
@@ -162,14 +165,27 @@ def tile_list_htabg_mul_res_kernel(
                 if c < 3:
                     empty_yb(c, u)
 
-        got_w = held([P, J], U32, "got_w")
-        parted = held([P, 2, 2 * J], U8, "parted")
-        nc.vector.tensor_copy(got_w[:], tab_w[:].bitcast(U32).indirect(tab_list[:]))
-        permute(wb_c[:].rearrange("p a r -> p (a r)"), wb_raw[:].rearrange("p a r -> p (a r)"), 4)
-        nc.vector.tensor_copy(parted[:].bitcast(U16), got_w[:].bitcast(U16).rearrange("p (j d) -> p d j", d=2))
-        permute(wb_sc[:].rearrange("p a r -> p (a r)").bitcast(I32), wb_s[:].rearrange("p a r -> p (a r)"), 1)
+        def part(half, tag):
+            parted[half] = held([P, 2, 2 * HALF], U8, "parted%d" % half, tag)
+            nc.vector.tensor_copy(
+                parted[half][:].bitcast(U16), got_w[half][:].bitcast(U16).rearrange("p (j d) -> p d j", d=2)
+            )
+
+        wb_c = held([P, 2, R], I32, "wb_c", "w_cols")
+        got_w = [held([P, HALF], U32, "got_w%d" % half) for half in range(2)]
+        parted = {}
+        for half in range(2):
+            entries = tab_list[:, half * HALF // LIST : (half + 1) * HALF // LIST]
+            nc.vector.tensor_copy(got_w[half][:], tab_w[:].bitcast(U32).indirect(entries))
+        part(0, "parted0")
+        part(1, "parted1")
+        permute(wb_c[:].rearrange("p a r -> p (a r)"), wb_raw[:].rearrange("p a r -> p (a r)"), 8)
+        permute(wb_sc[:].rearrange("p a r -> p (a r)"), wb_s[:].rearrange("p a r -> p (a r)"), 2)
+        permute(wa_sc[:], wa_s[:], 2)
         table_product(0)
         table_product(1)
+        table_product(2)
+        table_product(3)
 
         planes.append(placed(after_wb, 0, [P, T], F32, "plane3"))
         wa_raw = placed(after_wb, PLANE_BYTES + 2048, [P, R // 2], I32, "wa_raw")
@@ -179,11 +195,12 @@ def tile_list_htabg_mul_res_kernel(
         for t in range(PACK):
             nc.sync.dma_start(wd_raw[:, t, :], wd_v[t])
 
-        res_sb = [held([P, N // P, HALF], F32, "res0", "rows"), held([P, N // P, HALF], F32, "res1", "parted")]
+        res_sb = [held([P, N // P, HALF], F32, "res0", "slot0"), placed(after_scales, 0, [P, N // P, HALF], F32, "res1")]
         for half in range(2):
             nc.sync.dma_start(res_sb[half][:], res_v[:, :, half * HALF : (half + 1) * HALF])
         for i in range(PACK - 1):
-            pick(i, 0, MAIN)
+            pick(i, 0, HALF)
+            pick(i, HALF, J)
 
         def interleave(dst, src):
             nc.scalar.copy(
@@ -196,8 +213,8 @@ def tile_list_htabg_mul_res_kernel(
         x_c, x_s, h_c, h_s, ya, y, wd_c, y_sb = {}, {}, {}, {}, {}, {}, {}, {}
 
         def new_x(c):
-            x_c[c] = ring.tile([P, CHUNK], U32, name="x_c", align_bytes=64)
-            x_s[c] = ring.tile([P, CHUNK], U8, name="x_s", align_bytes=64)
+            x_c[c] = held([P, CHUNK], U32, "x_c%d" % c)
+            x_s[c] = held([P, CHUNK], U8, "x_s%d" % c)
 
         def first(c, u):
             cols = slice(u * SUB, (u + 1) * SUB)
@@ -262,95 +279,78 @@ def tile_list_htabg_mul_res_kernel(
             queue.dma_start(out_v[:, blocks, cols], total[:])
 
         def empty(c, g):
-            if (c, g) == (0, 0):
-                y_sb[c, g] = placed(after_wb, 15360, [P, 2, CHUNK], F32, "y_sb00")
-            else:
-                y_sb[c, g] = held([P, 2, CHUNK], F32, "y_sb%d%d" % (c, g))
+            y_sb[c, g] = held([P, 2, CHUNK], F32, "y_sb%d%d" % (c, g))
             nc.scalar.copy(y_sb[c, g][:], y[c, g][:])
 
-        def finish_beside(c, g, total):
+        def finish_beside(c, g, total, lo=0, hi=2):
             cols = slice(c * CHUNK, (c + 1) * CHUNK)
             res_cols = slice((c % 2) * CHUNK, (c % 2 + 1) * CHUNK)
-            blocks = slice(2 * g, 2 * g + 2)
-            nc.gpsimd.tensor_tensor(total[:], y_sb[c, g][:], res_sb[c // 2][:, blocks, res_cols], ADD)
+            blocks = slice(2 * g + lo, 2 * g + hi)
+            nc.gpsimd.tensor_tensor(total[:], y_sb[c, g][:, lo:hi, :], res_sb[c // 2][:, blocks, res_cols], ADD)
             nc.sync.dma_start(out_v[:, blocks, cols], total[:])
 
-        wide, pair = [P, CHUNK, PACK], [P, 2, CHUNK]
+        def round_wd(g, tag):
+            wd_bf = held(wide, BF16, "wd_bf%d" % g, tag)
+            cols = slice(g * CHUNK, (g + 1) * CHUNK)
+            nc.gpsimd.tensor_scalar(
+                wd_bf[:], wd_raw[:, :, cols].rearrange("p i n -> p n i"), 1.0, 0.0, op0=MULT, op1=ADD
+            )
+            wd_c[g] = held([P, CHUNK], U32, "wd_c%d" % g)
+            return wd_bf
+
+        wide, pair, single = [P, CHUNK, PACK], [P, 2, CHUNK], [P, 1, CHUNK]
         pick(3, 0, CHUNK)
-        x_bf0 = [placed(late, 0, [P, SUB, PACK], BF16, "x_bf0a")[:], held([P, SUB, PACK], BF16, "x_bf0b")[:]]
-        for u in range(2):
-            interleave(x_bf0[u], picked_main[:, :, u * SUB : (u + 1) * SUB])
-        permute(wa_c[:].bitcast(I32), wa_raw[:], 2)
-        permute(wa_sc[:].bitcast(I32), wa_s[:], 1)
-        pick(3, CHUNK, MAIN)
-        x_bf1 = held(wide, BF16, "x_bf1")
-        interleave(x_bf1[:], picked_main[:, :, CHUNK : 2 * CHUNK])
+        pick(3, CHUNK, HALF)
+        pick(3, HALF, J)
+        permute(wa_c[:], wa_raw[:], 4)
+        x_bf = [held(wide, BF16, "x_bf%d" % c) for c in range(4)]
+        for c in range(4):
+            interleave(x_bf[c][:], picked_chunk(c))
 
-        new_x(0)
-        for u in range(2):
-            cols = slice(u * SUB, (u + 1) * SUB)
-            quantise(x_c[0][:, cols], x_s[0][:, cols], x_bf0[u])
-            first(0, u)
-        last = placed(late, 0, [P, PACK * CHUNK], F32, "last")
-        picked_last = last[:].rearrange("p (i j) -> p i j", i=PACK)
-        pick(0, MAIN, J)
-        wd_bf0 = last[:, 2 * CHUNK : 4 * CHUNK].bitcast(BF16).rearrange("p (n i) -> p n i", i=PACK)
-        interleave(wd_bf0, wd_raw[:, :, 0:256])
-        wd_bf1 = held(wide, BF16, "wd_bf1", "slot0")
-        nc.gpsimd.tensor_scalar(
-            wd_bf1[:], wd_raw[:, :, 256:512].rearrange("p i n -> p n i"), 1.0, 0.0, op0=MULT, op1=ADD
-        )
-
-        x_bf2 = placed(after_wb, 12288, wide, BF16, "x_bf2")
-        interleave(x_bf2[:], picked_main[:, :, 2 * CHUNK : MAIN])
-        h_bf0 = held(wide, BF16, "h_bf0")
+        quant_x(0, x_bf[0][:])
+        quant_x(1, x_bf[1][:])
+        wd_bf0 = round_wd(0, "x_bf1")
+        h_bf0 = held(wide, BF16, "h_bf0", "low")
         products(0, h_bf0)
-        quant_x(1, x_bf1[:])
-        wd_c[0] = held([P, N // 2], U32, "wd_c0", "yb_sb0")
-        quantise(wd_c[0][:], wd_s[:, 0:256], wd_bf0)
+
+        quant_x(2, x_bf[2][:])
+        quantise(wd_c[0][:], wd_s[:, 0:CHUNK], wd_bf0[:])
         quant_h(0, h_bf0[:])
         second(0, 0)
         empty(0, 0)
-        for i in range(1, PACK):
-            pick(i, MAIN, J)
-        wd_c[1] = placed(after_scales, PLANE_BYTES + 1024, [P, N // 2], U32, "wd_c1")
-        quantise(wd_c[1][:], wd_s[:, 256:512], wd_bf1[:])
-        second(0, 1)
-        x_bf3 = held(wide, BF16, "x_bf3", "slot0")
-        interleave(x_bf3[:], picked_last)
-        empty(0, 1)
-        quant_x(2, x_bf2[:])
+        wd_bf1 = round_wd(1, "low")
+        h_bf1 = held(wide, BF16, "h_bf1", "x_bf1")
+        products(1, h_bf1)
 
-        finish_beside(0, 0, placed(after_wb, 13312, pair, F32, "total00"))
         for u in range(2):
             empty_yb(3, u)
-        h_bf1 = placed(after_wb, 11264, wide, BF16, "h_bf1")
-        products(1, h_bf1)
         new_x(3)
-        quantise(x_c[3][:], x_s[3][:], x_bf3[:])
+        quantise(x_c[3][:], x_s[3][:], x_bf[3][:])
+        quantise(wd_c[1][:], wd_s[:, CHUNK:N], wd_bf1[:])
         quant_h(1, h_bf1[:])
-        second(1, 1)
-        second(1, 0)
+        second(0, 1)
         first(3, 0)
         first(3, 1)
+        second(1, 0)
+        second(1, 1)
+        empty(0, 1)
         empty(1, 0)
-
-        finish_beside(0, 1, placed(after_wb, 11264, pair, F32, "total01"))
-        h_bf2 = held(wide, BF16, "h_bf2", "slot0")
+        finish_beside(0, 0, held(pair, F32, "total00", "x_bf1"))
+        finish_beside(0, 1, held(pair, F32, "total01"))
+        h_bf2 = held(wide, BF16, "h_bf2", "low")
         products(2, h_bf2)
-        finish(1, 1)
+        h_bf3 = held(wide, BF16, "h_bf3", "h3")
+        products(3, h_bf3)
+
         quant_h(2, h_bf2[:])
         second(2, 1)
         second(2, 0)
-
-        finish_beside(1, 0, held(pair, F32, "total10", "slot0"))
-        h_bf3 = held(wide, BF16, "h_bf3", "h3")
-        products(3, h_bf3)
-        finish(2, 1)
+        finish(1, 1)
         quant_h(3, h_bf3[:])
         second(3, 0)
         second(3, 1)
-
+        finish_beside(1, 0, held(pair, F32, "total10", "h3"))
+        finish(2, 1)
         finish(2, 0)
         finish(3, 0)
         finish(3, 1, 0, 1)

@@ -138,9 +138,7 @@ def tile_list_htabg_mul_res_kernel(
 
         def empty_yb(c, u):
             shape = [P, CHUNK // SUB, SUB // 2, PACK, 2]
-            if c == 3 and u == 0:
-                yb_sb[c] = held(shape, F32, "yb_sb3", "high")
-            elif u == 0:
+            if u == 0:
                 yb_sb[c] = held(shape, F32, "yb_sb%d" % c)
             nc.scalar.copy(yb_sb[c][:, u], yb[c, u][:].rearrange("p t (c e) -> p c t e", e=2))
 
@@ -162,8 +160,7 @@ def tile_list_htabg_mul_res_kernel(
                             stop=(a == 1),
                         )
                 yb[c, u] = bank
-                if c < 3:
-                    empty_yb(c, u)
+                empty_yb(c, u)
 
         def part(half, tag):
             parted[half] = held([P, 2, 2 * HALF], U8, "parted%d" % half, tag)
@@ -289,56 +286,54 @@ def tile_list_htabg_mul_res_kernel(
             nc.gpsimd.tensor_tensor(total[:], y_sb[c, g][:, lo:hi, :], res_sb[c // 2][:, blocks, res_cols], ADD)
             nc.sync.dma_start(out_v[:, blocks, cols], total[:])
 
-        def round_wd(g, tag):
-            wd_bf = held(wide, BF16, "wd_bf%d" % g, tag)
-            cols = slice(g * CHUNK, (g + 1) * CHUNK)
-            nc.gpsimd.tensor_scalar(
-                wd_bf[:], wd_raw[:, :, cols].rearrange("p i n -> p n i"), 1.0, 0.0, op0=MULT, op1=ADD
-            )
+        def round_wd(g):
+            wd_bf[g] = held(wide, BF16, "wd_bf%d" % g)
+            interleave(wd_bf[g][:], wd_raw[:, :, g * CHUNK : (g + 1) * CHUNK])
+
+        def quant_wd(g):
             wd_c[g] = held([P, CHUNK], U32, "wd_c%d" % g)
-            return wd_bf
+            quantise(wd_c[g][:], wd_s[:, g * CHUNK : (g + 1) * CHUNK], wd_bf[g][:])
 
         wide, pair, single = [P, CHUNK, PACK], [P, 2, CHUNK], [P, 1, CHUNK]
         pick(3, 0, CHUNK)
         pick(3, CHUNK, HALF)
         pick(3, HALF, J)
         permute(wa_c[:], wa_raw[:], 4)
+        wd_bf = {}
         x_bf = [held(wide, BF16, "x_bf%d" % c) for c in range(4)]
         for c in range(4):
             interleave(x_bf[c][:], picked_chunk(c))
+            if c % 2 == 1:
+                round_wd(c // 2)
 
         quant_x(0, x_bf[0][:])
         quant_x(1, x_bf[1][:])
-        wd_bf0 = round_wd(0, "x_bf1")
         h_bf0 = held(wide, BF16, "h_bf0", "low")
         products(0, h_bf0)
 
-        quant_x(2, x_bf[2][:])
-        quantise(wd_c[0][:], wd_s[:, 0:CHUNK], wd_bf0[:])
+        quant_wd(0)
         quant_h(0, h_bf0[:])
         second(0, 0)
         empty(0, 0)
-        wd_bf1 = round_wd(1, "low")
-        h_bf1 = held(wide, BF16, "h_bf1", "x_bf1")
+        quant_x(2, x_bf[2][:])
+        h_bf1 = held(wide, BF16, "h_bf1")
         products(1, h_bf1)
 
-        for u in range(2):
-            empty_yb(3, u)
         new_x(3)
         quantise(x_c[3][:], x_s[3][:], x_bf[3][:])
-        quantise(wd_c[1][:], wd_s[:, CHUNK:N], wd_bf1[:])
         quant_h(1, h_bf1[:])
-        second(0, 1)
+        quant_wd(1)
+        second(1, 0)
         first(3, 0)
         first(3, 1)
-        second(1, 0)
+        second(0, 1)
         second(1, 1)
-        empty(0, 1)
         empty(1, 0)
-        finish_beside(0, 0, held(pair, F32, "total00", "x_bf1"))
-        finish_beside(0, 1, held(pair, F32, "total01"))
-        h_bf2 = held(wide, BF16, "h_bf2", "low")
+        finish_beside(0, 0, held(pair, F32, "total00", "wd_bf1"))
+        finish_beside(1, 0, held(pair, F32, "total10"))
+        h_bf2 = placed(after_wb, PLANE_BYTES + 3072, wide, BF16, "h_bf2")
         products(2, h_bf2)
+        finish(0, 1)
         h_bf3 = held(wide, BF16, "h_bf3", "h3")
         products(3, h_bf3)
 
@@ -349,7 +344,6 @@ def tile_list_htabg_mul_res_kernel(
         quant_h(3, h_bf3[:])
         second(3, 0)
         second(3, 1)
-        finish_beside(1, 0, held(pair, F32, "total10", "h3"))
         finish(2, 1)
         finish(2, 0)
         finish(3, 0)

@@ -36,7 +36,8 @@ def tile_list_htabg_mul_res_kernel(
         ring = ctx.enter_context(tc.tile_pool(name="ring", bufs=1))
         after_wb = ctx.enter_context(tc.tile_pool(name="after_wb", bufs=1))
         after_scales = ctx.enter_context(tc.tile_pool(name="after_scales", bufs=1))
-        psum = ctx.enter_context(tc.psum_pool(name="psum", bufs=8))
+        psum = ctx.enter_context(tc.psum_pool(name="psum", bufs=6))
+        psum_late = ctx.enter_context(tc.psum_pool(name="psum_late", bufs=2))
 
         def held(shape, dtype, name, tag=""):
             return keep.tile(shape, dtype, name=name, tag=tag or name, align_bytes=64)
@@ -61,7 +62,15 @@ def tile_list_htabg_mul_res_kernel(
         ident = held([P, P], F32, "ident")
         planes = [held([P, T], F32, "plane0", "slot0")]
         wd_s = held([P, N], U8, "wd_s")
-        picked = [held([P, PACK * HALF], F32, "picked0", "low"), held([P, PACK * HALF], F32, "picked1", "high")]
+        picked = held([P, 24 * CHUNK], F32, "picked")
+        picked1 = held([P, PACK * CHUNK], F32, "picked1", "low")
+        upper = picked[:, 13 * CHUNK : 21 * CHUNK].rearrange("p (i j) -> p i j", i=PACK)
+        picked_chunks = [
+            picked[:].rearrange("p (i j) -> p i j", i=PACK)[:, :, 0:CHUNK],
+            picked1[:].rearrange("p (i j) -> p i j", i=PACK),
+            upper[:, :, 0:CHUNK],
+            upper[:, :, CHUNK:HALF],
+        ]
 
         nc.gpsimd.memset(wb_s[:], 0)
         nc.vector.memset(tab_s[0:SCALE_ROW0, :], 0)
@@ -120,18 +129,15 @@ def tile_list_htabg_mul_res_kernel(
             )
 
         def pick(i, lo, hi):
-            half = lo // HALF
-            at = i * HALF - half * HALF
+            if lo == 0:
+                dst = picked[:, 6 * i * CHUNK : (6 * i + 1) * CHUNK]
+            elif lo == CHUNK:
+                dst = picked1[:, i * CHUNK : (i + 1) * CHUNK]
+            else:
+                dst = picked[:, 11 * CHUNK + i * HALF + lo : 11 * CHUNK + i * HALF + hi]
             nc.vector.tensor_tensor(
-                picked[half][:, at + lo : at + hi],
-                planes[i][:].indirect(head_lists[:, lo // LIST : hi // LIST]),
-                wgt[:, lo:hi],
-                MULT,
+                dst, planes[i][:].indirect(head_lists[:, lo // LIST : hi // LIST]), wgt[:, lo:hi], MULT
             )
-
-        def picked_chunk(c):
-            rows = picked[c // 2][:].rearrange("p (i j) -> p i j", i=PACK)
-            return rows[:, :, (c % 2) * CHUNK : (c % 2 + 1) * CHUNK]
 
         yb, yb_sb = {}, {}
 
@@ -139,14 +145,14 @@ def tile_list_htabg_mul_res_kernel(
         def empty_yb(c, u):
             shape = [P, CHUNK // SUB, SUB // 2, PACK, 2]
             if u == 0:
-                yb_sb[c] = held(shape, F32, "yb_sb%d" % c)
+                yb_sb[c] = held(shape, F32, "yb_sb%d" % c, "picked" if c == 3 else "")
             nc.scalar.copy(yb_sb[c][:, u], yb[c, u][:].rearrange("p t (c e) -> p c t e", e=2))
 
         def table_product(c):
             for u in range(CHUNK // SUB):
                 lo = (c % 2) * CHUNK + u * SUB
                 cols = slice(c * CHUNK + u * SUB, c * CHUNK + (u + 1) * SUB)
-                bank = psum.tile([P, PACK, SUB], F32, name="yb", tag="bank")
+                bank = (psum if c < 3 else psum_late).tile([P, PACK, SUB], F32, name="yb", tag="bank")
                 for t in range(PACK):
                     ch = slice(t * P, (t + 1) * P)
                     for a in range(2):
@@ -160,7 +166,8 @@ def tile_list_htabg_mul_res_kernel(
                             stop=(a == 1),
                         )
                 yb[c, u] = bank
-                empty_yb(c, u)
+                if c < 3:
+                    empty_yb(c, u)
 
         def part(half, tag):
             parted[half] = held([P, 2, 2 * HALF], U8, "parted%d" % half, tag)
@@ -196,8 +203,9 @@ def tile_list_htabg_mul_res_kernel(
         for half in range(2):
             nc.sync.dma_start(res_sb[half][:], res_v[:, :, half * HALF : (half + 1) * HALF])
         for i in range(PACK - 1):
-            pick(i, 0, HALF)
-            pick(i, HALF, J)
+            pick(i, 0, CHUNK)
+            pick(i, CHUNK, HALF)
+            pick(i, HALF, J if i < 2 else J - CHUNK)
 
         def interleave(dst, src):
             nc.scalar.copy(
@@ -301,12 +309,14 @@ def tile_list_htabg_mul_res_kernel(
         permute(wa_c[:], wa_raw[:], 4)
         wd_bf = {}
         x_bf = [held(wide, BF16, "x_bf%d" % c) for c in range(4)]
-        for c in range(4):
-            interleave(x_bf[c][:], picked_chunk(c))
+        interleave(x_bf[0][:], picked_chunks[0])
+        quant_x(0, x_bf[0][:])
+        pick(2, J - CHUNK, J)
+        for c in range(1, 4):
+            interleave(x_bf[c][:], picked_chunks[c])
             if c % 2 == 1:
                 round_wd(c // 2)
 
-        quant_x(0, x_bf[0][:])
         quant_x(1, x_bf[1][:])
         h_bf0 = held(wide, BF16, "h_bf0", "low")
         products(0, h_bf0)
@@ -329,6 +339,8 @@ def tile_list_htabg_mul_res_kernel(
         second(0, 1)
         second(1, 1)
         empty(1, 0)
+        for u in range(2):
+            empty_yb(3, u)
         finish_beside(0, 0, held(pair, F32, "total00", "wd_bf1"))
         finish_beside(1, 0, held(pair, F32, "total10"))
         h_bf2 = placed(after_wb, PLANE_BYTES + 3072, wide, BF16, "h_bf2")

@@ -62,15 +62,14 @@ def tile_list_htabg_mul_res_kernel(
         ident = held([P, P], F32, "ident")
         planes = [held([P, T], F32, "plane0", "slot0")]
         wd_s = held([P, N], U8, "wd_s")
-        picked = held([P, 24 * CHUNK], F32, "picked")
-        picked1 = held([P, PACK * CHUNK], F32, "picked1", "low")
-        upper = picked[:, 13 * CHUNK : 21 * CHUNK].rearrange("p (i j) -> p i j", i=PACK)
-        picked_chunks = [
-            picked[:].rearrange("p (i j) -> p i j", i=PACK)[:, :, 0:CHUNK],
-            picked1[:].rearrange("p (i j) -> p i j", i=PACK),
-            upper[:, :, 0:CHUNK],
-            upper[:, :, CHUNK:HALF],
+        outer = held([P, 6 * CHUNK], F32, "picked")
+        picked = [
+            outer[:, 2 * CHUNK : 6 * CHUNK],
+            held([P, PACK * CHUNK], F32, "picked1", "low")[:],
+            held([P, PACK * CHUNK], F32, "picked2")[:],
+            outer[:, 0 : PACK * CHUNK],
         ]
+        picked_chunks = [rows.rearrange("p (i j) -> p i j", i=PACK) for rows in picked]
 
         nc.gpsimd.memset(wb_s[:], 0)
         nc.vector.memset(tab_s[0:SCALE_ROW0, :], 0)
@@ -129,12 +128,8 @@ def tile_list_htabg_mul_res_kernel(
             )
 
         def pick(i, lo, hi):
-            if lo == 0:
-                dst = picked[:, 6 * i * CHUNK : (6 * i + 1) * CHUNK]
-            elif lo == CHUNK:
-                dst = picked1[:, i * CHUNK : (i + 1) * CHUNK]
-            else:
-                dst = picked[:, 11 * CHUNK + i * HALF + lo : 11 * CHUNK + i * HALF + hi]
+            c = lo // CHUNK
+            dst = picked[c][:, (i - c) * CHUNK + lo : (i - c) * CHUNK + hi]
             nc.vector.tensor_tensor(
                 dst, planes[i][:].indirect(head_lists[:, lo // LIST : hi // LIST]), wgt[:, lo:hi], MULT
             )
@@ -203,9 +198,8 @@ def tile_list_htabg_mul_res_kernel(
         for half in range(2):
             nc.sync.dma_start(res_sb[half][:], res_v[:, :, half * HALF : (half + 1) * HALF])
         for i in range(PACK - 1):
-            pick(i, 0, CHUNK)
-            pick(i, CHUNK, HALF)
-            pick(i, HALF, J if i < 2 else J - CHUNK)
+            for c in range(4 if i < 2 else 3):
+                pick(i, c * CHUNK, (c + 1) * CHUNK)
 
         def interleave(dst, src):
             nc.scalar.copy(
@@ -303,15 +297,19 @@ def tile_list_htabg_mul_res_kernel(
             quantise(wd_c[g][:], wd_s[:, g * CHUNK : (g + 1) * CHUNK], wd_bf[g][:])
 
         wide, pair, single = [P, CHUNK, PACK], [P, 2, CHUNK], [P, 1, CHUNK]
-        pick(3, 0, CHUNK)
+        pick(3, 0, SUB)
+        pick(3, SUB, CHUNK)
         pick(3, CHUNK, HALF)
-        pick(3, HALF, J)
+        pick(3, HALF, J - CHUNK)
         permute(wa_c[:], wa_raw[:], 4)
         wd_bf = {}
         x_bf = [held(wide, BF16, "x_bf%d" % c) for c in range(4)]
-        interleave(x_bf[0][:], picked_chunks[0])
+        for u in range(2):
+            cols = slice(u * SUB, (u + 1) * SUB)
+            interleave(x_bf[0][:, cols, :], picked_chunks[0][:, :, cols])
         quant_x(0, x_bf[0][:])
         pick(2, J - CHUNK, J)
+        pick(3, J - CHUNK, J)
         for c in range(1, 4):
             interleave(x_bf[c][:], picked_chunks[c])
             if c % 2 == 1:
@@ -352,10 +350,10 @@ def tile_list_htabg_mul_res_kernel(
         quant_h(2, h_bf2[:])
         second(2, 1)
         second(2, 0)
-        finish(1, 1)
         quant_h(3, h_bf3[:])
         second(3, 0)
         second(3, 1)
+        finish(1, 1)
         finish(2, 1)
         finish(2, 0)
         finish(3, 0)

@@ -62,9 +62,9 @@ def tile_list_htabg_mul_res_kernel(
         ident = held([P, P], F32, "ident")
         planes = [held([P, T], F32, "plane0", "slot0")]
         wd_s = held([P, N], U8, "wd_s")
-        outer = held([P, 6 * CHUNK], F32, "picked")
+        outer = held([P, 7 * CHUNK], F32, "picked")
         picked = [
-            outer[:, 2 * CHUNK : 6 * CHUNK],
+            outer[:, 3 * CHUNK : 7 * CHUNK],
             held([P, PACK * CHUNK], F32, "picked1", "low")[:],
             held([P, PACK * CHUNK], F32, "picked2")[:],
             outer[:, 0 : PACK * CHUNK],
@@ -198,7 +198,7 @@ def tile_list_htabg_mul_res_kernel(
         for half in range(2):
             nc.sync.dma_start(res_sb[half][:], res_v[:, :, half * HALF : (half + 1) * HALF])
         for i in range(PACK - 1):
-            for c in range(4 if i < 2 else 3):
+            for c in range(4):
                 pick(i, c * CHUNK, (c + 1) * CHUNK)
 
         def interleave(dst, src):
@@ -308,7 +308,6 @@ def tile_list_htabg_mul_res_kernel(
             cols = slice(u * SUB, (u + 1) * SUB)
             interleave(x_bf[0][:, cols, :], picked_chunks[0][:, :, cols])
         quant_x(0, x_bf[0][:])
-        pick(2, J - CHUNK, J)
         pick(3, J - CHUNK, J)
         for c in range(1, 4):
             interleave(x_bf[c][:], picked_chunks[c])

@@ -203,7 +203,7 @@ def tile_list_htabg_mul_res_kernel(
 
         def interleave(dst, src):
             nc.scalar.copy(
-                dst.rearrange("p (c e) i -> p c i e", e=4), src.rearrange("p i (c e) -> p c i e", e=4)
+                dst.rearrange("p (c e) i -> p c i e", e=2), src.rearrange("p i (c e) -> p c i e", e=2)
             )
 
         def quantise(codes, scales, src):

@@ -36,8 +36,10 @@ def tile_list_htabg_mul_res_kernel(
         ring = ctx.enter_context(tc.tile_pool(name="ring", bufs=1))
         after_wb = ctx.enter_context(tc.tile_pool(name="after_wb", bufs=1))
         after_scales = ctx.enter_context(tc.tile_pool(name="after_scales", bufs=1))
-        psum = ctx.enter_context(tc.psum_pool(name="psum", bufs=6))
-        psum_late = ctx.enter_context(tc.psum_pool(name="psum_late", bufs=2))
+        psum = ctx.enter_context(tc.psum_pool(name="psum", bufs=1))
+
+        def bank(number, shape, name):
+            return psum.tile(shape, F32, name=name, tag="bank%d" % number)
 
         def held(shape, dtype, name, tag=""):
             return keep.tile(shape, dtype, name=name, tag=tag or name, align_bytes=64)
@@ -95,14 +97,14 @@ def tile_list_htabg_mul_res_kernel(
         nc.sync.dma_start(planes[0][:], x_planes[0])
         nc.sync.dma_start(head_lists[:], offs2)
 
-        turned = psum.tile([P, P], F32, name="turned", tag="bank")
+        turned = bank(7, [P, P], "turned")
         nc.tensor.transpose(turned[:], w_rows[:], ident[:])
         nc.scalar.copy(
             w_cols[:].rearrange("m c (g r) -> m c g r", r=LIST),
             turned[:, 0:64].rearrange("m (g c) -> m c g", c=J // P).unsqueeze(3).to_broadcast([P, J // P, 8, LIST]),
         )
         for half in range(2):
-            spread = psum.tile([P, PACK, P], F32, name="spread", tag="bank")
+            spread = bank(5 + half, [P, PACK, P], "spread")
             for c in range(PACK):
                 nc.tensor.transpose(spread[:, c, :], w_cols[:, PACK * half + c, :], ident[:])
             nc.scalar.copy(wgt[:, half * HALF : (half + 1) * HALF], spread[:].rearrange("p c m -> p (c m)"))
@@ -147,12 +149,12 @@ def tile_list_htabg_mul_res_kernel(
             for u in range(CHUNK // SUB):
                 lo = (c % 2) * CHUNK + u * SUB
                 cols = slice(c * CHUNK + u * SUB, c * CHUNK + (u + 1) * SUB)
-                bank = (psum if c < 3 else psum_late).tile([P, PACK, SUB], F32, name="yb", tag="bank")
+                sums = bank(2 * c + u, [P, PACK, SUB], "yb")
                 for t in range(PACK):
                     ch = slice(t * P, (t + 1) * P)
                     for a in range(2):
                         nc.tensor.matmul_mx(
-                            out=bank[:, t, :],
+                            out=sums[:, t, :],
                             lhsT=wb_c[:, a, ch].bitcast(FP8X4),
                             lhsT_scale=wb_sc[:, a, ch],
                             rhs=parted[c // 2][:, a, 2 * lo : 2 * (lo + SUB)].bitcast(FP4X4),
@@ -160,7 +162,7 @@ def tile_list_htabg_mul_res_kernel(
                             start=(a == 0),
                             stop=(a == 1),
                         )
-                yb[c, u] = bank
+                yb[c, u] = sums
                 if c < 3:
                     empty_yb(c, u)
 
@@ -215,9 +217,9 @@ def tile_list_htabg_mul_res_kernel(
             x_c[c] = held([P, CHUNK], U32, "x_c%d" % c)
             x_s[c] = held([P, CHUNK], U8, "x_s%d" % c)
 
-        def first(c, u):
+        def first(c, u, number):
             cols = slice(u * SUB, (u + 1) * SUB)
-            ya[c, u] = psum.tile([P, PACK, SUB], F32, name="ya", tag="bank")
+            ya[c, u] = bank(number, [P, PACK, SUB], "ya")
             for t in range(PACK):
                 ch = slice(t * P, (t + 1) * P)
                 nc.tensor.matmul_mx(
@@ -233,8 +235,8 @@ def tile_list_htabg_mul_res_kernel(
         def quant_x(c, src):
             new_x(c)
             quantise(x_c[c][:], x_s[c][:], src)
-            first(c, 0)
-            first(c, 1)
+            first(c, 0, 2 * c)
+            first(c, 1, 2 * c + 1)
 
         def product(c, u, dst):
             nc.vector.tensor_tensor(
@@ -256,8 +258,8 @@ def tile_list_htabg_mul_res_kernel(
             new_h(c)
             quantise(h_c[c][:], h_s[c][:], src)
 
-        def second(c, g):
-            y[c, g] = psum.tile([P, 2, CHUNK], F32, name="y", tag="bank")
+        def second(c, g, number):
+            y[c, g] = bank(number, [P, 2, CHUNK], "y")
             for b in range(2):
                 nc.tensor.matmul_mx(
                     out=y[c, g][:, b, :],
@@ -320,7 +322,7 @@ def tile_list_htabg_mul_res_kernel(
 
         quant_wd(0)
         quant_h(0, h_bf0[:])
-        second(0, 0)
+        second(0, 0, 0)
         empty(0, 0)
         quant_x(2, x_bf[2][:])
         h_bf1 = held(wide, BF16, "h_bf1")
@@ -330,11 +332,9 @@ def tile_list_htabg_mul_res_kernel(
         quantise(x_c[3][:], x_s[3][:], x_bf[3][:])
         quant_h(1, h_bf1[:])
         quant_wd(1)
-        second(1, 0)
-        first(3, 0)
-        first(3, 1)
-        second(0, 1)
-        second(1, 1)
+        second(1, 0, 1)
+        first(3, 0, 2)
+        second(0, 1, 3)
         empty(1, 0)
         for u in range(2):
             empty_yb(3, u)
@@ -342,16 +342,19 @@ def tile_list_htabg_mul_res_kernel(
         finish_beside(1, 0, held(pair, F32, "total10"))
         h_bf2 = placed(after_wb, PLANE_BYTES + 3072, wide, BF16, "h_bf2")
         products(2, h_bf2)
+        first(3, 1, 5)
         finish(0, 1)
         h_bf3 = held(wide, BF16, "h_bf3", "h3")
-        products(3, h_bf3)
+        product(3, 0, h_bf3[:, 0:SUB, :])
+        second(1, 1, 2)
+        product(3, 1, h_bf3[:, SUB:CHUNK, :])
 
         quant_h(2, h_bf2[:])
-        second(2, 1)
-        second(2, 0)
+        second(2, 1, 4)
+        second(2, 0, 0)
         quant_h(3, h_bf3[:])
-        second(3, 0)
-        second(3, 1)
+        second(3, 0, 1)
+        second(3, 1, 3)
         finish(1, 1)
         finish(2, 1)
         finish(2, 0)

@@ -42,10 +42,10 @@ def tile_list_htabg_mul_res_kernel(
             return psum.tile(shape, F32, name=name, tag="bank%d" % number)
 
         def held(shape, dtype, name, tag=""):
-            return keep.tile(shape, dtype, name=name, tag=tag or name, align_bytes=64)
+            return keep.tile(shape, dtype, name=name, tag=tag or name, align_bytes=256)
 
         def placed(pool, offset, shape, dtype, name):
-            return pool.tile(shape, dtype, name=name, offset=offset, align_bytes=64)
+            return pool.tile(shape, dtype, name=name, offset=offset, align_bytes=256)
 
         tab_list = keep.tile([P, J // LIST], U16, name="tab_list")
         head_lists = keep.tile([P, J // LIST], U16, name="head_lists")
@@ -275,7 +275,7 @@ def tile_list_htabg_mul_res_kernel(
             cols = slice(c * CHUNK, (c + 1) * CHUNK)
             res_cols = slice((c % 2) * CHUNK, (c % 2 + 1) * CHUNK)
             blocks = slice(2 * g + lo, 2 * g + hi)
-            total = ring.tile([P, hi - lo, CHUNK], F32, name="total", bufs=6)
+            total = ring.tile([P, hi - lo, CHUNK], F32, name="total", bufs=6, align_bytes=256)
             nc.vector.tensor_tensor(total[:], y[c, g][:, lo:hi, :], res_sb[c // 2][:, blocks, res_cols], ADD)
             queue.dma_start(out_v[:, blocks, cols], total[:])
 

@@ -54,12 +54,11 @@ def tile_list_htabg_mul_res_kernel(
         wb_raw = placed(after_wb, PLANE_BYTES - 512, [P, 2, R], I32, "wb_raw")
         wb_s = held([P, 2, R // 4], I32, "wb_s", "rows")
         got_s = held([P, J], U8, "got_s")
-        tab_sc = held([P, 2, J // 4], I32, "tab_sc")
         wb_sc = held([P, 2, R], U8, "wb_sc")
         wa_c = held([P, 2 * R], U8, "wa_c")
         wa_sc = held([P, R], U8, "wa_sc")
         wgt = held([P, J], F32, "wgt")
-        w_rows = held([P, P], F32, "w_rows")
+        w_rows = held([P, P], F32, "w_rows", "early")
         w_cols = held([P, J // P, P], F32, "w_cols")
         ident = held([P, P], F32, "ident")
         planes = [held([P, T], F32, "plane0", "slot0")]
@@ -77,7 +76,6 @@ def tile_list_htabg_mul_res_kernel(
         nc.vector.memset(tab_s[0:SCALE_ROW0, :], 0)
         nc.vector.memset(w_rows[64:P, :], 0.0)
         make_identity(nc, ident[:])
-        nc.gpsimd.memset(tab_sc[:], 0)
 
         tab_scales_i = tab_scales.bitcast(I32)
         wa_scales_i = wa_scales.bitcast(I32)
@@ -87,8 +85,8 @@ def tile_list_htabg_mul_res_kernel(
         res_v = res.rearrange("(b m) j -> m b j", m=P)
         out_v = out.rearrange("(b m) j -> m b j", m=P)
 
-        nc.sync.dma_start(tab_list[:], offs)
         nc.sync.dma_start(tab_s[SCALE_ROW0:P, :], tab_scales_i.rearrange("a q n -> q a n"))
+        nc.sync.dma_start(tab_list[:], offs)
         nc.sync.dma_start(w_rows[0:64, :], wgt2.rearrange("(g r) (c m) -> g r c m", r=LIST, m=P)[:, 0])
         nc.sync.dma_start(tab_w[:], tab_words[0].rearrange("p t b -> p (t b)").bitcast(I32))
         nc.sync.dma_start(wb_raw[:], wb_words.rearrange("a p r i -> p a (r i)").bitcast(I32))
@@ -99,6 +97,8 @@ def tile_list_htabg_mul_res_kernel(
 
         turned = bank(7, [P, P], "turned")
         nc.tensor.transpose(turned[:], w_rows[:], ident[:])
+        tab_sc = held([P, 2, J // 4], I32, "tab_sc", "early")
+        nc.gpsimd.memset(tab_sc[:], 0)
         nc.scalar.copy(
             w_cols[:].rearrange("m c (g r) -> m c g r", r=LIST),
             turned[:, 0:64].rearrange("m (g c) -> m c g", c=J // P).unsqueeze(3).to_broadcast([P, J // P, 8, LIST]),

from contextlib import ExitStack

import concourse.mybir as mybir
from concourse.masks import make_identity

K, L, R, N, T, J = 512, 1024, 512, 512, 2048, 1024
FLOPS = 2 * J * (K * R + L * R + R * N)

F32 = mybir.dt.float32
BF16 = mybir.dt.bfloat16
I32 = mybir.dt.int32
U32 = mybir.dt.uint32
U16 = mybir.dt.uint16
U8 = mybir.dt.uint8
FP8X4 = mybir.dt.float8_e4m3fn_x4
FP4X4 = mybir.dt.float4_e2m1fn_x4
MULT = mybir.AluOpType.mult
ADD = mybir.AluOpType.add

P = 128
PACK = 4
SUB = 128
CHUNK = 256
HALF = 512
LIST = 16
PLANE_BYTES = 4 * T
SCALE_ROW0 = 96


def tile_list_htabg_mul_res_kernel(
    tc, tab_words, tab_scales, xT, wgt2, wa_words, wa_scales, wb_words, wb_scales, wd, res, offs, offs2, out
):
    nc = tc.nc
    with ExitStack() as ctx:
        keep = ctx.enter_context(tc.tile_pool(name="keep", bufs=1))
        ring = ctx.enter_context(tc.tile_pool(name="ring", bufs=1))
        after_wb = ctx.enter_context(tc.tile_pool(name="after_wb", bufs=1))
        after_scales = ctx.enter_context(tc.tile_pool(name="after_scales", bufs=1))
        psum = ctx.enter_context(tc.psum_pool(name="psum", bufs=1))

        def bank(number, shape, name):
            return psum.tile(shape, F32, name=name, tag="bank%d" % number)

        def held(shape, dtype, name, tag=""):
            return keep.tile(shape, dtype, name=name, tag=tag or name, align_bytes=256)

        def placed(pool, offset, shape, dtype, name):
            return pool.tile(shape, dtype, name=name, offset=offset, align_bytes=256)

        tab_list = keep.tile([P, J // LIST], U16, name="tab_list")
        head_lists = keep.tile([P, J // LIST], U16, name="head_lists")
        tab_s = placed(after_scales, PLANE_BYTES - 512, [P, T // 4], I32, "tab_s")
        tab_w = held([P, T], I32, "tab_w")
        wb_raw = placed(after_wb, PLANE_BYTES - 512, [P, 2, R], I32, "wb_raw")
        wb_s = held([P, 2, R // 4], I32, "wb_s", "rows")
        got_s = held([P, J], U8, "got_s")
        wb_sc = held([P, 2, R], U8, "wb_sc")
        wa_c = held([P, 2 * R], U8, "wa_c")
        wa_sc = held([P, R], U8, "wa_sc")
        wgt = held([P, J], F32, "wgt")
        w_rows = held([P, P], F32, "w_rows", "early")
        w_cols = held([P, J // P, P], F32, "w_cols")
        ident = held([P, P], F32, "ident")
        planes = [held([P, T], F32, "plane0", "slot0")]
        wd_s = held([P, N], U8, "wd_s")
        outer = held([P, 7 * CHUNK], F32, "picked")
        picked = [
            outer[:, 3 * CHUNK : 7 * CHUNK],
            held([P, PACK * CHUNK], F32, "picked1", "low")[:],
            held([P, PACK * CHUNK], F32, "picked2")[:],
            outer[:, 0 : PACK * CHUNK],
        ]
        picked_chunks = [rows.rearrange("p (i j) -> p i j", i=PACK) for rows in picked]

        nc.gpsimd.memset(wb_s[:], 0)
        nc.vector.memset(tab_s[0:SCALE_ROW0, :], 0)
        nc.vector.memset(w_rows[64:P, :], 0.0)
        make_identity(nc, ident[:])

        tab_scales_i = tab_scales.bitcast(I32)
        wa_scales_i = wa_scales.bitcast(I32)
        wb_scales_i = wb_scales.bitcast(I32)
        x_planes = xT.rearrange("(p i) t -> i p t", i=PACK)
        wd_v = wd.rearrange("(g t s) n -> t g s n", t=PACK, s=8)
        res_v = res.rearrange("(b m) j -> m b j", m=P)
        out_v = out.rearrange("(b m) j -> m b j", m=P)

        nc.sync.dma_start(tab_s[SCALE_ROW0:P, :], tab_scales_i.rearrange("a q n -> q a n"))
        nc.sync.dma_start(tab_list[:], offs)
        nc.sync.dma_start(w_rows[0:64, :], wgt2.rearrange("(g r) (c m) -> g r c m", r=LIST, m=P)[:, 0])
        nc.sync.dma_start(tab_w[:], tab_words[0].rearrange("p t b -> p (t b)").bitcast(I32))
        nc.sync.dma_start(wb_raw[:], wb_words.rearrange("a p r i -> p a (r i)").bitcast(I32))
        for r in range(4):
            nc.sync.dma_start(wb_s[r:P:32, :, :], wb_scales_i.rearrange("a (q r) n -> r q a n", r=4)[r])
        nc.sync.dma_start(planes[0][:], x_planes[0])
        nc.sync.dma_start(head_lists[:], offs2)

        turned = bank(7, [P, P], "turned")
        nc.tensor.transpose(turned[:], w_rows[:], ident[:])
        tab_sc = held([P, 2, J // 4], I32, "tab_sc", "early")
        nc.gpsimd.memset(tab_sc[:], 0)
        nc.scalar.copy(
            w_cols[:].rearrange("m c (g r) -> m c g r", r=LIST),
            turned[:, 0:64].rearrange("m (g c) -> m c g", c=J // P).unsqueeze(3).to_broadcast([P, J // P, 8, LIST]),
        )
        for half in range(2):
            spread = bank(5 + half, [P, PACK, P], "spread")
            for c in range(PACK):
                nc.tensor.transpose(spread[:, c, :], w_cols[:, PACK * half + c, :], ident[:])
            nc.scalar.copy(wgt[:, half * HALF : (half + 1) * HALF], spread[:].rearrange("p c m -> p (c m)"))

        nc.vector.tensor_copy(got_s[:], tab_s[:].bitcast(U8).indirect(tab_list[:]))
        for q in (0, 2, 1, 3):
            row = SCALE_ROW0 + 8 * q
            nc.sync.dma_start(tab_sc[32 * q : 32 * q + 4, :, :], got_s[:].bitcast(I32)[row : row + 8, :])

        planes.append(placed(after_scales, 0, [P, T], F32, "plane1"))
        wa_s = placed(after_scales, PLANE_BYTES, [P, R // 4], I32, "wa_s")
        planes.append(placed(after_scales, PLANE_BYTES + 1024, [P, T], F32, "plane2"))
        nc.gpsimd.memset(wa_s[:], 0)
        nc.sync.dma_start(planes[1][:], x_planes[1])
        nc.sync.dma_start(planes[2][:], x_planes[2])
        for r in range(4):
            nc.sync.dma_start(wa_s[r:P:32, :], wa_scales_i[0].rearrange("(q r) n -> r q n", r=4)[r])

        def permute(dst, src, run):
            nc.scalar.copy(
                dst.bitcast(U32).rearrange("p (a t g s) -> p a t g s", t=PACK, g=16, s=run),
                src.bitcast(U32).rearrange("p (a g t s) -> p a t g s", t=PACK, g=16, s=run),
            )

        def pick(i, lo, hi):
            c = lo // CHUNK
            dst = picked[c][:, (i - c) * CHUNK + lo : (i - c) * CHUNK + hi]
            nc.vector.tensor_tensor(
                dst, planes[i][:].indirect(head_lists[:, lo // LIST : hi // LIST]), wgt[:, lo:hi], MULT
            )

        yb, yb_sb = {}, {}


        def empty_yb(c, u):
            shape = [P, CHUNK // SUB, SUB // 2, PACK, 2]
            if u == 0:
                yb_sb[c] = held(shape, F32, "yb_sb%d" % c, "picked" if c == 3 else "")
            nc.scalar.copy(yb_sb[c][:, u], yb[c, u][:].rearrange("p t (c e) -> p c t e", e=2))

        def table_product(c):
            for u in range(CHUNK // SUB):
                lo = (c % 2) * CHUNK + u * SUB
                cols = slice(c * CHUNK + u * SUB, c * CHUNK + (u + 1) * SUB)
                sums = bank(2 * c + u, [P, PACK, SUB], "yb")
                for t in range(PACK):
                    ch = slice(t * P, (t + 1) * P)
                    for a in range(2):
                        nc.tensor.matmul_mx(
                            out=sums[:, t, :],
                            lhsT=wb_c[:, a, ch].bitcast(FP8X4),
                            lhsT_scale=wb_sc[:, a, ch],
                            rhs=parted[c // 2][:, a, 2 * lo : 2 * (lo + SUB)].bitcast(FP4X4),
                            rhs_scale=tab_sc[:, a, :].bitcast(U8)[:, cols],
                            start=(a == 0),
                            stop=(a == 1),
                        )
                yb[c, u] = sums
                if c < 3:
                    empty_yb(c, u)

        def part(half, tag):
            parted[half] = held([P, 2, 2 * HALF], U8, "parted%d" % half, tag)
            nc.vector.tensor_copy(
                parted[half][:].bitcast(U16), got_w[half][:].bitcast(U16).rearrange("p (j d) -> p d j", d=2)
            )

        wb_c = held([P, 2, R], I32, "wb_c", "w_cols")
        got_w = [held([P, HALF], U32, "got_w%d" % half) for half in range(2)]
        parted = {}
        for half in range(2):
            entries = tab_list[:, half * HALF // LIST : (half + 1) * HALF // LIST]
            nc.vector.tensor_copy(got_w[half][:], tab_w[:].bitcast(U32).indirect(entries))
        part(0, "parted0")
        part(1, "parted1")
        permute(wb_c[:].rearrange("p a r -> p (a r)"), wb_raw[:].rearrange("p a r -> p (a r)"), 8)
        permute(wb_sc[:].rearrange("p a r -> p (a r)"), wb_s[:].rearrange("p a r -> p (a r)"), 2)
        permute(wa_sc[:], wa_s[:], 2)
        table_product(0)
        table_product(1)
        table_product(2)
        table_product(3)

        planes.append(placed(after_wb, 0, [P, T], F32, "plane3"))
        wa_raw = placed(after_wb, PLANE_BYTES + 2048, [P, R // 2], I32, "wa_raw")
        wd_raw = placed(after_wb, PLANE_BYTES + 3072, [P, PACK, N], F32, "wd_raw")
        nc.sync.dma_start(planes[3][:], x_planes[3])
        nc.sync.dma_start(wa_raw[:], wa_words[0].bitcast(I32))
        for t in range(PACK):
            nc.sync.dma_start(wd_raw[:, t, :], wd_v[t])

        res_sb = [held([P, N // P, HALF], F32, "res0", "slot0"), placed(after_scales, 0, [P, N // P, HALF], F32, "res1")]
        for half in range(2):
            nc.sync.dma_start(res_sb[half][:], res_v[:, :, half * HALF : (half + 1) * HALF])
        for i in range(PACK - 1):
            for c in range(4):
                pick(i, c * CHUNK, (c + 1) * CHUNK)

        def interleave(dst, src):
            nc.scalar.copy(
                dst.rearrange("p (c e) i -> p c i e", e=2), src.rearrange("p i (c e) -> p c i e", e=2)
            )

        def quantise(codes, scales, src):
            nc.vector.quantize_mx(out=codes.bitcast(FP8X4), scales=scales, in_=src.rearrange("p n i -> p (n i)"))

        x_c, x_s, h_c, h_s, ya, y, wd_c, y_sb = {}, {}, {}, {}, {}, {}, {}, {}

        def new_x(c):
            x_c[c] = held([P, CHUNK], U32, "x_c%d" % c)
            x_s[c] = held([P, CHUNK], U8, "x_s%d" % c)

        def first(c, u, number):
            cols = slice(u * SUB, (u + 1) * SUB)
            ya[c, u] = bank(number, [P, PACK, SUB], "ya")
            for t in range(PACK):
                ch = slice(t * P, (t + 1) * P)
                nc.tensor.matmul_mx(
                    out=ya[c, u][:, t, :],
                    lhsT=wa_c[:, 2 * t * P : 2 * (t + 1) * P].bitcast(FP4X4),
                    lhsT_scale=wa_sc[:, ch],
                    rhs=x_c[c][:, cols].bitcast(FP8X4),
                    rhs_scale=x_s[c][:, cols],
                    start=True,
                    stop=True,
                )

        def quant_x(c, src):
            new_x(c)
            quantise(x_c[c][:], x_s[c][:], src)
            first(c, 0, 2 * c)
            first(c, 1, 2 * c + 1)

        def product(c, u, dst):
            nc.vector.tensor_tensor(
                dst.rearrange("p (c e) t -> p c t e", e=2),
                ya[c, u][:].rearrange("p t (c e) -> p c t e", e=2),
                yb_sb[c][:, u],
                MULT,
            )

        def products(c, h_bf):
            for u in range(CHUNK // SUB):
                product(c, u, h_bf[:, u * SUB : (u + 1) * SUB, :])

        def new_h(c):
            h_c[c] = held([P, CHUNK], U32, "h_c%d" % c)
            h_s[c] = held([P, CHUNK], U8, "h_s%d" % c)

        def quant_h(c, src):
            new_h(c)
            quantise(h_c[c][:], h_s[c][:], src)

        def second(c, g, number):
            y[c, g] = bank(number, [P, 2, CHUNK], "y")
            for b in range(2):
                nc.tensor.matmul_mx(
                    out=y[c, g][:, b, :],
                    lhsT=wd_c[g][:, b * P : (b + 1) * P].bitcast(FP8X4),
                    lhsT_scale=wd_s[:, (2 * g + b) * P : (2 * g + b + 1) * P],
                    rhs=h_c[c][:].bitcast(FP8X4),
                    rhs_scale=h_s[c][:],
                    start=True,
                    stop=True,
                )

        def finish(c, g, lo=0, hi=2, queue=nc.sync):
            cols = slice(c * CHUNK, (c + 1) * CHUNK)
            res_cols = slice((c % 2) * CHUNK, (c % 2 + 1) * CHUNK)
            blocks = slice(2 * g + lo, 2 * g + hi)
            total = ring.tile([P, hi - lo, CHUNK], F32, name="total", bufs=6, align_bytes=256)
            nc.vector.tensor_tensor(total[:], y[c, g][:, lo:hi, :], res_sb[c // 2][:, blocks, res_cols], ADD)
            queue.dma_start(out_v[:, blocks, cols], total[:])

        def empty(c, g):
            y_sb[c, g] = held([P, 2, CHUNK], F32, "y_sb%d%d" % (c, g))
            nc.scalar.copy(y_sb[c, g][:], y[c, g][:])

        def finish_beside(c, g, total, lo=0, hi=2):
            cols = slice(c * CHUNK, (c + 1) * CHUNK)
            res_cols = slice((c % 2) * CHUNK, (c % 2 + 1) * CHUNK)
            blocks = slice(2 * g + lo, 2 * g + hi)
            nc.gpsimd.tensor_tensor(total[:], y_sb[c, g][:, lo:hi, :], res_sb[c // 2][:, blocks, res_cols], ADD)
            nc.sync.dma_start(out_v[:, blocks, cols], total[:])

        def round_wd(g):
            wd_bf[g] = held(wide, BF16, "wd_bf%d" % g)
            interleave(wd_bf[g][:], wd_raw[:, :, g * CHUNK : (g + 1) * CHUNK])

        def quant_wd(g):
            wd_c[g] = held([P, CHUNK], U32, "wd_c%d" % g)
            quantise(wd_c[g][:], wd_s[:, g * CHUNK : (g + 1) * CHUNK], wd_bf[g][:])

        wide, pair, single = [P, CHUNK, PACK], [P, 2, CHUNK], [P, 1, CHUNK]
        pick(3, 0, SUB)
        pick(3, SUB, CHUNK)
        pick(3, CHUNK, HALF)
        pick(3, HALF, J - CHUNK)
        permute(wa_c[:], wa_raw[:], 4)
        wd_bf = {}
        x_bf = [held(wide, BF16, "x_bf%d" % c) for c in range(4)]
        for u in range(2):
            cols = slice(u * SUB, (u + 1) * SUB)
            interleave(x_bf[0][:, cols, :], picked_chunks[0][:, :, cols])
        quant_x(0, x_bf[0][:])
        pick(3, J - CHUNK, J)
        for c in range(1, 4):
            interleave(x_bf[c][:], picked_chunks[c])
            if c % 2 == 1:
                round_wd(c // 2)

        quant_x(1, x_bf[1][:])
        h_bf0 = held(wide, BF16, "h_bf0", "low")
        products(0, h_bf0)

        quant_wd(0)
        quant_h(0, h_bf0[:])
        second(0, 0, 0)
        empty(0, 0)
        quant_x(2, x_bf[2][:])
        h_bf1 = held(wide, BF16, "h_bf1")
        products(1, h_bf1)

        new_x(3)
        quantise(x_c[3][:], x_s[3][:], x_bf[3][:])
        quant_h(1, h_bf1[:])
        quant_wd(1)
        second(1, 0, 1)
        first(3, 0, 2)
        second(0, 1, 3)
        empty(1, 0)
        for u in range(2):
            empty_yb(3, u)
        finish_beside(0, 0, held(pair, F32, "total00", "wd_bf1"))
        finish_beside(1, 0, held(pair, F32, "total10"))
        h_bf2 = placed(after_wb, PLANE_BYTES + 3072, wide, BF16, "h_bf2")
        products(2, h_bf2)
        first(3, 1, 5)
        finish(0, 1)
        h_bf3 = held(wide, BF16, "h_bf3", "h3")
        product(3, 0, h_bf3[:, 0:SUB, :])
        second(1, 1, 2)
        product(3, 1, h_bf3[:, SUB:CHUNK, :])

        quant_h(2, h_bf2[:])
        second(2, 1, 4)
        second(2, 0, 0)
        quant_h(3, h_bf3[:])
        second(3, 0, 1)
        second(3, 1, 3)
        finish(1, 1)
        finish(2, 1)
        finish(2, 0)
        finish(3, 0)
        finish(3, 1, 0, 1)
        finish(3, 1, 1, 2, nc.scalar)
